import numpy as np
import ml_dtypes


def mxq(x, axis, fmt="e4m3"):
    dtype, down = {"e4m3": (ml_dtypes.float8_e4m3fn, 7), "e5m2": (ml_dtypes.float8_e5m2, 14)}[fmt]
    v = np.moveaxis(np.asarray(x, np.float32).astype(ml_dtypes.bfloat16).astype(np.float64), axis, -1)
    blocks = v.reshape(v.shape[:-1] + (-1, 32))
    amax = np.abs(blocks).max(-1, keepdims=True)
    byte = np.maximum(np.where(amax > 0, np.frexp(amax)[1] - 1 + 127, 0) - down, 1)
    scale = np.exp2(byte - 127.0)
    codes = (blocks / scale).astype(np.float32).astype(dtype).astype(np.float64)
    return np.moveaxis((codes * scale).reshape(v.shape), -1, axis)


WIDE = False


def mx_kscale(k):
    if not WIDE:
        return np.ones(k)
    levels = np.array([10, -10, 5, -5, 0])
    if k % 512:
        return np.exp2(np.random.permutation(np.resize(levels, k // 32))).repeat(32)
    a = np.empty((k // 512, 16))
    for p in range(k // 512):
        a[p, :8] = np.random.permutation(np.resize(levels, 8))
        for g in range(8):
            far = levels[np.abs(levels - a[p, g]) >= 10]
            a[p, g + 8] = far[np.random.randint(len(far))]
    return np.exp2(a.ravel()).repeat(32)


def f64(x):
    return np.asarray(x).astype(np.float64)


E2M1 = np.array([0.0, 0.5, 1.0, 1.5, 2.0, 3.0, 4.0, 6.0, -0.0, -0.5, -1.0, -1.5, -2.0, -3.0, -4.0, -6.0])


def pack_weight(w, fmt):
    k, n = w.shape
    w = f64(np.asarray(w, np.float32).astype(ml_dtypes.bfloat16)).reshape(k // 32, 32, n)
    amax = np.abs(w).max(1)
    if fmt == "e4m3":
        byte = np.frexp(amax)[1] - 1 + 127 - 7
    else:
        mant, ex = np.frexp(amax / 6.0)
        byte = np.where(mant > 0.5, ex, ex - 1) + 127
    byte = np.clip(np.where(amax > 0, byte, 1), 1, 254)
    scaled = (w * np.exp2(127.0 - byte)[:, None, :]).reshape(k, n).astype(np.float32)
    by_word = np.ascontiguousarray(scaled.reshape(k // 512, 128, 4, n).transpose(0, 1, 3, 2))
    if fmt == "e4m3":
        words = by_word.astype(ml_dtypes.float8_e4m3fn).view(np.uint8)
    else:
        c = by_word.astype(ml_dtypes.float4_e2m1fn).view(np.uint8) & 0xF
        words = (c[..., 0::2] | (c[..., 1::2] << 4)).reshape(k // 512, 128, 2 * n)
    return np.ascontiguousarray(words), np.ascontiguousarray(byte.astype(np.uint8).reshape(k // 512, 16, n))


def unpack_weight(words, scales, fmt):
    g, _, n = scales.shape
    words = np.ascontiguousarray(words).reshape(g, 128, n, -1)
    if fmt == "e4m3":
        vals = words.view(ml_dtypes.float8_e4m3fn).astype(np.float64)
    else:
        nib = np.empty((g, 128, n, 4), np.uint8)
        nib[..., 0::2] = words & 0xF
        nib[..., 1::2] = words >> 4
        vals = E2M1[nib]
    vals = vals * np.repeat(np.exp2(scales.astype(np.float64) - 127.0), 8, axis=1)[..., None]
    return vals.transpose(0, 1, 3, 2).reshape(g * 512, n)


def planes(y):
    n, m = y.shape
    v = y.astype(np.float32).astype(ml_dtypes.bfloat16).astype(np.float64).reshape(n // 32, 32, m)
    top = np.abs(v).max(1)
    byte = np.clip(np.where(top > 0, np.frexp(top)[1] - 1 + 127 - 7, 1), 1, 254)
    codes = (v * np.exp2(127.0 - byte)[:, None, :]).reshape(n, m).astype(np.float32).astype(ml_dtypes.float8_e4m3fn).view(np.uint8)
    words = codes.reshape(n // 512, 128, 4, m).transpose(0, 1, 3, 2)
    return np.ascontiguousarray(words), np.ascontiguousarray(byte.astype(np.uint8).reshape(n // 512, 16, m))


K, M, T = 2048, 512, 1024


def setup_inputs():
    n = np.random.standard_normal
    s = mx_kscale(K)[:, None]
    p_w4 = pack_weight(n((K, M)) / np.sqrt(K) / s ** 2, "e2m1")
    p_w8 = pack_weight(n((K, M)) / np.sqrt(K) / s, "e4m3")
    return {
        "x": (n((K, T)) * s).astype(np.float32),
        "w4_words": p_w4[0],
        "w4_scales": p_w4[1],
        "w8_words": p_w8[0],
        "w8_scales": p_w8[1],
    }


def reference(x, w4_words, w4_scales, w8_words, w8_scales):
    xa_, xb_ = mxq(f64(x) ** 2, 0, "e4m3"), mxq(f64(x), 0, "e4m3")
    w4_ = unpack_weight(w4_words, w4_scales, "e2m1")
    w8_ = unpack_weight(w8_words, w8_scales, "e4m3")
    y = w4_.T @ xa_ + w8_.T @ xb_
    out_0 = y
    return (out_0,) + planes(out_0)

@@ -1,0 +1,416 @@
+from contextlib import ExitStack
+
+import concourse.mybir as mybir
+
+K, M, T = 2048, 512, 1024
+FLOPS = 2 * 2 * K * M * T
+
+F32 = mybir.dt.float32
+BF16 = mybir.dt.bfloat16
+I32 = mybir.dt.int32
+U8 = mybir.dt.uint8
+FP8X4 = mybir.dt.float8_e4m3fn_x4
+FP4X4 = mybir.dt.float4_e2m1fn_x4
+ACT = mybir.ActivationFunctionType
+
+P = 128
+PACK = 4
+PASSES = K // (P * PACK)
+HALF = 512
+W8_ROW = 4
+RUN = 4
+
+
+def tile_mix_feat_fm_quadpl_none_kernel(
+    tc, x, w4_words, w4_scales, w8_words, w8_scales, out_0, out_1, out_2
+):
+    nc = tc.nc
+    with ExitStack() as ctx:
+        keep = ctx.enter_context(tc.tile_pool(name="keep", bufs=1))
+        stage = ctx.enter_context(tc.tile_pool(name="stage", bufs=8))
+        psum = ctx.enter_context(tc.psum_pool(name="psum", bufs=1))
+        ctx.enter_context(tc.manual_schedule())
+
+        units = [(h, a) for h in range(2) for a in range(PASSES)]
+        xs = {}
+        w4_raw = keep.tile([P, PASSES, 2 * M], U8, align_bytes=64)
+        w8_raw = keep.tile([P, PASSES, M], I32, align_bytes=64)
+        sc_raw = keep.tile([P, PASSES, M], U8, align_bytes=64)
+        w4 = keep.tile([P, PASSES, 2 * M], U8, align_bytes=64)
+        w8 = keep.tile([P, PASSES, M], I32, align_bytes=64)
+        sc = keep.tile([P, PASSES, M], U8, align_bytes=64)
+        zero = keep.tile([P, 1], F32)
+        bias = keep.tile([P, 1], F32)
+        a_codes, a_scales, b_codes, b_scales = {}, {}, {}, {}
+        for u in range(8):
+            a_codes[u] = keep.tile([P, HALF], I32, name="ac%d" % u, align_bytes=64)
+            b_codes[u] = keep.tile([P, HALF], I32, name="bc%d" % u, align_bytes=64)
+            a_scales[u] = keep.tile([P, HALF], U8, name="as%d" % u, align_bytes=64)
+            b_scales[u] = keep.tile([P, HALF], U8, name="bs%d" % u, align_bytes=64)
+        res, res16, acc = {}, {}, {}
+        for h in range(2):
+            res[h] = keep.tile([P, PACK, HALF], F32, name="res%d" % h, align_bytes=64)
+            res16[h] = keep.tile([P, HALF, PACK], BF16, name="res16_%d" % h, align_bytes=64)
+            for r in range(PACK):
+                acc[h, r] = psum.tile([P, HALF], F32, name="acc%d_%d" % (h, r))
+        o_codes = keep.tile([P, T], I32, align_bytes=64)
+        o_scales = keep.tile([P, T], U8, align_bytes=64)
+
+        def load_x(u, t0, t1):
+            h, a = units[u]
+            src = x[512 * a : 512 * (a + 1), HALF * h + t0 : HALF * h + t1]
+            piece = keep.tile([P, PACK, t1 - t0], F32, name="x%d_%d" % (u, t0), align_bytes=64)
+            xs.setdefault(u, []).append((t0, t1, piece))
+            nc.sync.dma_start(out=piece[:], in_=src.rearrange("(p j) t -> p j t", j=PACK))
+
+        def load_scales(src, row, r):
+            nc.sync.dma_start(
+                out=sc_raw[row + r : P : 32, :, :].bitcast(I32),
+                in_=src[:, r:16:4, :].rearrange("a q n -> q a n").bitcast(I32),
+            )
+
+        def load_w4(a0, a1):
+            nc.sync.dma_start(
+                out=w4_raw[:, a0:a1, :].bitcast(I32),
+                in_=w4_words[a0:a1].rearrange("a p n -> p a n").bitcast(I32),
+            )
+
+        def load_w8(a0, a1):
+            nc.sync.dma_start(
+                out=w8_raw[:, a0:a1, :],
+                in_=w8_words[a0:a1].rearrange("a p n i -> p a (n i)").bitcast(I32),
+            )
+
+        ga, gb = {}, {}
+
+        def open_unit(u):
+            ga[u] = stage.tile([P, HALF, PACK], BF16, name="ga", align_bytes=64)
+            gb[u] = stage.tile([P, HALF, PACK], BF16, name="gb", align_bytes=64)
+
+        def views(dst, src, t0, t1):
+            p0, p1, piece = [c for c in src if c[0] <= t0 and t1 <= c[1]][0]
+            return (
+                dst[:, t0:t1, :].rearrange("p (c i) j -> p c j i", i=RUN),
+                piece[:, :, t0 - p0 : t1 - p0].rearrange("p j (c i) -> p c j i", i=RUN),
+            )
+
+        def cast_v(dst, src, t0, t1):
+            o, i = views(dst, src, t0, t1)
+            nc.vector.tensor_copy(out=o, in_=i)
+
+        def cast_s(dst, src, t0, t1):
+            o, i = views(dst, src, t0, t1)
+            nc.scalar.copy(out=o, in_=i)
+
+        def square(u, t0, t1):
+            o, i = views(ga[u], xs[u], t0, t1)
+            nc.scalar.activation(out=o, in_=i, func=ACT.Square, bias=bias[:])
+
+        def quant(codes, scales, src, t0, t1, off=0):
+            nc.vector.quantize_mx(
+                out=codes[:, off + t0 : off + t1].bitcast(FP8X4),
+                scales=scales[:, off + t0 : off + t1],
+                in_=src[:, t0:t1, :].rearrange("p t j -> p (t j)"),
+            )
+
+        def qa(u, t0=0, t1=HALF):
+            quant(a_codes[u], a_scales[u], ga[u], t0, t1)
+
+        def qb(u, t0=0, t1=HALF):
+            quant(b_codes[u], b_scales[u], gb[u], t0, t1)
+
+        def deal_w4(a):
+            nc.vector.tensor_copy(
+                out=w4[:, a, :].rearrange("p (r c i b) -> p c r i b", r=PACK, i=8, b=2),
+                in_=w4_raw[:, a, :].rearrange("p (c i r b) -> p c r i b", r=PACK, i=8, b=2),
+            )
+
+        def deal_w8(a):
+            nc.vector.tensor_copy(
+                out=w8[:, a, :].rearrange("p (r c i) -> p c r i", r=PACK, i=4),
+                in_=w8_raw[:, a, :].rearrange("p (c i r) -> p c r i", r=PACK, i=4),
+            )
+
+        def deal_scales(a0, a1):
+            nc.vector.tensor_copy(
+                out=sc[:, a0:a1, :].rearrange("p a (r c i) -> p a c r i", r=PACK, i=16),
+                in_=sc_raw[:, a0:a1, :].rearrange("p a (c i r) -> p a c r i", r=PACK, i=16),
+            )
+
+        def mm(kind, u, r):
+            h, a = units[u]
+            cols = slice(P * r, P * (r + 1))
+            if kind == "b":
+                nc.tensor.matmul_mx(
+                    out=acc[h, r][:],
+                    lhsT=w8[:, a, cols].bitcast(FP8X4),
+                    lhsT_scale=sc[W8_ROW:P, a, cols],
+                    rhs=b_codes[u][:].bitcast(FP8X4),
+                    rhs_scale=b_scales[u][:],
+                    start=(a == 0),
+                    stop=False,
+                )
+            else:
+                nc.tensor.matmul_mx(
+                    out=acc[h, r][:],
+                    lhsT=w4[:, a, 2 * P * r : 2 * P * (r + 1)].bitcast(FP4X4),
+                    lhsT_scale=sc[:, a, cols],
+                    rhs=a_codes[u][:].bitcast(FP8X4),
+                    rhs_scale=a_scales[u][:],
+                    start=False,
+                    stop=(a == PASSES - 1),
+                )
+
+        def cast_xv(u, t0, t1):
+            cast_v(gb[u], xs[u], t0, t1)
+
+        def cast_xs(u, t0, t1):
+            cast_s(gb[u], xs[u], t0, t1)
+
+        def round_v(h, t0, t1):
+            cast_v(res16[h], [(0, HALF, res[h])], t0, t1)
+
+        def round_s(h, t0, t1):
+            cast_s(res16[h], [(0, HALF, res[h])], t0, t1)
+
+        def drain_s(h, r):
+            nc.scalar.copy(out=res[h][:, r, :], in_=acc[h, r][:])
+
+        def drain_v(h, r):
+            nc.vector.tensor_copy(out=res[h][:, r, :], in_=acc[h, r][:])
+
+        out_rows = out_0.rearrange("(p r) t -> p r t", r=PACK)
+
+        def store_res(h, r0, r1):
+            nc.sync.dma_start(out=out_rows[:, r0:r1, HALF * h : HALF * (h + 1)], in_=res[h][:, r0:r1, :])
+
+        def q_out(h, t0, t1):
+            quant(o_codes, o_scales, res16[h], t0, t1, off=HALF * h)
+
+        words_out = out_1[0].rearrange("p t i -> p (t i)").bitcast(I32)
+
+        def store_words(t0, t1):
+            nc.sync.dma_start(out=words_out[:, t0:t1], in_=o_codes[:, t0:t1])
+
+        def store_scales(q):
+            (nc.scalar if q < 2 else nc.sync).dma_start(
+                out=out_2[0, 4 * q : 4 * q + 4, :].bitcast(I32),
+                in_=o_scales[32 * q : 32 * q + 4, :].bitcast(I32),
+            )
+
+        nc.vector.memset(zero[:], 0.0)
+        nc.vector.memset(sc_raw[:].rearrange("p a n -> p (a n)").bitcast(I32), 0)
+        nc.scalar.activation(out=bias[:], in_=zero[:], func=ACT.Square)
+
+        load_x(0, 0, 256)
+        load_scales(w8_scales, W8_ROW, 0)
+        load_scales(w8_scales, W8_ROW, 1)
+        load_scales(w8_scales, W8_ROW, 2)
+        load_scales(w8_scales, W8_ROW, 3)
+        load_x(0, 256, 512)
+        load_scales(w4_scales, 0, 0)
+        load_scales(w4_scales, 0, 1)
+        load_scales(w4_scales, 0, 2)
+        load_scales(w4_scales, 0, 3)
+        load_x(1, 0, 256)
+        load_w8(0, 1)
+        load_w4(0, 1)
+        load_x(1, 256, 512)
+        load_x(2, 0, 256)
+        load_w8(1, 2)
+        load_w4(1, 2)
+        load_x(2, 256, 512)
+        load_x(3, 0, 256)
+        load_w8(2, 3)
+        load_w4(2, 3)
+        load_x(3, 256, 512)
+        load_x(4, 0, 256)
+        load_w8(3, 4)
+        load_w4(3, 4)
+        load_x(4, 256, 512)
+        load_x(5, 0, 256)
+        load_x(5, 256, 512)
+        load_x(6, 0, 256)
+        load_x(6, 256, 512)
+        load_x(7, 0, 256)
+        load_x(7, 256, 512)
+        for u in range(8):
+            open_unit(u)
+        deal_scales(0, 1)
+        cast_xs(0, 64, 256)
+        square(0, 0, 256)
+        cast_xv(0, 0, 64)
+        deal_scales(1, 2)
+        qb(0, 0, 256)
+        cast_xs(0, 352, 512)
+        square(0, 256, 512)
+        cast_xv(0, 256, 352)
+        qa(0, 0, 256)
+        qb(0, 256, 512)
+        cast_xs(1, 128, 256)
+        square(1, 0, 256)
+        cast_xv(1, 0, 128)
+        deal_scales(2, 3)
+        qa(0, 256, 512)
+        deal_w8(0)
+        mm('b', 0, 0)
+        mm('b', 0, 1)
+        mm('b', 0, 2)
+        mm('b', 0, 3)
+        qb(1, 0, 256)
+        cast_xs(1, 256, 512)
+        square(1, 256, 512)
+        qa(1, 0, 256)
+        deal_w4(0)
+        mm('a', 0, 0)
+        mm('a', 0, 1)
+        mm('a', 0, 2)
+        mm('a', 0, 3)
+        qb(1, 256, 512)
+        cast_xs(2, 192, 256)
+        square(2, 0, 256)
+        cast_xv(2, 0, 192)
+        deal_w4(1)
+        qa(1, 256, 512)
+        qb(2, 0, 256)
+        cast_xs(2, 448, 512)
+        square(2, 256, 512)
+        cast_xv(2, 256, 448)
+        deal_w8(1)
+        mm('b', 1, 0)
+        mm('b', 1, 1)
+        mm('b', 1, 2)
+        mm('b', 1, 3)
+        mm('a', 1, 0)
+        mm('a', 1, 1)
+        mm('a', 1, 2)
+        mm('a', 1, 3)
+        deal_scales(3, 4)
+        qa(2, 0, 256)
+        qb(2, 256, 512)
+        cast_xs(3, 128, 256)
+        square(3, 0, 256)
+        cast_xv(3, 0, 128)
+        deal_w8(2)
+        mm('b', 2, 0)
+        mm('b', 2, 1)
+        mm('b', 2, 2)
+        mm('b', 2, 3)
+        deal_w4(2)
+        qa(2, 256, 512)
+        mm('a', 2, 0)
+        mm('a', 2, 1)
+        mm('a', 2, 2)
+        mm('a', 2, 3)
+        qb(3, 0, 256)
+        square(3, 256, 512)
+        cast_xv(3, 256, 512)
+        qa(3, 0, 256)
+        qb(3, 256, 512)
+        cast_xs(4, 64, 256)
+        square(4, 0, 256)
+        cast_xv(4, 0, 64)
+        qa(3, 256, 512)
+        deal_w8(3)
+        mm('b', 3, 0)
+        mm('b', 3, 1)
+        mm('b', 3, 2)
+        mm('b', 3, 3)
+        deal_w4(3)
+        mm('a', 3, 0)
+        mm('a', 3, 1)
+        mm('a', 3, 2)
+        mm('a', 3, 3)
+        qb(4, 0, 256)
+        square(4, 256, 512)
+        cast_xv(4, 256, 512)
+        drain_s(0, 0)
+        qa(4, 0, 256)
+        qb(4, 256, 512)
+        mm('b', 4, 0)
+        mm('b', 4, 1)
+        mm('b', 4, 2)
+        mm('b', 4, 3)
+        cast_xs(5, 192, 256)
+        square(5, 0, 256)
+        cast_xv(5, 0, 192)
+        qa(4, 256, 512)
+        mm('a', 4, 0)
+        mm('a', 4, 1)
+        mm('a', 4, 2)
+        mm('a', 4, 3)
+        drain_v(0, 1)
+        store_res(0, 0, 2)
+        qb(5, 0, 256)
+        square(5, 256, 512)
+        cast_xv(5, 256, 512)
+        qa(5, 0, 256)
+        qb(5, 256, 512)
+        mm('b', 5, 0)
+        mm('b', 5, 1)
+        mm('b', 5, 2)
+        mm('b', 5, 3)
+        square(6, 0, 256)
+        cast_xv(6, 0, 256)
+        qa(5, 256, 512)
+        mm('a', 5, 0)
+        mm('a', 5, 1)
+        mm('a', 5, 2)
+        mm('a', 5, 3)
+        drain_v(0, 2)
+        store_res(0, 2, 3)
+        qb(6, 0, 256)
+        drain_v(0, 3)
+        store_res(0, 3, 4)
+        cast_xs(6, 320, 512)
+        square(6, 256, 512)
+        cast_xv(6, 256, 320)
+        qa(6, 0, 256)
+        qb(6, 256, 512)
+        mm('b', 6, 0)
+        mm('b', 6, 1)
+        mm('b', 6, 2)
+        mm('b', 6, 3)
+        square(7, 0, 256)
+        cast_xv(7, 0, 256)
+        qa(6, 256, 512)
+        mm('a', 6, 0)
+        mm('a', 6, 1)
+        mm('a', 6, 2)
+        mm('a', 6, 3)
+        qb(7, 0, 256)
+        square(7, 256, 512)
+        cast_xv(7, 256, 512)
+        round_s(0, 288, 512)
+        qa(7, 0, 256)
+        qb(7, 256, 512)
+        mm('b', 7, 0)
+        mm('b', 7, 1)
+        mm('b', 7, 2)
+        mm('b', 7, 3)
+        qa(7, 256, 512)
+        mm('a', 7, 0)
+        mm('a', 7, 1)
+        mm('a', 7, 2)
+        mm('a', 7, 3)
+        round_v(0, 256, 288)
+        round_v(0, 0, 256)
+        q_out(0, 256, 512)
+        q_out(0, 0, 256)
+        store_words(0, 512)
+        drain_s(1, 0)
+        drain_v(1, 1)
+        store_res(1, 0, 2)
+        drain_v(1, 2)
+        drain_s(1, 3)
+        store_res(1, 2, 4)
+        round_s(1, 256, 384)
+        round_v(1, 0, 256)
+        round_v(1, 384, 512)
+        q_out(1, 0, 256)
+        q_out(1, 256, 512)
+        store_words(512, 1024)
+        store_scales(0)
+        store_scales(1)
+        store_scales(2)
+        store_scales(3)

@@ -212,203 +212,168 @@ def tile_mix_feat_fm_quadpl_none_kernel(
         load_scales(w4_scales, 0, 1)
         load_scales(w4_scales, 0, 2)
         load_scales(w4_scales, 0, 3)
-        load_x(1, 0, 256)
         load_w8(0, 1)
         load_w4(0, 1)
-        load_x(1, 256, 512)
-        load_x(2, 0, 256)
+        load_x(1, 0, 512)
         load_w8(1, 2)
         load_w4(1, 2)
-        load_x(2, 256, 512)
-        load_x(3, 0, 256)
+        load_x(2, 0, 512)
         load_w8(2, 3)
-        load_w4(2, 3)
-        load_x(3, 256, 512)
-        load_x(4, 0, 256)
         load_w8(3, 4)
+        load_w4(2, 3)
         load_w4(3, 4)
-        load_x(4, 256, 512)
-        load_x(5, 0, 256)
-        load_x(5, 256, 512)
-        load_x(6, 0, 256)
-        load_x(6, 256, 512)
+        load_x(3, 0, 512)
+        load_x(4, 0, 512)
+        load_x(5, 0, 512)
+        load_x(6, 0, 512)
         load_x(7, 0, 256)
         load_x(7, 256, 512)
         for u in range(8):
             open_unit(u)
-        deal_scales(0, 1)
-        cast_xs(0, 64, 256)
+        cast_xv(0, 0, 224)
+        cast_xs(0, 224, 256)
         square(0, 0, 256)
-        cast_xv(0, 0, 64)
-        deal_scales(1, 2)
-        qb(0, 0, 256)
-        cast_xs(0, 352, 512)
-        square(0, 256, 512)
-        cast_xv(0, 256, 352)
         qa(0, 0, 256)
+        cast_xv(0, 256, 352)
+        cast_xs(0, 352, 512)
+        qb(0, 0, 256)
+        square(0, 256, 512)
+        deal_scales(0, 1)
         qb(0, 256, 512)
-        cast_xs(1, 128, 256)
-        square(1, 0, 256)
-        cast_xv(1, 0, 128)
-        deal_scales(2, 3)
-        qa(0, 256, 512)
         deal_w8(0)
         mm('b', 0, 0)
         mm('b', 0, 1)
         mm('b', 0, 2)
         mm('b', 0, 3)
-        qb(1, 0, 256)
-        cast_xs(1, 256, 512)
-        square(1, 256, 512)
-        qa(1, 0, 256)
+        cast_xs(1, 224, 512)
+        deal_scales(1, 2)
         deal_w4(0)
+        qa(0, 256, 512)
         mm('a', 0, 0)
         mm('a', 0, 1)
         mm('a', 0, 2)
         mm('a', 0, 3)
-        qb(1, 256, 512)
-        cast_xs(2, 192, 256)
-        square(2, 0, 256)
-        cast_xv(2, 0, 192)
+        deal_scales(2, 3)
+        square(1, 0, 512)
+        cast_xv(1, 0, 224)
+        cast_xs(2, 192, 512)
+        deal_scales(3, 4)
+        square(2, 0, 512)
         deal_w4(1)
-        qa(1, 256, 512)
-        qb(2, 0, 256)
-        cast_xs(2, 448, 512)
-        square(2, 256, 512)
-        cast_xv(2, 256, 448)
+        qb(1, 0, 512)
+        square(3, 0, 512)
         deal_w8(1)
         mm('b', 1, 0)
         mm('b', 1, 1)
         mm('b', 1, 2)
         mm('b', 1, 3)
+        cast_xv(2, 0, 192)
+        deal_w8(2)
+        cast_xs(4, 416, 512)
+        qa(1, 0, 512)
         mm('a', 1, 0)
         mm('a', 1, 1)
         mm('a', 1, 2)
         mm('a', 1, 3)
-        deal_scales(3, 4)
-        qa(2, 0, 256)
-        qb(2, 256, 512)
-        cast_xs(3, 128, 256)
-        square(3, 0, 256)
-        cast_xv(3, 0, 128)
-        deal_w8(2)
+        deal_w4(2)
+        square(4, 0, 512)
+        deal_w4(3)
+        deal_w8(3)
+        square(5, 0, 512)
+        qb(2, 0, 512)
         mm('b', 2, 0)
         mm('b', 2, 1)
         mm('b', 2, 2)
         mm('b', 2, 3)
-        deal_w4(2)
-        qa(2, 256, 512)
+        square(6, 0, 512)
+        cast_xv(3, 0, 512)
+        qa(2, 0, 512)
         mm('a', 2, 0)
         mm('a', 2, 1)
         mm('a', 2, 2)
         mm('a', 2, 3)
-        qb(3, 0, 256)
-        square(3, 256, 512)
-        cast_xv(3, 256, 512)
-        qa(3, 0, 256)
-        qb(3, 256, 512)
-        cast_xs(4, 64, 256)
-        square(4, 0, 256)
-        cast_xv(4, 0, 64)
-        qa(3, 256, 512)
-        deal_w8(3)
+        qb(3, 0, 512)
         mm('b', 3, 0)
-        mm('b', 3, 1)
-        mm('b', 3, 2)
-        mm('b', 3, 3)
-        deal_w4(3)
+        qa(3, 0, 512)
         mm('a', 3, 0)
+        mm('b', 3, 1)
         mm('a', 3, 1)
+        mm('b', 3, 2)
         mm('a', 3, 2)
+        mm('b', 3, 3)
         mm('a', 3, 3)
-        qb(4, 0, 256)
-        square(4, 256, 512)
-        cast_xv(4, 256, 512)
-        drain_s(0, 0)
-        qa(4, 0, 256)
-        qb(4, 256, 512)
+        cast_xv(4, 0, 416)
+        drain_v(0, 0)
+        store_res(0, 0, 1)
+        qb(4, 0, 512)
         mm('b', 4, 0)
         mm('b', 4, 1)
         mm('b', 4, 2)
         mm('b', 4, 3)
-        cast_xs(5, 192, 256)
-        square(5, 0, 256)
-        cast_xv(5, 0, 192)
-        qa(4, 256, 512)
+        cast_xv(5, 0, 512)
+        square(7, 0, 256)
+        qa(4, 0, 512)
         mm('a', 4, 0)
         mm('a', 4, 1)
         mm('a', 4, 2)
         mm('a', 4, 3)
-        drain_v(0, 1)
-        store_res(0, 0, 2)
-        qb(5, 0, 256)
-        square(5, 256, 512)
-        cast_xv(5, 256, 512)
-        qa(5, 0, 256)
-        qb(5, 256, 512)
+        qb(5, 0, 512)
         mm('b', 5, 0)
         mm('b', 5, 1)
         mm('b', 5, 2)
         mm('b', 5, 3)
-        square(6, 0, 256)
-        cast_xv(6, 0, 256)
-        qa(5, 256, 512)
+        cast_xv(6, 0, 512)
+        square(7, 256, 512)
+        qa(5, 0, 512)
         mm('a', 5, 0)
         mm('a', 5, 1)
         mm('a', 5, 2)
         mm('a', 5, 3)
-        drain_v(0, 2)
-        store_res(0, 2, 3)
-        qb(6, 0, 256)
-        drain_v(0, 3)
-        store_res(0, 3, 4)
-        cast_xs(6, 320, 512)
-        square(6, 256, 512)
-        cast_xv(6, 256, 320)
-        qa(6, 0, 256)
-        qb(6, 256, 512)
+        qb(6, 0, 512)
         mm('b', 6, 0)
         mm('b', 6, 1)
         mm('b', 6, 2)
         mm('b', 6, 3)
-        square(7, 0, 256)
         cast_xv(7, 0, 256)
-        qa(6, 256, 512)
+        drain_s(0, 1)
+        store_res(0, 1, 2)
+        qa(6, 0, 512)
         mm('a', 6, 0)
         mm('a', 6, 1)
         mm('a', 6, 2)
         mm('a', 6, 3)
-        qb(7, 0, 256)
-        square(7, 256, 512)
         cast_xv(7, 256, 512)
-        round_s(0, 288, 512)
-        qa(7, 0, 256)
+        qb(7, 0, 256)
         qb(7, 256, 512)
         mm('b', 7, 0)
-        mm('b', 7, 1)
-        mm('b', 7, 2)
-        mm('b', 7, 3)
+        qa(7, 0, 256)
         qa(7, 256, 512)
         mm('a', 7, 0)
+        mm('b', 7, 1)
         mm('a', 7, 1)
+        mm('b', 7, 2)
         mm('a', 7, 2)
+        mm('b', 7, 3)
         mm('a', 7, 3)
-        round_v(0, 256, 288)
-        round_v(0, 0, 256)
-        q_out(0, 256, 512)
-        q_out(0, 0, 256)
-        store_words(0, 512)
+        drain_s(0, 3)
+        store_res(0, 3, 4)
+        drain_v(0, 2)
+        store_res(0, 2, 3)
         drain_s(1, 0)
+        store_res(1, 0, 1)
+        round_v(0, 0, 416)
         drain_v(1, 1)
-        store_res(1, 0, 2)
-        drain_v(1, 2)
+        store_res(1, 1, 2)
+        round_s(0, 416, 512)
+        q_out(0, 0, 512)
+        store_words(0, 512)
+        drain_s(1, 2)
+        store_res(1, 2, 3)
         drain_s(1, 3)
-        store_res(1, 2, 4)
-        round_s(1, 256, 384)
-        round_v(1, 0, 256)
-        round_v(1, 384, 512)
-        q_out(1, 0, 256)
-        q_out(1, 256, 512)
+        store_res(1, 3, 4)
+        round_s(1, 320, 512)
+        round_v(1, 0, 320)
+        q_out(1, 0, 512)
         store_words(512, 1024)
         store_scales(0)
         store_scales(1)

@@ -36,9 +36,7 @@ def tile_mix_feat_fm_quadpl_none_kernel(
         w4_raw = keep.tile([P, PASSES, 2 * M], U8, align_bytes=64)
         w8_raw = keep.tile([P, PASSES, M], I32, align_bytes=64)
         sc_raw = keep.tile([P, PASSES, M], U8, align_bytes=64)
-        w4 = keep.tile([P, PASSES, 2 * M], U8, align_bytes=64)
-        w8 = keep.tile([P, PASSES, M], I32, align_bytes=64)
-        sc = keep.tile([P, PASSES, M], U8, align_bytes=64)
+        w4, w8, sc = {}, {}, {}
         zero = keep.tile([P, 1], F32)
         bias = keep.tile([P, 1], F32)
         a_codes, a_scales, b_codes, b_scales = {}, {}, {}, {}
@@ -119,32 +117,40 @@ def tile_mix_feat_fm_quadpl_none_kernel(
         def qb(u, t0=0, t1=HALF):
             quant(b_codes[u], b_scales[u], gb[u], t0, t1)
 
-        def deal_w4(a):
+        def dealt(table, label, a0, a1, width, dtype):
+            t = keep.tile([P, PACK, a1 - a0, width], dtype, name="%s%d" % (label, a0), align_bytes=64)
+            for a in range(a0, a1):
+                table[a] = (t, a - a0)
+            return t
+
+        def deal_w4(a0, a1):
+            t = dealt(w4, "w4d", a0, a1, 2 * P, U8)
             nc.vector.tensor_copy(
-                out=w4[:, a, :].rearrange("p (r c i b) -> p c r i b", r=PACK, i=8, b=2),
-                in_=w4_raw[:, a, :].rearrange("p (c i r b) -> p c r i b", r=PACK, i=8, b=2),
+                out=t[:].rearrange("p r a (c i b) -> p (a c) r i b", i=8, b=2),
+                in_=w4_raw[:, a0:a1, :].rearrange("p a (c i r b) -> p (a c) r i b", r=PACK, i=8, b=2),
             )
 
-        def deal_w8(a):
+        def deal_w8(a0, a1):
+            t = dealt(w8, "w8d", a0, a1, P, I32)
             nc.vector.tensor_copy(
-                out=w8[:, a, :].rearrange("p (r c i) -> p c r i", r=PACK, i=4),
-                in_=w8_raw[:, a, :].rearrange("p (c i r) -> p c r i", r=PACK, i=4),
+                out=t[:].rearrange("p r a (c i) -> p (a c) r i", i=4),
+                in_=w8_raw[:, a0:a1, :].rearrange("p a (c i r) -> p (a c) r i", r=PACK, i=4),
             )
 
         def deal_scales(a0, a1):
+            t = dealt(sc, "scd", a0, a1, P, U8)
             nc.vector.tensor_copy(
-                out=sc[:, a0:a1, :].rearrange("p a (r c i) -> p a c r i", r=PACK, i=16),
-                in_=sc_raw[:, a0:a1, :].rearrange("p a (c i r) -> p a c r i", r=PACK, i=16),
+                out=t[:].rearrange("p r a (c i) -> p (a c) r i", i=16),
+                in_=sc_raw[:, a0:a1, :].rearrange("p a (c i r) -> p (a c) r i", r=PACK, i=16),
             )
 
         def mm(kind, u, r):
             h, a = units[u]
-            cols = slice(P * r, P * (r + 1))
             if kind == "b":
                 nc.tensor.matmul_mx(
                     out=acc[h, r][:],
-                    lhsT=w8[:, a, cols].bitcast(FP8X4),
-                    lhsT_scale=sc[W8_ROW:P, a, cols],
+                    lhsT=w8[a][0][:, r, w8[a][1], :].bitcast(FP8X4),
+                    lhsT_scale=sc[a][0][W8_ROW:P, r, sc[a][1], :],
                     rhs=b_codes[u][:].bitcast(FP8X4),
                     rhs_scale=b_scales[u][:],
                     start=(a == 0),
@@ -153,8 +159,8 @@ def tile_mix_feat_fm_quadpl_none_kernel(
             else:
                 nc.tensor.matmul_mx(
                     out=acc[h, r][:],
-                    lhsT=w4[:, a, 2 * P * r : 2 * P * (r + 1)].bitcast(FP4X4),
-                    lhsT_scale=sc[:, a, cols],
+                    lhsT=w4[a][0][:, r, w4[a][1], :].bitcast(FP4X4),
+                    lhsT_scale=sc[a][0][:, r, sc[a][1], :],
                     rhs=a_codes[u][:].bitcast(FP8X4),
                     rhs_scale=a_scales[u][:],
                     start=False,
@@ -173,11 +179,11 @@ def tile_mix_feat_fm_quadpl_none_kernel(
         def round_s(h, t0, t1):
             cast_s(res16[h], [(0, HALF, res[h])], t0, t1)
 
-        def drain_s(h, r):
-            nc.scalar.copy(out=res[h][:, r, :], in_=acc[h, r][:])
+        def drain_s(h, r, t0, t1):
+            nc.scalar.copy(out=res[h][:, r, t0:t1], in_=acc[h, r][:, t0:t1])
 
-        def drain_v(h, r):
-            nc.vector.tensor_copy(out=res[h][:, r, :], in_=acc[h, r][:])
+        def drain_v(h, r, t0, t1):
+            nc.vector.tensor_copy(out=res[h][:, r, t0:t1], in_=acc[h, r][:, t0:t1])
 
         out_rows = out_0.rearrange("(p r) t -> p r t", r=PACK)
 
@@ -203,179 +209,107 @@ def tile_mix_feat_fm_quadpl_none_kernel(
         nc.scalar.activation(out=bias[:], in_=zero[:], func=ACT.Square)
 
         load_x(0, 0, 256)
-        load_scales(w8_scales, W8_ROW, 0)
-        load_scales(w8_scales, W8_ROW, 1)
-        load_scales(w8_scales, W8_ROW, 2)
-        load_scales(w8_scales, W8_ROW, 3)
+        for r in range(4):
+            load_scales(w8_scales, W8_ROW, r)
         load_x(0, 256, 512)
-        load_scales(w4_scales, 0, 0)
-        load_scales(w4_scales, 0, 1)
-        load_scales(w4_scales, 0, 2)
-        load_scales(w4_scales, 0, 3)
-        load_w8(0, 1)
-        load_w4(0, 1)
+        for r in range(4):
+            load_scales(w4_scales, 0, r)
         load_x(1, 0, 512)
-        load_w8(1, 2)
-        load_w4(1, 2)
+        load_w8(0, 1)
+        load_w4(0, 2)
         load_x(2, 0, 512)
-        load_w8(2, 3)
-        load_w8(3, 4)
-        load_w4(2, 3)
-        load_w4(3, 4)
+        load_w4(2, 4)
+        load_w8(1, 2)
         load_x(3, 0, 512)
-        load_x(4, 0, 512)
-        load_x(5, 0, 512)
-        load_x(6, 0, 512)
+        load_w8(2, 4)
+        for u in range(4, 7):
+            load_x(u, 0, 512)
         load_x(7, 0, 256)
         load_x(7, 256, 512)
         for u in range(8):
             open_unit(u)
-        cast_xv(0, 0, 224)
-        cast_xs(0, 224, 256)
+
+        def mms(kind, u):
+            for r in range(PACK):
+                mm(kind, u, r)
+
         square(0, 0, 256)
-        qa(0, 0, 256)
-        cast_xv(0, 256, 352)
-        cast_xs(0, 352, 512)
-        qb(0, 0, 256)
+        cast_xv(0, 0, 256)
         square(0, 256, 512)
-        deal_scales(0, 1)
-        qb(0, 256, 512)
-        deal_w8(0)
-        mm('b', 0, 0)
-        mm('b', 0, 1)
-        mm('b', 0, 2)
-        mm('b', 0, 3)
-        cast_xs(1, 224, 512)
-        deal_scales(1, 2)
-        deal_w4(0)
+        cast_xs(0, 256, 512)
+        qb(0, 0, 256)
+        qa(0, 0, 256)
+        deal_scales(0, 4)
         qa(0, 256, 512)
-        mm('a', 0, 0)
-        mm('a', 0, 1)
-        mm('a', 0, 2)
-        mm('a', 0, 3)
-        deal_scales(2, 3)
+        qb(0, 256, 512)
+
         square(1, 0, 512)
-        cast_xv(1, 0, 224)
-        cast_xs(2, 192, 512)
-        deal_scales(3, 4)
+        cast_xs(1, 128, 512)
+        deal_w8(0, 1)
+        mms("b", 0)
+        cast_xv(1, 0, 128)
+        deal_w4(0, 2)
+        mms("a", 0)
+        qa(1)
+
         square(2, 0, 512)
-        deal_w4(1)
-        qb(1, 0, 512)
-        square(3, 0, 512)
-        deal_w8(1)
-        mm('b', 1, 0)
-        mm('b', 1, 1)
-        mm('b', 1, 2)
-        mm('b', 1, 3)
-        cast_xv(2, 0, 192)
-        deal_w8(2)
-        cast_xs(4, 416, 512)
-        qa(1, 0, 512)
-        mm('a', 1, 0)
-        mm('a', 1, 1)
-        mm('a', 1, 2)
-        mm('a', 1, 3)
-        deal_w4(2)
-        square(4, 0, 512)
-        deal_w4(3)
-        deal_w8(3)
-        square(5, 0, 512)
-        qb(2, 0, 512)
-        mm('b', 2, 0)
-        mm('b', 2, 1)
-        mm('b', 2, 2)
-        mm('b', 2, 3)
-        square(6, 0, 512)
-        cast_xv(3, 0, 512)
-        qa(2, 0, 512)
-        mm('a', 2, 0)
-        mm('a', 2, 1)
-        mm('a', 2, 2)
-        mm('a', 2, 3)
-        qb(3, 0, 512)
-        mm('b', 3, 0)
-        qa(3, 0, 512)
-        mm('a', 3, 0)
-        mm('b', 3, 1)
-        mm('a', 3, 1)
-        mm('b', 3, 2)
-        mm('a', 3, 2)
-        mm('b', 3, 3)
-        mm('a', 3, 3)
-        cast_xv(4, 0, 416)
-        drain_v(0, 0)
-        store_res(0, 0, 1)
-        qb(4, 0, 512)
-        mm('b', 4, 0)
-        mm('b', 4, 1)
-        mm('b', 4, 2)
-        mm('b', 4, 3)
-        cast_xv(5, 0, 512)
+        cast_xs(2, 448, 512)
+        cast_xv(2, 0, 448)
+        qb(1)
+        deal_w8(1, 2)
+        mms("b", 1)
+        mms("a", 1)
+        deal_w4(2, 4)
+        qb(2)
+        deal_w8(2, 4)
+        mms("b", 2)
+
+        cast_xs(3, 352, 512)
+        for u in range(3, 7):
+            square(u, 0, 512)
+            cast_xv(u, 0, 352 if u == 3 else 512)
+            qa(u - 1)
+            mms("a", u - 1)
+            qb(u)
+            mms("b", u)
+            if u == 5:
+                drain_s(0, 3, 0, 512)
+                store_res(0, 3, 4)
+
         square(7, 0, 256)
-        qa(4, 0, 512)
-        mm('a', 4, 0)
-        mm('a', 4, 1)
-        mm('a', 4, 2)
-        mm('a', 4, 3)
-        qb(5, 0, 512)
-        mm('b', 5, 0)
-        mm('b', 5, 1)
-        mm('b', 5, 2)
-        mm('b', 5, 3)
-        cast_xv(6, 0, 512)
-        square(7, 256, 512)
-        qa(5, 0, 512)
-        mm('a', 5, 0)
-        mm('a', 5, 1)
-        mm('a', 5, 2)
-        mm('a', 5, 3)
-        qb(6, 0, 512)
-        mm('b', 6, 0)
-        mm('b', 6, 1)
-        mm('b', 6, 2)
-        mm('b', 6, 3)
         cast_xv(7, 0, 256)
-        drain_s(0, 1)
-        store_res(0, 1, 2)
-        qa(6, 0, 512)
-        mm('a', 6, 0)
-        mm('a', 6, 1)
-        mm('a', 6, 2)
-        mm('a', 6, 3)
+        qa(6)
+        mms("a", 6)
+        square(7, 256, 512)
         cast_xv(7, 256, 512)
-        qb(7, 0, 256)
-        qb(7, 256, 512)
-        mm('b', 7, 0)
         qa(7, 0, 256)
+        qb(7)
         qa(7, 256, 512)
-        mm('a', 7, 0)
-        mm('b', 7, 1)
-        mm('a', 7, 1)
-        mm('b', 7, 2)
-        mm('a', 7, 2)
-        mm('b', 7, 3)
-        mm('a', 7, 3)
-        drain_s(0, 3)
-        store_res(0, 3, 4)
-        drain_v(0, 2)
+        for r in range(PACK):
+            mm("b", 7, r)
+            mm("a", 7, r)
+
+        drain_s(0, 2, 0, 512)
         store_res(0, 2, 3)
-        drain_s(1, 0)
-        store_res(1, 0, 1)
-        round_v(0, 0, 416)
-        drain_v(1, 1)
-        store_res(1, 1, 2)
-        round_s(0, 416, 512)
+        drain_s(0, 0, 0, 512)
+        store_res(0, 0, 1)
+        drain_v(0, 1, 0, 512)
+        store_res(0, 1, 2)
+        round_v(0, 0, 512)
+        for r in range(3):
+            drain_s(1, r, 0, 512)
+            store_res(1, r, r + 1)
         q_out(0, 0, 512)
         store_words(0, 512)
-        drain_s(1, 2)
-        store_res(1, 2, 3)
-        drain_s(1, 3)
+        drain_s(1, 3, 0, 256)
+        drain_s(1, 3, 256, 512)
         store_res(1, 3, 4)
-        round_s(1, 320, 512)
-        round_v(1, 0, 320)
-        q_out(1, 0, 512)
-        store_words(512, 1024)
-        store_scales(0)
-        store_scales(1)
-        store_scales(2)
-        store_scales(3)
+        round_v(1, 0, 256)
+        round_s(1, 352, 512)
+        round_v(1, 256, 352)
+        q_out(1, 0, 256)
+        store_words(512, 768)
+        q_out(1, 256, 512)
+        store_words(768, 1024)
+        for q in range(4):
+            store_scales(q)

@@ -9,6 +9,7 @@ F32 = mybir.dt.float32
 BF16 = mybir.dt.bfloat16
 I32 = mybir.dt.int32
 U8 = mybir.dt.uint8
+U16 = mybir.dt.uint16
 FP8X4 = mybir.dt.float8_e4m3fn_x4
 FP4X4 = mybir.dt.float4_e2m1fn_x4
 ACT = mybir.ActivationFunctionType
@@ -16,9 +17,11 @@ ACT = mybir.ActivationFunctionType
 P = 128
 PACK = 4
 PASSES = K // (P * PACK)
-HALF = 512
+BANK = 512
 W8_ROW = 4
 RUN = 4
+SIDE = 512
+RANGES = [(0, 512, 512), (512, 512, SIDE)]
 
 
 def tile_mix_feat_fm_quadpl_none_kernel(
@@ -27,11 +30,10 @@ def tile_mix_feat_fm_quadpl_none_kernel(
     nc = tc.nc
     with ExitStack() as ctx:
         keep = ctx.enter_context(tc.tile_pool(name="keep", bufs=1))
-        stage = ctx.enter_context(tc.tile_pool(name="stage", bufs=8))
         psum = ctx.enter_context(tc.psum_pool(name="psum", bufs=1))
         ctx.enter_context(tc.manual_schedule())
 
-        units = [(h, a) for h in range(2) for a in range(PASSES)]
+        units = [(h, a) for h in range(len(RANGES)) for a in range(PASSES)]
         xs = {}
         w4_raw = keep.tile([P, PASSES, 2 * M], U8, align_bytes=64)
         w8_raw = keep.tile([P, PASSES, M], I32, align_bytes=64)
@@ -39,26 +41,35 @@ def tile_mix_feat_fm_quadpl_none_kernel(
         w4, w8, sc = {}, {}, {}
         zero = keep.tile([P, 1], F32)
         bias = keep.tile([P, 1], F32)
-        a_codes, a_scales, b_codes, b_scales = {}, {}, {}, {}
-        for u in range(8):
-            a_codes[u] = keep.tile([P, HALF], I32, name="ac%d" % u, align_bytes=64)
-            b_codes[u] = keep.tile([P, HALF], I32, name="bc%d" % u, align_bytes=64)
-            a_scales[u] = keep.tile([P, HALF], U8, name="as%d" % u, align_bytes=64)
-            b_scales[u] = keep.tile([P, HALF], U8, name="bs%d" % u, align_bytes=64)
-        res, res16, acc = {}, {}, {}
-        for h in range(2):
-            res[h] = keep.tile([P, PACK, HALF], F32, name="res%d" % h, align_bytes=64)
-            res16[h] = keep.tile([P, HALF, PACK], BF16, name="res16_%d" % h, align_bytes=64)
-            for r in range(PACK):
-                acc[h, r] = psum.tile([P, HALF], F32, name="acc%d_%d" % (h, r))
+        a_codes, a_scales, b_codes, b_scales, ga, gb = {}, {}, {}, {}, {}, {}
+        for u, (h, a) in enumerate(units):
+            wd = RANGES[h][1]
+            a_codes[u] = keep.tile([P, wd], I32, name="ac%d" % u, align_bytes=64)
+            b_codes[u] = keep.tile([P, wd], I32, name="bc%d" % u, align_bytes=64)
+            a_scales[u] = keep.tile([P, wd], U8, name="as%d" % u, align_bytes=64)
+            b_scales[u] = keep.tile([P, wd], U8, name="bs%d" % u, align_bytes=64)
+            ga[u] = keep.tile([P, wd, PACK], BF16, name="ga%d" % u, align_bytes=64)
+            gb[u] = keep.tile([P, wd, PACK], BF16, name="gb%d" % u, align_bytes=64)
+        res, res16, banks = {}, {}, {}
+        for h, (first, wd, side) in enumerate(RANGES):
+            res[h] = keep.tile([P, PACK, wd], F32, name="res%d" % h, align_bytes=64)
+            res16[h] = keep.tile([P, wd, PACK], BF16, name="res16_%d" % h, align_bytes=64)
+            for b in range(PACK * wd // BANK):
+                banks[h, b] = psum.tile([P, BANK // side, side], F32, name="acc%d_%d" % (h, b))
         o_codes = keep.tile([P, T], I32, align_bytes=64)
         o_scales = keep.tile([P, T], U8, align_bytes=64)
 
-        def load_x(u, t0, t1):
-            h, a = units[u]
-            src = x[512 * a : 512 * (a + 1), HALF * h + t0 : HALF * h + t1]
-            piece = keep.tile([P, PACK, t1 - t0], F32, name="x%d_%d" % (u, t0), align_bytes=64)
-            xs.setdefault(u, []).append((t0, t1, piece))
+        def place(h, r, t0):
+            first, wd, side = RANGES[h]
+            hands = BANK // side
+            return (t0 // side) * (PACK // hands) + r // hands, r % hands, t0 % side
+
+        def load_x(a, t0, t1):
+            src = x[512 * a : 512 * (a + 1), t0:t1]
+            piece = keep.tile([P, PACK, t1 - t0], F32, name="x%d_%d" % (a, t0), align_bytes=64)
+            for u, (h, b) in enumerate(units):
+                if b == a:
+                    xs.setdefault(u, []).append((t0 - RANGES[h][0], t1 - RANGES[h][0], piece))
             nc.sync.dma_start(out=piece[:], in_=src.rearrange("(p j) t -> p j t", j=PACK))
 
         def load_scales(src, row, r):
@@ -78,12 +89,6 @@ def tile_mix_feat_fm_quadpl_none_kernel(
                 out=w8_raw[:, a0:a1, :],
                 in_=w8_words[a0:a1].rearrange("a p n i -> p a (n i)").bitcast(I32),
             )
-
-        ga, gb = {}, {}
-
-        def open_unit(u):
-            ga[u] = stage.tile([P, HALF, PACK], BF16, name="ga", align_bytes=64)
-            gb[u] = stage.tile([P, HALF, PACK], BF16, name="gb", align_bytes=64)
 
         def views(dst, src, t0, t1):
             p0, p1, piece = [c for c in src if c[0] <= t0 and t1 <= c[1]][0]
@@ -111,10 +116,10 @@ def tile_mix_feat_fm_quadpl_none_kernel(
                 in_=src[:, t0:t1, :].rearrange("p t j -> p (t j)"),
             )
 
-        def qa(u, t0=0, t1=HALF):
+        def qa(u, t0, t1):
             quant(a_codes[u], a_scales[u], ga[u], t0, t1)
 
-        def qb(u, t0=0, t1=HALF):
+        def qb(u, t0, t1):
             quant(b_codes[u], b_scales[u], gb[u], t0, t1)
 
         def dealt(table, label, a0, a1, width, dtype):
@@ -126,8 +131,8 @@ def tile_mix_feat_fm_quadpl_none_kernel(
         def deal_w4(a0, a1):
             t = dealt(w4, "w4d", a0, a1, 2 * P, U8)
             nc.vector.tensor_copy(
-                out=t[:].rearrange("p r a (c i b) -> p (a c) r i b", i=8, b=2),
-                in_=w4_raw[:, a0:a1, :].rearrange("p a (c i r b) -> p (a c) r i b", r=PACK, i=8, b=2),
+                out=t[:].bitcast(U16).rearrange("p r a (c i) -> p (a c) r i", i=8),
+                in_=w4_raw[:, a0:a1, :].bitcast(U16).rearrange("p a (c i r) -> p (a c) r i", r=PACK, i=8),
             )
 
         def deal_w8(a0, a1):
@@ -144,28 +149,54 @@ def tile_mix_feat_fm_quadpl_none_kernel(
                 in_=sc_raw[:, a0:a1, :].rearrange("p a (c i r) -> p (a c) r i", r=PACK, i=16),
             )
 
-        def mm(kind, u, r):
+        written = {}
+
+        def flags(h, b, n):
+            before = written.get((h, b), 0)
+            written[h, b] = before + n
+            return before == 0, before + n == 2 * PASSES * BANK
+
+        def mm_b(u, r, t0, t1):
             h, a = units[u]
-            if kind == "b":
-                nc.tensor.matmul_mx(
-                    out=acc[h, r][:],
-                    lhsT=w8[a][0][:, r, w8[a][1], :].bitcast(FP8X4),
-                    lhsT_scale=sc[a][0][W8_ROW:P, r, sc[a][1], :],
-                    rhs=b_codes[u][:].bitcast(FP8X4),
-                    rhs_scale=b_scales[u][:],
-                    start=(a == 0),
-                    stop=False,
-                )
-            else:
-                nc.tensor.matmul_mx(
-                    out=acc[h, r][:],
-                    lhsT=w4[a][0][:, r, w4[a][1], :].bitcast(FP4X4),
-                    lhsT_scale=sc[a][0][:, r, sc[a][1], :],
-                    rhs=a_codes[u][:].bitcast(FP8X4),
-                    rhs_scale=a_scales[u][:],
-                    start=False,
-                    stop=(a == PASSES - 1),
-                )
+            b, hand, c0 = place(h, r, t0)
+            start, stop = flags(h, b, t1 - t0)
+            nc.tensor.matmul_mx(
+                out=banks[h, b][:, hand, c0 : c0 + t1 - t0],
+                lhsT=w8[a][0][:, r, w8[a][1], :].bitcast(FP8X4),
+                lhsT_scale=sc[a][0][W8_ROW:P, r, sc[a][1], :],
+                rhs=b_codes[u][:, t0:t1].bitcast(FP8X4),
+                rhs_scale=b_scales[u][:, t0:t1],
+                start=start,
+                stop=stop,
+            )
+
+        def mm_a(u, r, t0, t1):
+            h, a = units[u]
+            b, hand, c0 = place(h, r, t0)
+            start, stop = flags(h, b, t1 - t0)
+            nc.tensor.matmul_mx(
+                out=banks[h, b][:, hand, c0 : c0 + t1 - t0],
+                lhsT=w4[a][0][:, r, w4[a][1], :].bitcast(FP4X4),
+                lhsT_scale=sc[a][0][:, r, sc[a][1], :],
+                rhs=a_codes[u][:, t0:t1].bitcast(FP8X4),
+                rhs_scale=a_scales[u][:, t0:t1],
+                start=start,
+                stop=stop,
+            )
+
+        def mms_b(u, t0=0, t1=None):
+            first, wd, side = RANGES[units[u][0]]
+            for c in range(t0, wd if t1 is None else t1, side):
+                for r in range(PACK):
+                    mm_b(u, r, c, c + side)
+
+        def mms_a(u, t0=0, t1=None):
+            first, wd, side = RANGES[units[u][0]]
+            n = BANK if side == BANK else P
+            for s0 in range(t0, wd if t1 is None else t1, side):
+                for r in range(PACK):
+                    for c in range(s0, s0 + side, n):
+                        mm_a(u, r, c, c + n)
 
         def cast_xv(u, t0, t1):
             cast_v(gb[u], xs[u], t0, t1)
@@ -174,24 +205,37 @@ def tile_mix_feat_fm_quadpl_none_kernel(
             cast_s(gb[u], xs[u], t0, t1)
 
         def round_v(h, t0, t1):
-            cast_v(res16[h], [(0, HALF, res[h])], t0, t1)
+            cast_v(res16[h], [(0, T, res[h])], t0, t1)
 
         def round_s(h, t0, t1):
-            cast_s(res16[h], [(0, HALF, res[h])], t0, t1)
+            cast_s(res16[h], [(0, T, res[h])], t0, t1)
 
-        def drain_s(h, r, t0, t1):
-            nc.scalar.copy(out=res[h][:, r, t0:t1], in_=acc[h, r][:, t0:t1])
+        def drained(h, b):
+            first, wd, side = RANGES[h]
+            hands = BANK // side
+            r0, t0 = (b % (PACK // hands)) * hands, (b // (PACK // hands)) * side
+            return res[h][:, r0 : r0 + hands, t0 : t0 + side]
 
-        def drain_v(h, r, t0, t1):
-            nc.vector.tensor_copy(out=res[h][:, r, t0:t1], in_=acc[h, r][:, t0:t1])
+        def drain_s(h, b):
+            nc.scalar.copy(out=drained(h, b), in_=banks[h, b][:])
+
+        def drain_v(h, b):
+            nc.vector.tensor_copy(out=drained(h, b), in_=banks[h, b][:])
+
+        def round_bank_v(h, b):
+            nc.vector.tensor_copy(
+                out=res16[h][:, P * b : P * (b + 1), :], in_=banks[h, b][:].rearrange("p r t -> p t r")
+            )
 
         out_rows = out_0.rearrange("(p r) t -> p r t", r=PACK)
 
-        def store_res(h, r0, r1):
-            nc.sync.dma_start(out=out_rows[:, r0:r1, HALF * h : HALF * (h + 1)], in_=res[h][:, r0:r1, :])
+        def store_res(h, r0, r1, t0=0, t1=None):
+            first, wd, side = RANGES[h]
+            t1 = wd if t1 is None else t1
+            nc.sync.dma_start(out=out_rows[:, r0:r1, first + t0 : first + t1], in_=res[h][:, r0:r1, t0:t1])
 
         def q_out(h, t0, t1):
-            quant(o_codes, o_scales, res16[h], t0, t1, off=HALF * h)
+            quant(o_codes, o_scales, res16[h], t0, t1, off=RANGES[h][0])
 
         words_out = out_1[0].rearrange("p t i -> p (t i)").bitcast(I32)
 
@@ -208,105 +252,100 @@ def tile_mix_feat_fm_quadpl_none_kernel(
         nc.vector.memset(sc_raw[:].rearrange("p a n -> p (a n)").bitcast(I32), 0)
         nc.scalar.activation(out=bias[:], in_=zero[:], func=ACT.Square)
 
-        load_x(0, 0, 256)
+        def sq(u):
+            square(u, 0, 512)
+
+        def xb(u):
+            cast_xv(u, 0, 512)
+
+        def do_b(u):
+            qb(u, 0, 512)
+            mms_b(u)
+
+        def do_a(u):
+            qa(u, 0, 512)
+            mms_a(u)
+
+        load_x(0, 0, 1024)
         for r in range(4):
             load_scales(w8_scales, W8_ROW, r)
-        load_x(0, 256, 512)
+        load_w8(0, 2)
         for r in range(4):
             load_scales(w4_scales, 0, r)
-        load_x(1, 0, 512)
-        load_w8(0, 1)
         load_w4(0, 2)
-        load_x(2, 0, 512)
+        load_x(1, 0, 512)
         load_w4(2, 4)
-        load_w8(1, 2)
-        load_x(3, 0, 512)
         load_w8(2, 4)
-        for u in range(4, 7):
-            load_x(u, 0, 512)
-        load_x(7, 0, 256)
-        load_x(7, 256, 512)
-        for u in range(8):
-            open_unit(u)
+        load_x(2, 0, 512)
+        load_x(3, 0, 512)
+        for a in range(1, 4):
+            load_x(a, 512, 1024)
 
-        def mms(kind, u):
-            for r in range(PACK):
-                mm(kind, u, r)
-
-        square(0, 0, 256)
-        cast_xv(0, 0, 256)
-        square(0, 256, 512)
-        cast_xs(0, 256, 512)
-        qb(0, 0, 256)
-        qa(0, 0, 256)
+        order = [0, 4, 1, 2, 3, 5, 6, 7]
+        sq(0)
+        sq(4)
+        cast_xs(4, 256, 512)
+        xb(0)
+        cast_xv(4, 0, 256)
+        qb(0, 0, 512)
+        deal_w8(0, 2)
         deal_scales(0, 4)
-        qa(0, 256, 512)
-        qb(0, 256, 512)
-
-        square(1, 0, 512)
-        cast_xs(1, 128, 512)
-        deal_w8(0, 1)
-        mms("b", 0)
-        cast_xv(1, 0, 128)
+        mms_b(0)
+        qa(0, 0, 512)
         deal_w4(0, 2)
-        mms("a", 0)
-        qa(1)
+        mms_a(0)
+        do_a(4)
 
-        square(2, 0, 512)
-        cast_xs(2, 448, 512)
-        cast_xv(2, 0, 448)
-        qb(1)
-        deal_w8(1, 2)
-        mms("b", 1)
-        mms("a", 1)
+        sq(1)
+        cast_xs(1, 192, 512)
+        cast_xv(1, 0, 192)
+        do_b(4)
         deal_w4(2, 4)
-        qb(2)
         deal_w8(2, 4)
-        mms("b", 2)
+        do_a(1)
+        sq(2)
+        xb(2)
+        do_b(1)
+        do_b(2)
 
-        cast_xs(3, 352, 512)
-        for u in range(3, 7):
-            square(u, 0, 512)
-            cast_xv(u, 0, 352 if u == 3 else 512)
-            qa(u - 1)
-            mms("a", u - 1)
-            qb(u)
-            mms("b", u)
-            if u == 5:
-                drain_s(0, 3, 0, 512)
-                store_res(0, 3, 4)
+        for i in range(4, 7):
+            sq(order[i])
+            xb(order[i])
+            do_a(order[i - 1])
+            do_b(order[i])
+        drain_s(0, 0)
+        store_res(0, 0, 1)
 
         square(7, 0, 256)
-        cast_xv(7, 0, 256)
-        qa(6)
-        mms("a", 6)
         square(7, 256, 512)
-        cast_xv(7, 256, 512)
+        xb(7)
+        do_a(6)
+        qb(7, 0, 512)
         qa(7, 0, 256)
-        qb(7)
         qa(7, 256, 512)
         for r in range(PACK):
-            mm("b", 7, r)
-            mm("a", 7, r)
+            mm_b(7, r, 0, 512)
+            mm_a(7, r, 0, 512)
 
-        drain_s(0, 2, 0, 512)
-        store_res(0, 2, 3)
-        drain_s(0, 0, 0, 512)
-        store_res(0, 0, 1)
-        drain_v(0, 1, 0, 512)
+        drain_s(0, 1)
         store_res(0, 1, 2)
+        drain_s(0, 2)
+        drain_v(0, 3)
+        store_res(0, 2, 4)
         round_v(0, 0, 512)
-        for r in range(3):
-            drain_s(1, r, 0, 512)
-            store_res(1, r, r + 1)
+        drain_s(1, 0)
+        store_res(1, 0, 1)
+        drain_s(1, 1)
+        store_res(1, 1, 2)
+        drain_v(1, 2)
+        store_res(1, 2, 3)
         q_out(0, 0, 512)
-        store_words(0, 512)
-        drain_s(1, 3, 0, 256)
-        drain_s(1, 3, 256, 512)
+        drain_s(1, 3)
         store_res(1, 3, 4)
+        store_words(0, 512)
         round_v(1, 0, 256)
-        round_s(1, 352, 512)
-        round_v(1, 256, 352)
+        round_s(1, 384, 512)
+        round_v(1, 256, 384)
         q_out(1, 0, 256)
         store_words(512, 768)
         q_out(1, 256, 512)

@@ -35,12 +35,10 @@ def tile_mix_feat_fm_quadpl_none_kernel(
 
         units = [(h, a) for h in range(len(RANGES)) for a in range(PASSES)]
         xs = {}
-        w4_raw = keep.tile([P, PASSES, 2 * M], U8, align_bytes=64)
-        w8_raw = keep.tile([P, PASSES, M], I32, align_bytes=64)
-        sc_raw = keep.tile([P, PASSES, M], U8, align_bytes=64)
+        w4_raw = keep.tile([P, PASSES, 2 * M], U8, align_bytes=256)
+        w8_raw = keep.tile([P, PASSES, M], I32, align_bytes=256)
+        sc_raw = keep.tile([P, PASSES, M], U8, align_bytes=256)
         w4, w8, sc = {}, {}, {}
-        zero = keep.tile([P, 1], F32)
-        bias = keep.tile([P, 1], F32)
         a_codes, a_scales, b_codes, b_scales, ga, gb = {}, {}, {}, {}, {}, {}
         for u, (h, a) in enumerate(units):
             wd = RANGES[h][1]
@@ -52,12 +50,15 @@ def tile_mix_feat_fm_quadpl_none_kernel(
             gb[u] = keep.tile([P, wd, PACK], BF16, name="gb%d" % u, align_bytes=64)
         res, res16, banks = {}, {}, {}
         for h, (first, wd, side) in enumerate(RANGES):
-            res[h] = keep.tile([P, PACK, wd], F32, name="res%d" % h, align_bytes=64)
+            res[h] = keep.tile([P, PACK, wd], F32, name="res%d" % h, align_bytes=256)
             res16[h] = keep.tile([P, wd, PACK], BF16, name="res16_%d" % h, align_bytes=64)
             for b in range(PACK * wd // BANK):
                 banks[h, b] = psum.tile([P, BANK // side, side], F32, name="acc%d_%d" % (h, b))
-        o_codes = keep.tile([P, T], I32, align_bytes=64)
-        o_scales = keep.tile([P, T], U8, align_bytes=64)
+        o_codes = keep.tile([P, T], I32, align_bytes=256)
+        o_scales = keep.tile([P, T], U8, align_bytes=256)
+
+        zero = keep.tile([P, 1], F32)
+        bias = keep.tile([P, 1], F32)
 
         def place(h, r, t0):
             first, wd, side = RANGES[h]
@@ -66,7 +67,7 @@ def tile_mix_feat_fm_quadpl_none_kernel(
 
         def load_x(a, t0, t1):
             src = x[512 * a : 512 * (a + 1), t0:t1]
-            piece = keep.tile([P, PACK, t1 - t0], F32, name="x%d_%d" % (a, t0), align_bytes=64)
+            piece = keep.tile([P, PACK, t1 - t0], F32, name="x%d_%d" % (a, t0), align_bytes=256)
             for u, (h, b) in enumerate(units):
                 if b == a:
                     xs.setdefault(u, []).append((t0 - RANGES[h][0], t1 - RANGES[h][0], piece))
@@ -284,9 +285,9 @@ def tile_mix_feat_fm_quadpl_none_kernel(
         order = [0, 4, 1, 2, 3, 5, 6, 7]
         sq(0)
         sq(4)
-        cast_xs(4, 256, 512)
+        cast_xs(4, 320, 512)
         xb(0)
-        cast_xv(4, 0, 256)
+        cast_xv(4, 0, 320)
         qb(0, 0, 512)
         deal_w8(0, 2)
         deal_scales(0, 4)

@@ -271,9 +271,9 @@ def tile_mix_feat_fm_quadpl_none_kernel(
         for r in range(4):
             load_scales(w8_scales, W8_ROW, r)
         load_w8(0, 2)
+        load_w4(0, 2)
         for r in range(4):
             load_scales(w4_scales, 0, r)
-        load_w4(0, 2)
         load_x(1, 0, 512)
         load_w4(2, 4)
         load_w8(2, 4)
@@ -339,10 +339,9 @@ def tile_mix_feat_fm_quadpl_none_kernel(
         drain_s(1, 1)
         store_res(1, 1, 2)
         drain_v(1, 2)
-        store_res(1, 2, 3)
         q_out(0, 0, 512)
         drain_s(1, 3)
-        store_res(1, 3, 4)
+        store_res(1, 2, 4)
         store_words(0, 512)
         round_v(1, 0, 256)
         round_s(1, 384, 512)

@@ -267,13 +267,14 @@ def tile_mix_feat_fm_quadpl_none_kernel(
             qa(u, 0, 512)
             mms_a(u)
 
-        load_x(0, 0, 1024)
+        load_x(0, 0, 512)
         for r in range(4):
             load_scales(w8_scales, W8_ROW, r)
-        load_w8(0, 2)
-        load_w4(0, 2)
+        load_x(0, 512, 1024)
         for r in range(4):
             load_scales(w4_scales, 0, r)
+        load_w8(0, 2)
+        load_w4(0, 2)
         load_x(1, 0, 512)
         load_w4(2, 4)
         load_w8(2, 4)
@@ -285,28 +286,28 @@ def tile_mix_feat_fm_quadpl_none_kernel(
         order = [0, 4, 1, 2, 3, 5, 6, 7]
         sq(0)
         sq(4)
-        cast_xs(4, 320, 512)
+        cast_xs(4, 128, 512)
         xb(0)
-        cast_xv(4, 0, 320)
         qb(0, 0, 512)
-        deal_w8(0, 2)
-        deal_scales(0, 4)
-        mms_b(0)
         qa(0, 0, 512)
+        deal_scales(0, 4)
+        deal_w8(0, 2)
+        mms_b(0)
         deal_w4(0, 2)
         mms_a(0)
+        cast_xv(4, 0, 128)
         do_a(4)
 
         sq(1)
-        cast_xs(1, 192, 512)
-        cast_xv(1, 0, 192)
+        cast_xs(1, 320, 512)
+        cast_xv(1, 0, 320)
         do_b(4)
         deal_w4(2, 4)
         deal_w8(2, 4)
         do_a(1)
+        do_b(1)
         sq(2)
         xb(2)
-        do_b(1)
         do_b(2)
 
         for i in range(4, 7):
@@ -319,10 +320,10 @@ def tile_mix_feat_fm_quadpl_none_kernel(
 
         square(7, 0, 256)
         square(7, 256, 512)
-        xb(7)
         do_a(6)
-        qb(7, 0, 512)
+        xb(7)
         qa(7, 0, 256)
+        qb(7, 0, 512)
         qa(7, 256, 512)
         for r in range(PACK):
             mm_b(7, r, 0, 512)

@@ -13,15 +13,16 @@ U16 = mybir.dt.uint16
 FP8X4 = mybir.dt.float8_e4m3fn_x4
 FP4X4 = mybir.dt.float4_e2m1fn_x4
 ACT = mybir.ActivationFunctionType
+ALU = mybir.AluOpType
 
 P = 128
 PACK = 4
 PASSES = K // (P * PACK)
 BANK = 512
+HALF = 512
 W8_ROW = 4
 RUN = 4
-SIDE = 512
-RANGES = [(0, 512, 512), (512, 512, SIDE)]
+RANGES = [(0, 512), (512, 512)]
 
 
 def tile_mix_feat_fm_quadpl_none_kernel(
@@ -33,51 +34,44 @@ def tile_mix_feat_fm_quadpl_none_kernel(
         psum = ctx.enter_context(tc.psum_pool(name="psum", bufs=1))
         ctx.enter_context(tc.manual_schedule())
 
-        units = [(h, a) for h in range(len(RANGES)) for a in range(PASSES)]
-        xs = {}
+        xs = {a: [] for a in range(PASSES)}
         w4_raw = keep.tile([P, PASSES, 2 * M], U8, align_bytes=256)
         w8_raw = keep.tile([P, PASSES, M], I32, align_bytes=256)
         sc_raw = keep.tile([P, PASSES, M], U8, align_bytes=256)
         w4, w8, sc = {}, {}, {}
-        a_codes, a_scales, b_codes, b_scales, ga, gb = {}, {}, {}, {}, {}, {}
-        for u, (h, a) in enumerate(units):
-            wd = RANGES[h][1]
-            a_codes[u] = keep.tile([P, wd], I32, name="ac%d" % u, align_bytes=64)
-            b_codes[u] = keep.tile([P, wd], I32, name="bc%d" % u, align_bytes=64)
-            a_scales[u] = keep.tile([P, wd], U8, name="as%d" % u, align_bytes=64)
-            b_scales[u] = keep.tile([P, wd], U8, name="bs%d" % u, align_bytes=64)
-            ga[u] = keep.tile([P, wd, PACK], BF16, name="ga%d" % u, align_bytes=64)
-            gb[u] = keep.tile([P, wd, PACK], BF16, name="gb%d" % u, align_bytes=64)
+        codes, scales, wide = {}, {}, {}
+        for kind in "ab":
+            for a in range(PASSES):
+                for h in range(T // HALF):
+                    key = (kind, a, h)
+                    label = "%s%d%d" % key
+                    codes[key] = keep.tile([P, HALF], I32, name="c" + label, align_bytes=64)
+                    scales[key] = keep.tile([P, HALF], U8, name="s" + label, align_bytes=64)
+                    wide[key] = keep.tile([P, HALF, PACK], BF16, name="g" + label, align_bytes=64)
         res, res16, banks = {}, {}, {}
-        for h, (first, wd, side) in enumerate(RANGES):
-            res[h] = keep.tile([P, PACK, wd], F32, name="res%d" % h, align_bytes=256)
-            res16[h] = keep.tile([P, wd, PACK], BF16, name="res16_%d" % h, align_bytes=64)
+        for g, (first, wd) in enumerate(RANGES):
+            res[g] = keep.tile([P, PACK, wd], F32, name="res%d" % g, align_bytes=256)
+            res16[g] = keep.tile([P, wd, PACK], BF16, name="res16_%d" % g, align_bytes=64)
             for b in range(PACK * wd // BANK):
-                banks[h, b] = psum.tile([P, BANK // side, side], F32, name="acc%d_%d" % (h, b))
+                banks[g, b] = psum.tile([P, BANK // wd, wd], F32, name="acc%d_%d" % (g, b))
         o_codes = keep.tile([P, T], I32, align_bytes=256)
         o_scales = keep.tile([P, T], U8, align_bytes=256)
 
         zero = keep.tile([P, 1], F32)
         bias = keep.tile([P, 1], F32)
 
-        def place(h, r, t0):
-            first, wd, side = RANGES[h]
-            hands = BANK // side
-            return (t0 // side) * (PACK // hands) + r // hands, r % hands, t0 % side
-
         def load_x(a, t0, t1):
-            src = x[512 * a : 512 * (a + 1), t0:t1]
             piece = keep.tile([P, PACK, t1 - t0], F32, name="x%d_%d" % (a, t0), align_bytes=256)
-            for u, (h, b) in enumerate(units):
-                if b == a:
-                    xs.setdefault(u, []).append((t0 - RANGES[h][0], t1 - RANGES[h][0], piece))
+            xs[a].append((t0, t1, piece))
+            src = x[512 * a : 512 * (a + 1), t0:t1]
             nc.sync.dma_start(out=piece[:], in_=src.rearrange("(p j) t -> p j t", j=PACK))
 
-        def load_scales(src, row, r):
-            nc.sync.dma_start(
-                out=sc_raw[row + r : P : 32, :, :].bitcast(I32),
-                in_=src[:, r:16:4, :].rearrange("a q n -> q a n").bitcast(I32),
-            )
+        def load_scales(src, row):
+            for r in range(4):
+                nc.sync.dma_start(
+                    out=sc_raw[row + r : P : 32, :, :].bitcast(I32),
+                    in_=src[:, r:16:4, :].rearrange("a q n -> q a n").bitcast(I32),
+                )
 
         def load_w4(a0, a1):
             nc.sync.dma_start(
@@ -91,37 +85,41 @@ def tile_mix_feat_fm_quadpl_none_kernel(
                 in_=w8_words[a0:a1].rearrange("a p n i -> p a (n i)").bitcast(I32),
             )
 
-        def views(dst, src, t0, t1):
-            p0, p1, piece = [c for c in src if c[0] <= t0 and t1 <= c[1]][0]
+        def woven(dst, src):
             return (
-                dst[:, t0:t1, :].rearrange("p (c i) j -> p c j i", i=RUN),
-                piece[:, :, t0 - p0 : t1 - p0].rearrange("p j (c i) -> p c j i", i=RUN),
+                dst.rearrange("p (c i) j -> p c j i", i=RUN),
+                src.rearrange("p j (c i) -> p c j i", i=RUN),
             )
 
-        def cast_v(dst, src, t0, t1):
-            o, i = views(dst, src, t0, t1)
-            nc.vector.tensor_copy(out=o, in_=i)
+        def x_views(kind, a, t0, t1):
+            p0, p1, piece = [c for c in xs[a] if c[0] <= t0 and t1 <= c[1]][0]
+            h = t0 // HALF
+            return woven(wide[kind, a, h][:, t0 - h * HALF : t1 - h * HALF, :], piece[:, :, t0 - p0 : t1 - p0])
 
-        def cast_s(dst, src, t0, t1):
-            o, i = views(dst, src, t0, t1)
-            nc.scalar.copy(out=o, in_=i)
-
-        def square(u, t0, t1):
-            o, i = views(ga[u], xs[u], t0, t1)
+        def square(a, t0, t1):
+            o, i = x_views("a", a, t0, t1)
             nc.scalar.activation(out=o, in_=i, func=ACT.Square, bias=bias[:])
 
-        def quant(codes, scales, src, t0, t1, off=0):
+        def cast_v(a, t0, t1):
+            o, i = x_views("b", a, t0, t1)
+            nc.vector.tensor_copy(out=o, in_=i)
+
+        def cast_s(a, t0, t1):
+            o, i = x_views("b", a, t0, t1)
+            nc.scalar.copy(out=o, in_=i)
+
+        def cast_g(a, t0, t1):
+            o, i = x_views("b", a, t0, t1)
+            nc.gpsimd.tensor_scalar(out=o, in0=i, scalar1=1.0, scalar2=0.0, op0=ALU.mult, op1=ALU.add)
+
+        def quant(kind, a, t0, t1):
+            h = t0 // HALF
+            cols = slice(t0 - h * HALF, t1 - h * HALF)
             nc.vector.quantize_mx(
-                out=codes[:, off + t0 : off + t1].bitcast(FP8X4),
-                scales=scales[:, off + t0 : off + t1],
-                in_=src[:, t0:t1, :].rearrange("p t j -> p (t j)"),
+                out=codes[kind, a, h][:, cols].bitcast(FP8X4),
+                scales=scales[kind, a, h][:, cols],
+                in_=wide[kind, a, h][:, cols, :].rearrange("p t j -> p (t j)"),
             )
-
-        def qa(u, t0, t1):
-            quant(a_codes[u], a_scales[u], ga[u], t0, t1)
-
-        def qb(u, t0, t1):
-            quant(b_codes[u], b_scales[u], gb[u], t0, t1)
 
         def dealt(table, label, a0, a1, width, dtype):
             t = keep.tile([P, PACK, a1 - a0, width], dtype, name="%s%d" % (label, a0), align_bytes=64)
@@ -152,91 +150,76 @@ def tile_mix_feat_fm_quadpl_none_kernel(
 
         written = {}
 
-        def flags(h, b, n):
-            before = written.get((h, b), 0)
-            written[h, b] = before + n
-            return before == 0, before + n == 2 * PASSES * BANK
-
-        def mm_b(u, r, t0, t1):
-            h, a = units[u]
-            b, hand, c0 = place(h, r, t0)
-            start, stop = flags(h, b, t1 - t0)
+        def mm_cols(kind, a, g, r, c, n):
+            first, wd = RANGES[g]
+            hands = BANK // wd
+            b, hand = r // hands, r % hands
+            h = first // HALF
+            before = written.get((g, b), 0)
+            written[g, b] = before + n
+            cols = slice(first - h * HALF + c, first - h * HALF + c + n)
+            if kind == "b":
+                weights = w8[a][0][:, r, w8[a][1], :].bitcast(FP8X4)
+                plane = sc[a][0][W8_ROW:P, r, sc[a][1], :]
+            else:
+                weights = w4[a][0][:, r, w4[a][1], :].bitcast(FP4X4)
+                plane = sc[a][0][:, r, sc[a][1], :]
             nc.tensor.matmul_mx(
-                out=banks[h, b][:, hand, c0 : c0 + t1 - t0],
-                lhsT=w8[a][0][:, r, w8[a][1], :].bitcast(FP8X4),
-                lhsT_scale=sc[a][0][W8_ROW:P, r, sc[a][1], :],
-                rhs=b_codes[u][:, t0:t1].bitcast(FP8X4),
-                rhs_scale=b_scales[u][:, t0:t1],
-                start=start,
-                stop=stop,
+                out=banks[g, b][:, hand, c : c + n],
+                lhsT=weights,
+                lhsT_scale=plane,
+                rhs=codes[kind, a, h][:, cols].bitcast(FP8X4),
+                rhs_scale=scales[kind, a, h][:, cols],
+                start=before == 0,
+                stop=before + n == 2 * PASSES * BANK,
             )
 
-        def mm_a(u, r, t0, t1):
-            h, a = units[u]
-            b, hand, c0 = place(h, r, t0)
-            start, stop = flags(h, b, t1 - t0)
-            nc.tensor.matmul_mx(
-                out=banks[h, b][:, hand, c0 : c0 + t1 - t0],
-                lhsT=w4[a][0][:, r, w4[a][1], :].bitcast(FP4X4),
-                lhsT_scale=sc[a][0][:, r, sc[a][1], :],
-                rhs=a_codes[u][:, t0:t1].bitcast(FP8X4),
-                rhs_scale=a_scales[u][:, t0:t1],
-                start=start,
-                stop=stop,
-            )
+        def mm(kind, a, g, r):
+            wd = RANGES[g][1]
+            n = wd if kind == "b" or wd == BANK else P
+            for c in range(0, wd, n):
+                mm_cols(kind, a, g, r, c, n)
 
-        def mms_b(u, t0=0, t1=None):
-            first, wd, side = RANGES[units[u][0]]
-            for c in range(t0, wd if t1 is None else t1, side):
+        def mms_part(kind, a, g, c, n):
+            for r in range(PACK):
+                mm_cols(kind, a, g, r, c, n)
+
+        def mms(kind, a, *gs):
+            for g in gs:
                 for r in range(PACK):
-                    mm_b(u, r, c, c + side)
+                    mm(kind, a, g, r)
 
-        def mms_a(u, t0=0, t1=None):
-            first, wd, side = RANGES[units[u][0]]
-            n = BANK if side == BANK else P
-            for s0 in range(t0, wd if t1 is None else t1, side):
-                for r in range(PACK):
-                    for c in range(s0, s0 + side, n):
-                        mm_a(u, r, c, c + n)
+        def round_v(g, t0, t1):
+            o, i = woven(res16[g][:, t0:t1, :], res[g][:, :, t0:t1])
+            nc.vector.tensor_copy(out=o, in_=i)
 
-        def cast_xv(u, t0, t1):
-            cast_v(gb[u], xs[u], t0, t1)
+        def round_s(g, t0, t1):
+            o, i = woven(res16[g][:, t0:t1, :], res[g][:, :, t0:t1])
+            nc.scalar.copy(out=o, in_=i)
 
-        def cast_xs(u, t0, t1):
-            cast_s(gb[u], xs[u], t0, t1)
+        def drained(g, b):
+            hands = BANK // RANGES[g][1]
+            return res[g][:, b * hands : (b + 1) * hands, :]
 
-        def round_v(h, t0, t1):
-            cast_v(res16[h], [(0, T, res[h])], t0, t1)
+        def drain_s(g, b):
+            nc.scalar.copy(out=drained(g, b), in_=banks[g, b][:])
 
-        def round_s(h, t0, t1):
-            cast_s(res16[h], [(0, T, res[h])], t0, t1)
-
-        def drained(h, b):
-            first, wd, side = RANGES[h]
-            hands = BANK // side
-            r0, t0 = (b % (PACK // hands)) * hands, (b // (PACK // hands)) * side
-            return res[h][:, r0 : r0 + hands, t0 : t0 + side]
-
-        def drain_s(h, b):
-            nc.scalar.copy(out=drained(h, b), in_=banks[h, b][:])
-
-        def drain_v(h, b):
-            nc.vector.tensor_copy(out=drained(h, b), in_=banks[h, b][:])
-
-        def round_bank_v(h, b):
-            nc.vector.tensor_copy(
-                out=res16[h][:, P * b : P * (b + 1), :], in_=banks[h, b][:].rearrange("p r t -> p t r")
-            )
+        def drain_v(g, b):
+            nc.vector.tensor_copy(out=drained(g, b), in_=banks[g, b][:])
 
         out_rows = out_0.rearrange("(p r) t -> p r t", r=PACK)
 
-        def store_res(h, r0, r1, t0=0, t1=None):
-            first, wd, side = RANGES[h]
-            t1 = wd if t1 is None else t1
-            nc.sync.dma_start(out=out_rows[:, r0:r1, first + t0 : first + t1], in_=res[h][:, r0:r1, t0:t1])
+        def store_res(g, r0, r1):
+            first, wd = RANGES[g]
+            nc.sync.dma_start(out=out_rows[:, r0:r1, first : first + wd], in_=res[g][:, r0:r1, :])
 
-        def q_out(h, t0, t1):
-            quant(o_codes, o_scales, res16[h], t0, t1, off=RANGES[h][0])
+        def q_out(g, t0, t1):
+            first = RANGES[g][0]
+            nc.vector.quantize_mx(
+                out=o_codes[:, first + t0 : first + t1].bitcast(FP8X4),
+                scales=o_scales[:, first + t0 : first + t1],
+                in_=res16[g][:, t0:t1, :].rearrange("p t j -> p (t j)"),
+            )
 
         words_out = out_1[0].rearrange("p t i -> p (t i)").bitcast(I32)
 
@@ -253,97 +236,111 @@ def tile_mix_feat_fm_quadpl_none_kernel(
         nc.vector.memset(sc_raw[:].rearrange("p a n -> p (a n)").bitcast(I32), 0)
         nc.scalar.activation(out=bias[:], in_=zero[:], func=ACT.Square)
 
-        def sq(u):
-            square(u, 0, 512)
-
-        def xb(u):
-            cast_xv(u, 0, 512)
-
-        def do_b(u):
-            qb(u, 0, 512)
-            mms_b(u)
-
-        def do_a(u):
-            qa(u, 0, 512)
-            mms_a(u)
-
         load_x(0, 0, 512)
-        for r in range(4):
-            load_scales(w8_scales, W8_ROW, r)
+        load_scales(w8_scales, W8_ROW)
         load_x(0, 512, 1024)
-        for r in range(4):
-            load_scales(w4_scales, 0, r)
-        load_w8(0, 2)
+        load_scales(w4_scales, 0)
+        load_w8(0, 1)
         load_w4(0, 2)
         load_x(1, 0, 512)
-        load_w4(2, 4)
-        load_w8(2, 4)
         load_x(2, 0, 512)
+        load_w8(1, 3)
         load_x(3, 0, 512)
-        for a in range(1, 4):
-            load_x(a, 512, 1024)
+        load_w4(2, 4)
+        load_x(1, 512, 1024)
+        load_w8(3, 4)
+        load_x(2, 512, 1024)
+        load_x(3, 512, 1024)
 
-        order = [0, 4, 1, 2, 3, 5, 6, 7]
-        sq(0)
-        sq(4)
-        cast_xs(4, 128, 512)
-        xb(0)
-        qb(0, 0, 512)
-        qa(0, 0, 512)
+        square(0, 0, 512)
+        square(0, 512, 1024)
+        cast_s(0, 704, 1024)
+        cast_v(0, 0, 512)
+        quant("b", 0, 0, 512)
+        quant("a", 0, 0, 512)
+        cast_v(0, 512, 704)
         deal_scales(0, 4)
-        deal_w8(0, 2)
-        mms_b(0)
+        deal_w8(0, 1)
+        mms("b", 0, 0)
         deal_w4(0, 2)
-        mms_a(0)
-        cast_xv(4, 0, 128)
-        do_a(4)
+        mms("a", 0, 0)
+        quant("a", 0, 512, 1024)
+        mms("a", 0, 1)
 
-        sq(1)
-        cast_xs(1, 320, 512)
-        cast_xv(1, 0, 320)
-        do_b(4)
+        square(1, 0, 512)
+        cast_v(1, 0, 512)
+        quant("b", 0, 512, 1024)
+        mms("b", 0, 1)
+        quant("b", 1, 0, 512)
+        quant("a", 1, 0, 512)
+        mms("a", 1, 0)
+
+        square(2, 0, 512)
+        cast_s(2, 384, 512)
+        cast_v(2, 0, 384)
+        deal_w8(1, 3)
+        mms("b", 1, 0)
+        quant("a", 2, 0, 512)
+        quant("b", 2, 0, 512)
+        mms("b", 2, 0)
+
+        square(3, 0, 512)
+
+        cast_v(3, 0, 512)
         deal_w4(2, 4)
-        deal_w8(2, 4)
-        do_a(1)
-        do_b(1)
-        sq(2)
-        xb(2)
-        do_b(2)
+        mms("a", 2, 0)
+        quant("b", 3, 0, 512)
+        quant("a", 3, 0, 512)
+        mms("a", 3, 0)
 
-        for i in range(4, 7):
-            sq(order[i])
-            xb(order[i])
-            do_a(order[i - 1])
-            do_b(order[i])
+        square(1, 512, 1024)
+        cast_v(1, 512, 768)
+        deal_w8(3, 4)
+        mms("b", 3, 0)
+        cast_v(1, 768, 1024)
+        quant("b", 1, 512, 768)
+        quant("b", 1, 768, 1024)
+        mms("b", 1, 1)
         drain_s(0, 0)
-        store_res(0, 0, 1)
-
-        square(7, 0, 256)
-        square(7, 256, 512)
-        do_a(6)
-        xb(7)
-        qa(7, 0, 256)
-        qb(7, 0, 512)
-        qa(7, 256, 512)
-        for r in range(PACK):
-            mm_b(7, r, 0, 512)
-            mm_a(7, r, 0, 512)
-
-        drain_s(0, 1)
-        store_res(0, 1, 2)
+        quant("a", 1, 512, 1024)
+        mms("a", 1, 1)
+        drain_v(0, 1)
+        store_res(0, 0, 2)
+        square(2, 512, 1024)
+        cast_v(2, 512, 768)
+        cast_v(2, 768, 1024)
+        quant("b", 2, 512, 768)
+        quant("b", 2, 768, 1024)
+        mms("b", 2, 1)
         drain_s(0, 2)
-        drain_v(0, 3)
-        store_res(0, 2, 4)
-        round_v(0, 0, 512)
+        store_res(0, 2, 3)
+        square(3, 512, 768)
+        square(3, 768, 1024)
+        cast_v(3, 512, 768)
+        quant("a", 2, 512, 1024)
+        mms("a", 2, 1)
+        cast_v(3, 768, 1024)
+        quant("b", 3, 512, 768)
+        mms_part("b", 3, 1, 0, 256)
+        quant("a", 3, 512, 768)
+        quant("b", 3, 768, 1024)
+        quant("a", 3, 768, 1024)
+        for r in range(PACK):
+            mm_cols("b", 3, 1, r, 256, 256)
+            mm("a", 3, 1, r)
+        drain_s(0, 3)
+        store_res(0, 3, 4)
+        round_v(0, 0, 384)
+        round_s(0, 384, 512)
+        q_out(0, 0, 512)
         drain_s(1, 0)
         store_res(1, 0, 1)
+        store_words(0, 512)
         drain_s(1, 1)
         store_res(1, 1, 2)
         drain_v(1, 2)
-        q_out(0, 0, 512)
         drain_s(1, 3)
         store_res(1, 2, 4)
-        store_words(0, 512)
         round_v(1, 0, 256)
         round_s(1, 384, 512)
         round_v(1, 256, 384)

@@ -251,7 +251,6 @@ def tile_mix_feat_fm_quadpl_none_kernel(
         load_w8(3, 4)
         load_x(2, 512, 1024)
         load_x(3, 512, 1024)
-
         square(0, 0, 512)
         square(0, 512, 1024)
         cast_s(0, 704, 1024)
@@ -266,7 +265,6 @@ def tile_mix_feat_fm_quadpl_none_kernel(
         mms("a", 0, 0)
         quant("a", 0, 512, 1024)
         mms("a", 0, 1)
-
         square(1, 0, 512)
         cast_v(1, 0, 512)
         quant("b", 0, 512, 1024)
@@ -274,76 +272,65 @@ def tile_mix_feat_fm_quadpl_none_kernel(
         quant("b", 1, 0, 512)
         quant("a", 1, 0, 512)
         mms("a", 1, 0)
-
         square(2, 0, 512)
         cast_s(2, 384, 512)
         cast_v(2, 0, 384)
         deal_w8(1, 3)
         mms("b", 1, 0)
         quant("a", 2, 0, 512)
+        square(3, 0, 512)
+        cast_s(3, 384, 512)
+        cast_v(3, 0, 384)
         quant("b", 2, 0, 512)
         mms("b", 2, 0)
-
-        square(3, 0, 512)
-
-        cast_v(3, 0, 512)
         deal_w4(2, 4)
         mms("a", 2, 0)
-        quant("b", 3, 0, 512)
         quant("a", 3, 0, 512)
         mms("a", 3, 0)
-
         square(1, 512, 1024)
-        cast_v(1, 512, 768)
+        quant("b", 3, 0, 512)
+        cast_v(1, 512, 1024)
         deal_w8(3, 4)
         mms("b", 3, 0)
-        cast_v(1, 768, 1024)
-        quant("b", 1, 512, 768)
-        quant("b", 1, 768, 1024)
+        quant("b", 1, 512, 1024)
         mms("b", 1, 1)
-        drain_s(0, 0)
+        square(2, 512, 1024)
+        cast_v(2, 512, 1024)
         quant("a", 1, 512, 1024)
         mms("a", 1, 1)
-        drain_v(0, 1)
-        store_res(0, 0, 2)
-        square(2, 512, 1024)
-        cast_v(2, 512, 768)
-        cast_v(2, 768, 1024)
-        quant("b", 2, 512, 768)
-        quant("b", 2, 768, 1024)
+        quant("b", 2, 512, 1024)
         mms("b", 2, 1)
-        drain_s(0, 2)
-        store_res(0, 2, 3)
+        drain_s(0, 0)
+        store_res(0, 0, 1)
         square(3, 512, 768)
         square(3, 768, 1024)
-        cast_v(3, 512, 768)
         quant("a", 2, 512, 1024)
         mms("a", 2, 1)
-        cast_v(3, 768, 1024)
-        quant("b", 3, 512, 768)
-        mms_part("b", 3, 1, 0, 256)
+        cast_v(3, 512, 1024)
         quant("a", 3, 512, 768)
-        quant("b", 3, 768, 1024)
+        quant("b", 3, 512, 1024)
         quant("a", 3, 768, 1024)
         for r in range(PACK):
-            mm_cols("b", 3, 1, r, 256, 256)
+            mm("b", 3, 1, r)
             mm("a", 3, 1, r)
-        drain_s(0, 3)
-        store_res(0, 3, 4)
-        round_v(0, 0, 384)
-        round_s(0, 384, 512)
-        q_out(0, 0, 512)
+        drain_s(0, 1)
+        store_res(0, 1, 2)
+        drain_s(0, 2)
+        drain_v(0, 3)
+        store_res(0, 2, 4)
+        round_v(0, 0, 512)
         drain_s(1, 0)
         store_res(1, 0, 1)
-        store_words(0, 512)
         drain_s(1, 1)
         store_res(1, 1, 2)
-        drain_v(1, 2)
+        q_out(0, 0, 512)
+        store_words(0, 512)
+        drain_s(1, 2)
         drain_s(1, 3)
         store_res(1, 2, 4)
         round_v(1, 0, 256)
-        round_s(1, 384, 512)
-        round_v(1, 256, 384)
+        round_s(1, 320, 512)
+        round_v(1, 256, 320)
         q_out(1, 0, 256)
         store_words(512, 768)
         q_out(1, 256, 512)

@@ -130,22 +130,22 @@ def tile_mix_feat_fm_quadpl_none_kernel(
         def deal_w4(a0, a1):
             t = dealt(w4, "w4d", a0, a1, 2 * P, U8)
             nc.vector.tensor_copy(
-                out=t[:].bitcast(U16).rearrange("p r a (c i) -> p (a c) r i", i=8),
-                in_=w4_raw[:, a0:a1, :].bitcast(U16).rearrange("p a (c i r) -> p (a c) r i", r=PACK, i=8),
+                out=t[:].bitcast(U16).rearrange("p (g r) a (c i) -> p g (a c) r i", g=2, i=4),
+                in_=w4_raw[:, a0:a1, :].bitcast(U16).rearrange("p a (c i g r) -> p g (a c) r i", g=2, r=2, i=4),
             )
 
         def deal_w8(a0, a1):
             t = dealt(w8, "w8d", a0, a1, P, I32)
             nc.vector.tensor_copy(
-                out=t[:].rearrange("p r a (c i) -> p (a c) r i", i=4),
-                in_=w8_raw[:, a0:a1, :].rearrange("p a (c i r) -> p (a c) r i", r=PACK, i=4),
+                out=t[:].rearrange("p (g r) a (c i) -> p g (a c) r i", g=2, i=2),
+                in_=w8_raw[:, a0:a1, :].rearrange("p a (c i g r) -> p g (a c) r i", g=2, r=2, i=2),
             )
 
         def deal_scales(a0, a1):
             t = dealt(sc, "scd", a0, a1, P, U8)
             nc.vector.tensor_copy(
-                out=t[:].rearrange("p r a (c i) -> p (a c) r i", i=16),
-                in_=sc_raw[:, a0:a1, :].rearrange("p a (c i r) -> p (a c) r i", r=PACK, i=16),
+                out=t[:].rearrange("p (g r) a (c i) -> p g (a c) r i", g=2, i=8),
+                in_=sc_raw[:, a0:a1, :].rearrange("p a (c i g r) -> p g (a c) r i", g=2, r=2, i=8),
             )
 
         written = {}
@@ -228,8 +228,8 @@ def tile_mix_feat_fm_quadpl_none_kernel(
 
         def store_scales(q):
             (nc.scalar if q < 2 else nc.sync).dma_start(
-                out=out_2[0, 4 * q : 4 * q + 4, :].bitcast(I32),
-                in_=o_scales[32 * q : 32 * q + 4, :].bitcast(I32),
+                out=out_2[0, q:16:4, :].bitcast(I32),
+                in_=o_scales[q:P:32, :].bitcast(I32),
             )
 
         nc.vector.memset(zero[:], 0.0)

@@ -207,6 +207,12 @@ def tile_mix_feat_fm_quadpl_none_kernel(
         def drain_v(g, b):
             nc.vector.tensor_copy(out=drained(g, b), in_=banks[g, b][:])
 
+        def drain_v_cols(g, b, t0, t1):
+            nc.vector.tensor_copy(out=res[g][:, b, t0:t1], in_=banks[g, b][:, 0, t0:t1])
+
+        def drain_s_cols(g, b, t0, t1):
+            nc.scalar.copy(out=res[g][:, b, t0:t1], in_=banks[g, b][:, 0, t0:t1])
+
         out_rows = out_0.rearrange("(p r) t -> p r t", r=PACK)
 
         def store_res(g, r0, r1):
@@ -278,17 +284,17 @@ def tile_mix_feat_fm_quadpl_none_kernel(
         deal_w8(1, 3)
         mms("b", 1, 0)
         quant("a", 2, 0, 512)
-        square(3, 0, 512)
-        cast_s(3, 384, 512)
-        cast_v(3, 0, 384)
         quant("b", 2, 0, 512)
         mms("b", 2, 0)
+        cast_s(3, 448, 512)
+        square(3, 0, 512)
+        cast_v(3, 0, 448)
         deal_w4(2, 4)
         mms("a", 2, 0)
+        quant("b", 3, 0, 512)
         quant("a", 3, 0, 512)
         mms("a", 3, 0)
         square(1, 512, 1024)
-        quant("b", 3, 0, 512)
         cast_v(1, 512, 1024)
         deal_w8(3, 4)
         mms("b", 3, 0)
@@ -316,21 +322,25 @@ def tile_mix_feat_fm_quadpl_none_kernel(
         drain_s(0, 1)
         store_res(0, 1, 2)
         drain_s(0, 2)
+        store_res(0, 2, 3)
         drain_v(0, 3)
-        store_res(0, 2, 4)
-        round_v(0, 0, 512)
+        store_res(0, 3, 4)
+        round_v(0, 0, 256)
+        round_v(0, 256, 512)
         drain_s(1, 0)
         store_res(1, 0, 1)
         drain_s(1, 1)
         store_res(1, 1, 2)
-        q_out(0, 0, 512)
+        q_out(0, 0, 256)
+        q_out(0, 256, 512)
         store_words(0, 512)
         drain_s(1, 2)
-        drain_s(1, 3)
+        drain_s_cols(1, 3, 0, 256)
+        drain_s_cols(1, 3, 256, 512)
         store_res(1, 2, 4)
         round_v(1, 0, 256)
-        round_s(1, 320, 512)
-        round_v(1, 256, 320)
+        round_s(1, 352, 512)
+        round_v(1, 256, 352)
         q_out(1, 0, 256)
         store_words(512, 768)
         q_out(1, 256, 512)

@@ -40,14 +40,19 @@ def tile_mix_feat_fm_quadpl_none_kernel(
         sc_raw = keep.tile([P, PASSES, M], U8, align_bytes=256)
         w4, w8, sc = {}, {}, {}
         codes, scales, wide = {}, {}, {}
-        for kind in "ab":
-            for a in range(PASSES):
-                for h in range(T // HALF):
-                    key = (kind, a, h)
-                    label = "%s%d%d" % key
-                    codes[key] = keep.tile([P, HALF], I32, name="c" + label, align_bytes=64)
-                    scales[key] = keep.tile([P, HALF], U8, name="s" + label, align_bytes=64)
-                    wide[key] = keep.tile([P, HALF, PACK], BF16, name="g" + label, align_bytes=64)
+        both = {}
+        for a in range(PASSES):
+            for h in range(T // HALF):
+                label = "%d%d" % (a, h)
+                c = keep.tile([P, 2 * HALF], I32, name="c" + label, align_bytes=64)
+                s = keep.tile([P, 2 * HALF], U8, name="s" + label, align_bytes=64)
+                g = keep.tile([P, 2 * HALF, PACK], BF16, name="g" + label, align_bytes=64)
+                both[a, h] = (c, s, g)
+                for side, kind in enumerate("ab"):
+                    cols = slice(side * HALF, (side + 1) * HALF)
+                    codes[kind, a, h] = c[:, cols]
+                    scales[kind, a, h] = s[:, cols]
+                    wide[kind, a, h] = g[:, cols, :]
         res, res16, banks = {}, {}, {}
         for g, (first, wd) in enumerate(RANGES):
             res[g] = keep.tile([P, PACK, wd], F32, name="res%d" % g, align_bytes=256)
@@ -66,12 +71,35 @@ def tile_mix_feat_fm_quadpl_none_kernel(
             src = x[512 * a : 512 * (a + 1), t0:t1]
             nc.sync.dma_start(out=piece[:], in_=src.rearrange("(p j) t -> p j t", j=PACK))
 
+        joined = {}
+
+        def load_x2(a, t0):
+            both_parts = keep.tile([P, 2, PACK, HALF // 2], F32, name="x%d_%d" % (a, t0), align_bytes=256)
+            joined[a, t0] = both_parts
+            for s in range(2):
+                c0 = t0 + s * (HALF // 2)
+                xs[a].append((c0, c0 + HALF // 2, both_parts[:, s, :, :]))
+                src = x[512 * a : 512 * (a + 1), c0 : c0 + HALF // 2]
+                nc.sync.dma_start(out=both_parts[:, s, :, :], in_=src.rearrange("(p j) t -> p j t", j=PACK))
+
+        def cast_v2(a, t0):
+            nc.vector.tensor_copy(
+                out=wide["b", a, t0 // HALF].rearrange("p (s c i) j -> p s c j i", s=2, i=RUN),
+                in_=joined[a, t0][:].rearrange("p s j (c i) -> p s c j i", i=RUN),
+            )
+
         def load_scales(src, row):
             for r in range(4):
                 nc.sync.dma_start(
                     out=sc_raw[row + r : P : 32, :, :].bitcast(I32),
                     in_=src[:, r:16:4, :].rearrange("a q n -> q a n").bitcast(I32),
                 )
+
+        def load_sc(src, row, r):
+            nc.sync.dma_start(
+                out=sc_raw[row + r : P : 32, :, :].bitcast(I32),
+                in_=src[:, r:16:4, :].rearrange("a q n -> q a n").bitcast(I32),
+            )
 
         def load_w4(a0, a1):
             nc.sync.dma_start(
@@ -119,6 +147,12 @@ def tile_mix_feat_fm_quadpl_none_kernel(
                 out=codes[kind, a, h][:, cols].bitcast(FP8X4),
                 scales=scales[kind, a, h][:, cols],
                 in_=wide[kind, a, h][:, cols, :].rearrange("p t j -> p (t j)"),
+            )
+
+        def quant_both(a, h):
+            c, s, g = both[a, h]
+            nc.vector.quantize_mx(
+                out=c[:].bitcast(FP8X4), scales=s[:], in_=g[:].rearrange("p t j -> p (t j)")
             )
 
         def dealt(table, label, a0, a1, width, dtype):
@@ -243,9 +277,15 @@ def tile_mix_feat_fm_quadpl_none_kernel(
         nc.scalar.activation(out=bias[:], in_=zero[:], func=ACT.Square)
 
         load_x(0, 0, 512)
-        load_scales(w8_scales, W8_ROW)
+        load_sc(w8_scales, W8_ROW, 0)
+        load_sc(w8_scales, W8_ROW, 1)
+        load_sc(w8_scales, W8_ROW, 2)
+        load_sc(w8_scales, W8_ROW, 3)
         load_x(0, 512, 1024)
-        load_scales(w4_scales, 0)
+        load_sc(w4_scales, 0, 0)
+        load_sc(w4_scales, 0, 1)
+        load_sc(w4_scales, 0, 2)
+        load_sc(w4_scales, 0, 3)
         load_w8(0, 1)
         load_w4(0, 2)
         load_x(1, 0, 512)
@@ -259,91 +299,98 @@ def tile_mix_feat_fm_quadpl_none_kernel(
         load_x(3, 512, 1024)
         square(0, 0, 512)
         square(0, 512, 1024)
-        cast_s(0, 704, 1024)
+        cast_s(0, 640, 1024)
+        square(1, 0, 512)
+        square(2, 0, 512)
+        cast_s(2, 320, 512)
+        cast_s(3, 448, 512)
+        square(3, 0, 512)
+        cast_s(1, 896, 1024)
+        square(1, 512, 1024)
+        square(2, 512, 1024)
         cast_v(0, 0, 512)
         quant("b", 0, 0, 512)
         quant("a", 0, 0, 512)
-        cast_v(0, 512, 704)
+        cast_v(0, 512, 640)
         deal_scales(0, 4)
         deal_w8(0, 1)
-        mms("b", 0, 0)
         deal_w4(0, 2)
-        mms("a", 0, 0)
         quant("a", 0, 512, 1024)
-        mms("a", 0, 1)
-        square(1, 0, 512)
         cast_v(1, 0, 512)
         quant("b", 0, 512, 1024)
-        mms("b", 0, 1)
         quant("b", 1, 0, 512)
         quant("a", 1, 0, 512)
-        mms("a", 1, 0)
-        square(2, 0, 512)
-        cast_s(2, 384, 512)
-        cast_v(2, 0, 384)
+        cast_v(2, 0, 320)
         deal_w8(1, 3)
-        mms("b", 1, 0)
         quant("a", 2, 0, 512)
         quant("b", 2, 0, 512)
-        mms("b", 2, 0)
-        cast_s(3, 448, 512)
-        square(3, 0, 512)
         cast_v(3, 0, 448)
         deal_w4(2, 4)
-        mms("a", 2, 0)
-        quant("b", 3, 0, 512)
-        quant("a", 3, 0, 512)
-        mms("a", 3, 0)
-        square(1, 512, 1024)
-        cast_v(1, 512, 1024)
+        quant_both(3, 0)
+        cast_v(1, 512, 896)
         deal_w8(3, 4)
-        mms("b", 3, 0)
         quant("b", 1, 512, 1024)
-        mms("b", 1, 1)
-        square(2, 512, 1024)
         cast_v(2, 512, 1024)
         quant("a", 1, 512, 1024)
-        mms("a", 1, 1)
         quant("b", 2, 512, 1024)
+        quant("a", 2, 512, 1024)
+        cast_v(3, 512, 1024)
+        mms("b", 0, 0)
+        mms("a", 0, 0)
+        mms("a", 0, 1)
+        mms("b", 0, 1)
+        mms("a", 1, 0)
+        mms("b", 1, 0)
+        mms("b", 2, 0)
+        mms("a", 2, 0)
+        mms("a", 3, 0)
+        mms("b", 3, 0)
+        mms("b", 1, 1)
+        mms("a", 1, 1)
         mms("b", 2, 1)
+        mms("a", 2, 1)
         drain_s(0, 0)
-        store_res(0, 0, 1)
         square(3, 512, 768)
         square(3, 768, 1024)
-        quant("a", 2, 512, 1024)
-        mms("a", 2, 1)
-        cast_v(3, 512, 1024)
+        drain_s(0, 1)
+        drain_s(0, 2)
         quant("a", 3, 512, 768)
         quant("b", 3, 512, 1024)
         quant("a", 3, 768, 1024)
-        for r in range(PACK):
-            mm("b", 3, 1, r)
-            mm("a", 3, 1, r)
-        drain_s(0, 1)
-        store_res(0, 1, 2)
-        drain_s(0, 2)
-        store_res(0, 2, 3)
         drain_v(0, 3)
-        store_res(0, 3, 4)
         round_v(0, 0, 256)
         round_v(0, 256, 512)
-        drain_s(1, 0)
-        store_res(1, 0, 1)
-        drain_s(1, 1)
-        store_res(1, 1, 2)
         q_out(0, 0, 256)
         q_out(0, 256, 512)
-        store_words(0, 512)
+        mm("b", 3, 1, 0)
+        mm("a", 3, 1, 0)
+        mm("b", 3, 1, 1)
+        mm("a", 3, 1, 1)
+        mm("b", 3, 1, 2)
+        mm("a", 3, 1, 2)
+        mm("b", 3, 1, 3)
+        mm("a", 3, 1, 3)
+        store_res(0, 0, 1)
+        store_res(0, 1, 2)
+        store_res(0, 2, 3)
+        store_res(0, 3, 4)
+        drain_s(1, 0)
+        drain_s(1, 1)
         drain_s(1, 2)
         drain_s_cols(1, 3, 0, 256)
         drain_s_cols(1, 3, 256, 512)
-        store_res(1, 2, 4)
-        round_v(1, 0, 256)
         round_s(1, 352, 512)
+        round_v(1, 0, 256)
         round_v(1, 256, 352)
         q_out(1, 0, 256)
-        store_words(512, 768)
         q_out(1, 256, 512)
+        store_res(1, 0, 1)
+        store_res(1, 1, 2)
+        store_words(0, 512)
+        store_res(1, 2, 4)
+        store_words(512, 768)
         store_words(768, 1024)
-        for q in range(4):
-            store_scales(q)
+        store_scales(0)
+        store_scales(1)
+        store_scales(2)
+        store_scales(3)

@@ -88,6 +88,31 @@ def tile_mix_feat_fm_quadpl_none_kernel(
                 in_=joined[a, t0][:].rearrange("p s j (c i) -> p s c j i", i=RUN),
             )
 
+        def load_xh(a, t0, s):
+            if (a, t0) not in joined:
+                joined[a, t0] = keep.tile([P, 2, PACK, HALF // 2], F32, name="x%d_%d" % (a, t0), align_bytes=256)
+            c0 = t0 + s * (HALF // 2)
+            part = joined[a, t0][:, s, :, :]
+            xs[a].append((c0, c0 + HALF // 2, part))
+            src = x[512 * a : 512 * (a + 1), c0 : c0 + HALF // 2]
+            nc.sync.dma_start(out=part, in_=src.rearrange("(p j) t -> p j t", j=PACK))
+
+        def pair_views(a, t0, c0, c1):
+            dst = wide["b", a, t0 // HALF].rearrange("p (s t) j -> p s t j", s=2)[:, :, c0:c1, :]
+            src = joined[a, t0][:, :, :, c0:c1]
+            return (
+                dst.rearrange("p s (c i) j -> p s c j i", i=RUN),
+                src.rearrange("p s j (c i) -> p s c j i", i=RUN),
+            )
+
+        def cast_vj(a, t0, w):
+            o, i = pair_views(a, t0, 0, w)
+            nc.vector.tensor_copy(out=o, in_=i)
+
+        def cast_sj(a, t0, w):
+            o, i = pair_views(a, t0, w, HALF // 2)
+            nc.scalar.copy(out=o, in_=i)
+
         def load_scales(src, row):
             for r in range(4):
                 nc.sync.dma_start(
@@ -276,65 +301,89 @@ def tile_mix_feat_fm_quadpl_none_kernel(
         nc.vector.memset(sc_raw[:].rearrange("p a n -> p (a n)").bitcast(I32), 0)
         nc.scalar.activation(out=bias[:], in_=zero[:], func=ACT.Square)
 
-        load_x(0, 0, 512)
+        load_xh(0, 0, 0)
         load_sc(w8_scales, W8_ROW, 0)
         load_sc(w8_scales, W8_ROW, 1)
+        load_xh(0, 0, 1)
         load_sc(w8_scales, W8_ROW, 2)
         load_sc(w8_scales, W8_ROW, 3)
-        load_x(0, 512, 1024)
+        load_xh(0, 512, 0)
+        load_xh(0, 512, 1)
         load_sc(w4_scales, 0, 0)
         load_sc(w4_scales, 0, 1)
         load_sc(w4_scales, 0, 2)
         load_sc(w4_scales, 0, 3)
         load_w8(0, 1)
         load_w4(0, 2)
-        load_x(1, 0, 512)
-        load_x(2, 0, 512)
+        load_xh(1, 0, 0)
+        load_xh(1, 0, 1)
+        load_xh(2, 0, 0)
+        load_xh(2, 0, 1)
         load_w8(1, 3)
-        load_x(3, 0, 512)
+        load_xh(3, 0, 0)
+        load_xh(3, 0, 1)
         load_w4(2, 4)
-        load_x(1, 512, 1024)
+        load_xh(1, 512, 0)
+        load_xh(1, 512, 1)
         load_w8(3, 4)
-        load_x(2, 512, 1024)
-        load_x(3, 512, 1024)
-        square(0, 0, 512)
-        square(0, 512, 1024)
-        cast_s(0, 640, 1024)
-        square(1, 0, 512)
-        square(2, 0, 512)
-        cast_s(2, 320, 512)
-        cast_s(3, 448, 512)
-        square(3, 0, 512)
+        load_xh(2, 512, 0)
+        load_xh(2, 512, 1)
+        load_xh(3, 512, 0)
+        load_xh(3, 512, 1)
+        square(0, 0, 256)
+        square(0, 256, 512)
+        square(0, 512, 768)
+        cast_s(0, 768, 1024)
+        square(0, 768, 1024)
+        square(1, 0, 256)
+        square(1, 256, 512)
+        square(2, 0, 256)
+        square(2, 256, 512)
+        cast_sj(2, 0, 160)
+        square(3, 0, 256)
+        square(3, 256, 512)
+        cast_sj(3, 0, 224)
+        square(1, 512, 768)
         cast_s(1, 896, 1024)
-        square(1, 512, 1024)
-        square(2, 512, 1024)
-        cast_v(0, 0, 512)
+        square(1, 768, 1024)
+        square(2, 512, 768)
+        square(2, 768, 1024)
+        square(3, 512, 768)
+        square(3, 768, 1024)
+        cast_v(0, 0, 256)
+        cast_v(0, 256, 512)
         quant("b", 0, 0, 512)
         quant("a", 0, 0, 512)
-        cast_v(0, 512, 640)
+        cast_v(0, 512, 768)
         deal_scales(0, 4)
         deal_w8(0, 1)
         deal_w4(0, 2)
         quant("a", 0, 512, 1024)
-        cast_v(1, 0, 512)
+        cast_v(1, 0, 256)
+        cast_v(1, 256, 512)
         quant("b", 0, 512, 1024)
-        quant("b", 1, 0, 512)
-        quant("a", 1, 0, 512)
-        cast_v(2, 0, 320)
+        quant_both(1, 0)
+        cast_vj(2, 0, 160)
         deal_w8(1, 3)
         quant("a", 2, 0, 512)
         quant("b", 2, 0, 512)
-        cast_v(3, 0, 448)
+        cast_vj(3, 0, 224)
         deal_w4(2, 4)
         quant_both(3, 0)
-        cast_v(1, 512, 896)
+        cast_v(1, 512, 768)
+        cast_v(1, 768, 896)
         deal_w8(3, 4)
         quant("b", 1, 512, 1024)
-        cast_v(2, 512, 1024)
+        cast_v(2, 512, 768)
         quant("a", 1, 512, 1024)
+        cast_v(2, 768, 1024)
+        cast_v(3, 512, 768)
         quant("b", 2, 512, 1024)
         quant("a", 2, 512, 1024)
-        cast_v(3, 512, 1024)
+        cast_v(3, 768, 1024)
+        quant("a", 3, 512, 768)
+        quant("b", 3, 512, 1024)
+        quant("a", 3, 768, 1024)
         mms("b", 0, 0)
         mms("a", 0, 0)
         mms("a", 0, 1)
@@ -349,19 +398,6 @@ def tile_mix_feat_fm_quadpl_none_kernel(
         mms("a", 1, 1)
         mms("b", 2, 1)
         mms("a", 2, 1)
-        drain_s(0, 0)
-        square(3, 512, 768)
-        square(3, 768, 1024)
-        drain_s(0, 1)
-        drain_s(0, 2)
-        quant("a", 3, 512, 768)
-        quant("b", 3, 512, 1024)
-        quant("a", 3, 768, 1024)
-        drain_v(0, 3)
-        round_v(0, 0, 256)
-        round_v(0, 256, 512)
-        q_out(0, 0, 256)
-        q_out(0, 256, 512)
         mm("b", 3, 1, 0)
         mm("a", 3, 1, 0)
         mm("b", 3, 1, 1)
@@ -370,20 +406,28 @@ def tile_mix_feat_fm_quadpl_none_kernel(
         mm("a", 3, 1, 2)
         mm("b", 3, 1, 3)
         mm("a", 3, 1, 3)
-        store_res(0, 0, 1)
-        store_res(0, 1, 2)
-        store_res(0, 2, 3)
-        store_res(0, 3, 4)
+        drain_s(0, 0)
+        drain_s(0, 1)
+        drain_s(0, 2)
         drain_s(1, 0)
         drain_s(1, 1)
         drain_s(1, 2)
         drain_s_cols(1, 3, 0, 256)
         drain_s_cols(1, 3, 256, 512)
-        round_s(1, 352, 512)
+        round_s(1, 384, 512)
+        drain_v(0, 3)
+        round_v(0, 0, 256)
+        round_v(0, 256, 512)
+        q_out(0, 0, 256)
+        q_out(0, 256, 512)
         round_v(1, 0, 256)
-        round_v(1, 256, 352)
+        round_v(1, 256, 384)
         q_out(1, 0, 256)
         q_out(1, 256, 512)
+        store_res(0, 0, 1)
+        store_res(0, 1, 2)
+        store_res(0, 2, 3)
+        store_res(0, 3, 4)
         store_res(1, 0, 1)
         store_res(1, 1, 2)
         store_words(0, 512)

@@ -13,16 +13,17 @@ U16 = mybir.dt.uint16
 FP8X4 = mybir.dt.float8_e4m3fn_x4
 FP4X4 = mybir.dt.float4_e2m1fn_x4
 ACT = mybir.ActivationFunctionType
-ALU = mybir.AluOpType
 
 P = 128
 PACK = 4
 PASSES = K // (P * PACK)
-BANK = 512
 HALF = 512
-W8_ROW = 4
+PIECE = HALF // 2
+QUADRANT = 32
 RUN = 4
-RANGES = [(0, 512), (512, 512)]
+
+VECTOR_KEEPS = {(2, 0): 160, (3, 0): 224, (1, 1): 192}
+LAST_VECTOR = 384
 
 
 def tile_mix_feat_fm_quadpl_none_kernel(
@@ -34,97 +35,57 @@ def tile_mix_feat_fm_quadpl_none_kernel(
         psum = ctx.enter_context(tc.psum_pool(name="psum", bufs=1))
         ctx.enter_context(tc.manual_schedule())
 
-        xs = {a: [] for a in range(PASSES)}
         w4_raw = keep.tile([P, PASSES, 2 * M], U8, align_bytes=256)
         w8_raw = keep.tile([P, PASSES, M], I32, align_bytes=256)
-        sc_raw = keep.tile([P, PASSES, M], U8, align_bytes=256)
-        w4, w8, sc = {}, {}, {}
-        codes, scales, wide = {}, {}, {}
-        both = {}
+        sc_raw = keep.tile([P, PASSES + 1, M], U8, align_bytes=256)
+        sc8 = keep.tile([P, PACK, P], U8, align_bytes=64)
+        w4, w8, sc4 = {}, {}, {}
+
+        units = {}
         for a in range(PASSES):
             for h in range(T // HALF):
                 label = "%d%d" % (a, h)
-                c = keep.tile([P, 2 * HALF], I32, name="c" + label, align_bytes=64)
-                s = keep.tile([P, 2 * HALF], U8, name="s" + label, align_bytes=64)
-                g = keep.tile([P, 2 * HALF, PACK], BF16, name="g" + label, align_bytes=64)
-                both[a, h] = (c, s, g)
-                for side, kind in enumerate("ab"):
-                    cols = slice(side * HALF, (side + 1) * HALF)
-                    codes[kind, a, h] = c[:, cols]
-                    scales[kind, a, h] = s[:, cols]
-                    wide[kind, a, h] = g[:, cols, :]
+                units[a, h] = (
+                    keep.tile([P, 2 * HALF], I32, name="c" + label, align_bytes=64),
+                    keep.tile([P, 2 * HALF], U8, name="s" + label, align_bytes=64),
+                    keep.tile([P, 2 * HALF, PACK], BF16, name="g" + label, align_bytes=64),
+                )
         res, res16, banks = {}, {}, {}
-        for g, (first, wd) in enumerate(RANGES):
-            res[g] = keep.tile([P, PACK, wd], F32, name="res%d" % g, align_bytes=256)
-            res16[g] = keep.tile([P, wd, PACK], BF16, name="res16_%d" % g, align_bytes=64)
-            for b in range(PACK * wd // BANK):
-                banks[g, b] = psum.tile([P, BANK // wd, wd], F32, name="acc%d_%d" % (g, b))
+        for h in range(T // HALF):
+            res[h] = keep.tile([P, PACK, HALF], F32, name="res%d" % h, align_bytes=256)
+            res16[h] = keep.tile([P, HALF, PACK], BF16, name="res16_%d" % h, align_bytes=64)
+            for r in range(PACK):
+                banks[h, r] = psum.tile([P, HALF], F32, name="acc%d_%d" % (h, r))
         o_codes = keep.tile([P, T], I32, align_bytes=256)
         o_scales = keep.tile([P, T], U8, align_bytes=256)
-
         zero = keep.tile([P, 1], F32)
         bias = keep.tile([P, 1], F32)
+        xs = {}
 
-        def load_x(a, t0, t1):
-            piece = keep.tile([P, PACK, t1 - t0], F32, name="x%d_%d" % (a, t0), align_bytes=256)
-            xs[a].append((t0, t1, piece))
-            src = x[512 * a : 512 * (a + 1), t0:t1]
-            nc.sync.dma_start(out=piece[:], in_=src.rearrange("(p j) t -> p j t", j=PACK))
+        def load_piece(a, h, s):
+            if s == 0:
+                xs[a, h] = keep.tile([P, 2, PACK, PIECE], F32, name="x%d%d" % (a, h), align_bytes=256)
+            t0 = h * HALF + s * PIECE
+            src = x[P * PACK * a : P * PACK * (a + 1), t0 : t0 + PIECE]
+            nc.sync.dma_start(out=xs[a, h][:, s, :, :], in_=src.rearrange("(p j) t -> p j t", j=PACK))
 
-        joined = {}
+        def load_unit(a, h):
+            load_piece(a, h, 0)
+            load_piece(a, h, 1)
 
-        def load_x2(a, t0):
-            both_parts = keep.tile([P, 2, PACK, HALF // 2], F32, name="x%d_%d" % (a, t0), align_bytes=256)
-            joined[a, t0] = both_parts
-            for s in range(2):
-                c0 = t0 + s * (HALF // 2)
-                xs[a].append((c0, c0 + HALF // 2, both_parts[:, s, :, :]))
-                src = x[512 * a : 512 * (a + 1), c0 : c0 + HALF // 2]
-                nc.sync.dma_start(out=both_parts[:, s, :, :], in_=src.rearrange("(p j) t -> p j t", j=PACK))
-
-        def cast_v2(a, t0):
-            nc.vector.tensor_copy(
-                out=wide["b", a, t0 // HALF].rearrange("p (s c i) j -> p s c j i", s=2, i=RUN),
-                in_=joined[a, t0][:].rearrange("p s j (c i) -> p s c j i", i=RUN),
-            )
-
-        def load_xh(a, t0, s):
-            if (a, t0) not in joined:
-                joined[a, t0] = keep.tile([P, 2, PACK, HALF // 2], F32, name="x%d_%d" % (a, t0), align_bytes=256)
-            c0 = t0 + s * (HALF // 2)
-            part = joined[a, t0][:, s, :, :]
-            xs[a].append((c0, c0 + HALF // 2, part))
-            src = x[512 * a : 512 * (a + 1), c0 : c0 + HALF // 2]
-            nc.sync.dma_start(out=part, in_=src.rearrange("(p j) t -> p j t", j=PACK))
-
-        def pair_views(a, t0, c0, c1):
-            dst = wide["b", a, t0 // HALF].rearrange("p (s t) j -> p s t j", s=2)[:, :, c0:c1, :]
-            src = joined[a, t0][:, :, :, c0:c1]
-            return (
-                dst.rearrange("p s (c i) j -> p s c j i", i=RUN),
-                src.rearrange("p s j (c i) -> p s c j i", i=RUN),
-            )
-
-        def cast_vj(a, t0, w):
-            o, i = pair_views(a, t0, 0, w)
-            nc.vector.tensor_copy(out=o, in_=i)
-
-        def cast_sj(a, t0, w):
-            o, i = pair_views(a, t0, w, HALF // 2)
-            nc.scalar.copy(out=o, in_=i)
-
-        def load_scales(src, row):
-            for r in range(4):
+        def load_w8_scales():
+            for q in range(P // QUADRANT):
                 nc.sync.dma_start(
-                    out=sc_raw[row + r : P : 32, :, :].bitcast(I32),
-                    in_=src[:, r:16:4, :].rearrange("a q n -> q a n").bitcast(I32),
+                    out=sc_raw[QUADRANT * q : QUADRANT * q + 4 * PASSES, PASSES, :].bitcast(I32),
+                    in_=w8_scales[:, 4 * q : 4 * q + 4, :].bitcast(I32),
                 )
 
-        def load_sc(src, row, r):
-            nc.sync.dma_start(
-                out=sc_raw[row + r : P : 32, :, :].bitcast(I32),
-                in_=src[:, r:16:4, :].rearrange("a q n -> q a n").bitcast(I32),
-            )
+        def load_w4_scales():
+            for r in range(4):
+                nc.sync.dma_start(
+                    out=sc_raw[r:P:QUADRANT, 0:PASSES, :].bitcast(I32),
+                    in_=w4_scales[:, r:16:4, :].rearrange("a q n -> q a n").bitcast(I32),
+                )
 
         def load_w4(a0, a1):
             nc.sync.dma_start(
@@ -144,297 +105,259 @@ def tile_mix_feat_fm_quadpl_none_kernel(
                 src.rearrange("p j (c i) -> p c j i", i=RUN),
             )
 
-        def x_views(kind, a, t0, t1):
-            p0, p1, piece = [c for c in xs[a] if c[0] <= t0 and t1 <= c[1]][0]
-            h = t0 // HALF
-            return woven(wide[kind, a, h][:, t0 - h * HALF : t1 - h * HALF, :], piece[:, :, t0 - p0 : t1 - p0])
+        def columns(kind, c0, c1):
+            first = 0 if kind == "a" else HALF
+            return slice(first + c0, first + c1)
 
-        def square(a, t0, t1):
-            o, i = x_views("a", a, t0, t1)
+        def piece_views(kind, a, h, s):
+            dst = units[a, h][2][:, columns(kind, s * PIECE, (s + 1) * PIECE), :]
+            return woven(dst, xs[a, h][:, s, :, :])
+
+        def square(a, h, s):
+            o, i = piece_views("a", a, h, s)
             nc.scalar.activation(out=o, in_=i, func=ACT.Square, bias=bias[:])
 
-        def cast_v(a, t0, t1):
-            o, i = x_views("b", a, t0, t1)
+        def round_piece_vector(a, h, s):
+            o, i = piece_views("b", a, h, s)
             nc.vector.tensor_copy(out=o, in_=i)
 
-        def cast_s(a, t0, t1):
-            o, i = x_views("b", a, t0, t1)
+        def round_piece_scalar(a, h, s):
+            o, i = piece_views("b", a, h, s)
             nc.scalar.copy(out=o, in_=i)
 
-        def cast_g(a, t0, t1):
-            o, i = x_views("b", a, t0, t1)
-            nc.gpsimd.tensor_scalar(out=o, in0=i, scalar1=1.0, scalar2=0.0, op0=ALU.mult, op1=ALU.add)
-
-        def quant(kind, a, t0, t1):
-            h = t0 // HALF
-            cols = slice(t0 - h * HALF, t1 - h * HALF)
-            nc.vector.quantize_mx(
-                out=codes[kind, a, h][:, cols].bitcast(FP8X4),
-                scales=scales[kind, a, h][:, cols],
-                in_=wide[kind, a, h][:, cols, :].rearrange("p t j -> p (t j)"),
+        def share_views(a, h, c0, c1):
+            dst = units[a, h][2][:, columns("b", 0, HALF), :].rearrange("p (s t) j -> p s t j", s=2)
+            return (
+                dst[:, :, c0:c1, :].rearrange("p s (c i) j -> p s c j i", i=RUN),
+                xs[a, h][:, :, :, c0:c1].rearrange("p s j (c i) -> p s c j i", i=RUN),
             )
 
-        def quant_both(a, h):
-            c, s, g = both[a, h]
+        def round_share_vector(a, h):
+            o, i = share_views(a, h, 0, VECTOR_KEEPS[a, h])
+            nc.vector.tensor_copy(out=o, in_=i)
+
+        def round_share_scalar(a, h):
+            o, i = share_views(a, h, VECTOR_KEEPS[a, h], PIECE)
+            nc.scalar.copy(out=o, in_=i)
+
+        def quantise(a, h, cols):
+            codes, scales, wide = units[a, h]
             nc.vector.quantize_mx(
-                out=c[:].bitcast(FP8X4), scales=s[:], in_=g[:].rearrange("p t j -> p (t j)")
+                out=codes[:, cols].bitcast(FP8X4),
+                scales=scales[:, cols],
+                in_=wide[:, cols, :].rearrange("p t j -> p (t j)"),
             )
+
+        def quantise_one(kind, a, h):
+            quantise(a, h, columns(kind, 0, HALF))
+
+        def quantise_both(a, h):
+            quantise(a, h, slice(0, 2 * HALF))
 
         def dealt(table, label, a0, a1, width, dtype):
             t = keep.tile([P, PACK, a1 - a0, width], dtype, name="%s%d" % (label, a0), align_bytes=64)
             for a in range(a0, a1):
-                table[a] = (t, a - a0)
+                table[a] = t[:, :, a - a0, :]
             return t
+
+        def deal(dst, src, run):
+            nc.vector.tensor_copy(
+                out=dst.rearrange("p (g u) a (c i) -> p g (a c) u i", g=2, i=run),
+                in_=src.rearrange("p a (c i g u) -> p g (a c) u i", g=2, u=2, i=run),
+            )
 
         def deal_w4(a0, a1):
             t = dealt(w4, "w4d", a0, a1, 2 * P, U8)
-            nc.vector.tensor_copy(
-                out=t[:].bitcast(U16).rearrange("p (g r) a (c i) -> p g (a c) r i", g=2, i=4),
-                in_=w4_raw[:, a0:a1, :].bitcast(U16).rearrange("p a (c i g r) -> p g (a c) r i", g=2, r=2, i=4),
-            )
+            deal(t[:].bitcast(U16), w4_raw[:, a0:a1, :].bitcast(U16), 4)
 
         def deal_w8(a0, a1):
             t = dealt(w8, "w8d", a0, a1, P, I32)
+            deal(t[:], w8_raw[:, a0:a1, :], 2)
+
+        def deal_w4_scales():
+            t = dealt(sc4, "sc4d", 0, PASSES, P, U8)
+            deal(t[:], sc_raw[:, 0:PASSES, :], 8)
+
+        def deal_w8_scales():
             nc.vector.tensor_copy(
-                out=t[:].rearrange("p (g r) a (c i) -> p g (a c) r i", g=2, i=2),
-                in_=w8_raw[:, a0:a1, :].rearrange("p a (c i g r) -> p g (a c) r i", g=2, r=2, i=2),
+                out=sc8[:].rearrange("p (g u) (c i) -> p g c u i", g=2, i=8),
+                in_=sc_raw[:, PASSES, :].rearrange("p (c i g u) -> p g c u i", g=2, u=2, i=8),
             )
 
-        def deal_scales(a0, a1):
-            t = dealt(sc, "scd", a0, a1, P, U8)
-            nc.vector.tensor_copy(
-                out=t[:].rearrange("p (g r) a (c i) -> p g (a c) r i", g=2, i=8),
-                in_=sc_raw[:, a0:a1, :].rearrange("p a (c i g r) -> p g (a c) r i", g=2, r=2, i=8),
-            )
+        done = {}
 
-        written = {}
-
-        def mm_cols(kind, a, g, r, c, n):
-            first, wd = RANGES[g]
-            hands = BANK // wd
-            b, hand = r // hands, r % hands
-            h = first // HALF
-            before = written.get((g, b), 0)
-            written[g, b] = before + n
-            cols = slice(first - h * HALF + c, first - h * HALF + c + n)
-            if kind == "b":
-                weights = w8[a][0][:, r, w8[a][1], :].bitcast(FP8X4)
-                plane = sc[a][0][W8_ROW:P, r, sc[a][1], :]
+        def product(kind, a, h, r):
+            before = done.get((h, r), 0)
+            done[h, r] = before + 1
+            if kind == "a":
+                weights, weight_scales = w4[a][:, r, :].bitcast(FP4X4), sc4[a][:, r, :]
             else:
-                weights = w4[a][0][:, r, w4[a][1], :].bitcast(FP4X4)
-                plane = sc[a][0][:, r, sc[a][1], :]
+                weights, weight_scales = w8[a][:, r, :].bitcast(FP8X4), sc8[4 * a : P, r, :]
+            codes, scales = units[a, h][:2]
+            cols = columns(kind, 0, HALF)
             nc.tensor.matmul_mx(
-                out=banks[g, b][:, hand, c : c + n],
+                out=banks[h, r][:],
                 lhsT=weights,
-                lhsT_scale=plane,
-                rhs=codes[kind, a, h][:, cols].bitcast(FP8X4),
-                rhs_scale=scales[kind, a, h][:, cols],
+                lhsT_scale=weight_scales,
+                rhs=codes[:, cols].bitcast(FP8X4),
+                rhs_scale=scales[:, cols],
                 start=before == 0,
-                stop=before + n == 2 * PASSES * BANK,
+                stop=before == 2 * PASSES - 1,
             )
 
-        def mm(kind, a, g, r):
-            wd = RANGES[g][1]
-            n = wd if kind == "b" or wd == BANK else P
-            for c in range(0, wd, n):
-                mm_cols(kind, a, g, r, c, n)
-
-        def mms_part(kind, a, g, c, n):
+        def products(kind, a, h):
             for r in range(PACK):
-                mm_cols(kind, a, g, r, c, n)
-
-        def mms(kind, a, *gs):
-            for g in gs:
-                for r in range(PACK):
-                    mm(kind, a, g, r)
-
-        def round_v(g, t0, t1):
-            o, i = woven(res16[g][:, t0:t1, :], res[g][:, :, t0:t1])
-            nc.vector.tensor_copy(out=o, in_=i)
-
-        def round_s(g, t0, t1):
-            o, i = woven(res16[g][:, t0:t1, :], res[g][:, :, t0:t1])
-            nc.scalar.copy(out=o, in_=i)
-
-        def drained(g, b):
-            hands = BANK // RANGES[g][1]
-            return res[g][:, b * hands : (b + 1) * hands, :]
-
-        def drain_s(g, b):
-            nc.scalar.copy(out=drained(g, b), in_=banks[g, b][:])
-
-        def drain_v(g, b):
-            nc.vector.tensor_copy(out=drained(g, b), in_=banks[g, b][:])
-
-        def drain_v_cols(g, b, t0, t1):
-            nc.vector.tensor_copy(out=res[g][:, b, t0:t1], in_=banks[g, b][:, 0, t0:t1])
-
-        def drain_s_cols(g, b, t0, t1):
-            nc.scalar.copy(out=res[g][:, b, t0:t1], in_=banks[g, b][:, 0, t0:t1])
+                product(kind, a, h, r)
 
         out_rows = out_0.rearrange("(p r) t -> p r t", r=PACK)
+        out_words = out_1[0].rearrange("p t i -> p (t i)").bitcast(I32)
 
-        def store_res(g, r0, r1):
-            first, wd = RANGES[g]
-            nc.sync.dma_start(out=out_rows[:, r0:r1, first : first + wd], in_=res[g][:, r0:r1, :])
+        def drain_scalar(h, r, c0, c1):
+            nc.scalar.copy(out=res[h][:, r, c0:c1], in_=banks[h, r][:, c0:c1])
 
-        def q_out(g, t0, t1):
-            first = RANGES[g][0]
+        def store_rows(h, r0, r1):
+            nc.sync.dma_start(out=out_rows[:, r0:r1, h * HALF : (h + 1) * HALF], in_=res[h][:, r0:r1, :])
+
+        def round_result_vector(h, c0, c1):
+            o, i = woven(res16[h][:, c0:c1, :], res[h][:, :, c0:c1])
+            nc.vector.tensor_copy(out=o, in_=i)
+
+        def quantise_result(h, s):
+            t0 = h * HALF + s * PIECE
             nc.vector.quantize_mx(
-                out=o_codes[:, first + t0 : first + t1].bitcast(FP8X4),
-                scales=o_scales[:, first + t0 : first + t1],
-                in_=res16[g][:, t0:t1, :].rearrange("p t j -> p (t j)"),
+                out=o_codes[:, t0 : t0 + PIECE].bitcast(FP8X4),
+                scales=o_scales[:, t0 : t0 + PIECE],
+                in_=res16[h][:, s * PIECE : (s + 1) * PIECE, :].rearrange("p t j -> p (t j)"),
             )
-
-        words_out = out_1[0].rearrange("p t i -> p (t i)").bitcast(I32)
 
         def store_words(t0, t1):
-            nc.sync.dma_start(out=words_out[:, t0:t1], in_=o_codes[:, t0:t1])
-
-        def store_scales(q):
-            (nc.scalar if q < 2 else nc.sync).dma_start(
-                out=out_2[0, q:16:4, :].bitcast(I32),
-                in_=o_scales[q:P:32, :].bitcast(I32),
-            )
+            nc.sync.dma_start(out=out_words[:, t0:t1], in_=o_codes[:, t0:t1])
 
         nc.vector.memset(zero[:], 0.0)
         nc.vector.memset(sc_raw[:].rearrange("p a n -> p (a n)").bitcast(I32), 0)
         nc.scalar.activation(out=bias[:], in_=zero[:], func=ACT.Square)
 
-        load_xh(0, 0, 0)
-        load_sc(w8_scales, W8_ROW, 0)
-        load_sc(w8_scales, W8_ROW, 1)
-        load_xh(0, 0, 1)
-        load_sc(w8_scales, W8_ROW, 2)
-        load_sc(w8_scales, W8_ROW, 3)
-        load_xh(0, 512, 0)
-        load_xh(0, 512, 1)
-        load_sc(w4_scales, 0, 0)
-        load_sc(w4_scales, 0, 1)
-        load_sc(w4_scales, 0, 2)
-        load_sc(w4_scales, 0, 3)
+        load_piece(0, 0, 0)
+        load_w8_scales()
+        load_piece(0, 0, 1)
+        load_unit(0, 1)
         load_w8(0, 1)
+        load_w4_scales()
         load_w4(0, 2)
-        load_xh(1, 0, 0)
-        load_xh(1, 0, 1)
-        load_xh(2, 0, 0)
-        load_xh(2, 0, 1)
+        load_unit(1, 0)
+        load_unit(2, 0)
         load_w8(1, 3)
-        load_xh(3, 0, 0)
-        load_xh(3, 0, 1)
+        load_unit(3, 0)
         load_w4(2, 4)
-        load_xh(1, 512, 0)
-        load_xh(1, 512, 1)
+        load_unit(1, 1)
         load_w8(3, 4)
-        load_xh(2, 512, 0)
-        load_xh(2, 512, 1)
-        load_xh(3, 512, 0)
-        load_xh(3, 512, 1)
-        square(0, 0, 256)
-        square(0, 256, 512)
-        square(0, 512, 768)
-        cast_s(0, 768, 1024)
-        square(0, 768, 1024)
-        square(1, 0, 256)
-        square(1, 256, 512)
-        square(2, 0, 256)
-        square(2, 256, 512)
-        cast_sj(2, 0, 160)
-        square(3, 0, 256)
-        square(3, 256, 512)
-        cast_sj(3, 0, 224)
-        square(1, 512, 768)
-        cast_s(1, 896, 1024)
-        square(1, 768, 1024)
-        square(2, 512, 768)
-        square(2, 768, 1024)
-        square(3, 512, 768)
-        square(3, 768, 1024)
-        cast_v(0, 0, 256)
-        cast_v(0, 256, 512)
-        quant("b", 0, 0, 512)
-        quant("a", 0, 0, 512)
-        cast_v(0, 512, 768)
-        deal_scales(0, 4)
+        load_unit(2, 1)
+        load_unit(3, 1)
+
+        square(0, 0, 0)
+        round_piece_vector(0, 0, 0)
+        deal_w8_scales()
+        square(0, 0, 1)
+        round_piece_vector(0, 0, 1)
+        quantise_one("b", 0, 0)
+        quantise_one("a", 0, 0)
+
+        square(0, 1, 0)
+        round_piece_vector(0, 1, 0)
+        round_piece_scalar(0, 1, 1)
+        square(0, 1, 1)
         deal_w8(0, 1)
+        products("b", 0, 0)
+        deal_w4_scales()
         deal_w4(0, 2)
-        quant("a", 0, 512, 1024)
-        cast_v(1, 0, 256)
-        cast_v(1, 256, 512)
-        quant("b", 0, 512, 1024)
-        quant_both(1, 0)
-        cast_vj(2, 0, 160)
+        products("a", 0, 0)
+        quantise_one("a", 0, 1)
+        products("a", 0, 1)
+
+        for s in range(2):
+            square(1, 0, s)
+            round_piece_vector(1, 0, s)
+        quantise_one("b", 0, 1)
+        products("b", 0, 1)
+        quantise_both(1, 0)
+        products("a", 1, 0)
+
+        square(2, 0, 0)
+        square(2, 0, 1)
+        round_share_scalar(2, 0)
+        round_share_vector(2, 0)
         deal_w8(1, 3)
-        quant("a", 2, 0, 512)
-        quant("b", 2, 0, 512)
-        cast_vj(3, 0, 224)
+        products("b", 1, 0)
+        quantise_one("a", 2, 0)
+        quantise_one("b", 2, 0)
+        products("b", 2, 0)
+
+        square(3, 0, 0)
+        square(3, 0, 1)
+        round_share_scalar(3, 0)
+        round_share_vector(3, 0)
         deal_w4(2, 4)
-        quant_both(3, 0)
-        cast_v(1, 512, 768)
-        cast_v(1, 768, 896)
+        products("a", 2, 0)
+        quantise_both(3, 0)
+        products("a", 3, 0)
+
+        square(1, 1, 0)
+        round_share_scalar(1, 1)
+        square(1, 1, 1)
+        round_share_vector(1, 1)
         deal_w8(3, 4)
-        quant("b", 1, 512, 1024)
-        cast_v(2, 512, 768)
-        quant("a", 1, 512, 1024)
-        cast_v(2, 768, 1024)
-        cast_v(3, 512, 768)
-        quant("b", 2, 512, 1024)
-        quant("a", 2, 512, 1024)
-        cast_v(3, 768, 1024)
-        quant("a", 3, 512, 768)
-        quant("b", 3, 512, 1024)
-        quant("a", 3, 768, 1024)
-        mms("b", 0, 0)
-        mms("a", 0, 0)
-        mms("a", 0, 1)
-        mms("b", 0, 1)
-        mms("a", 1, 0)
-        mms("b", 1, 0)
-        mms("b", 2, 0)
-        mms("a", 2, 0)
-        mms("a", 3, 0)
-        mms("b", 3, 0)
-        mms("b", 1, 1)
-        mms("a", 1, 1)
-        mms("b", 2, 1)
-        mms("a", 2, 1)
-        mm("b", 3, 1, 0)
-        mm("a", 3, 1, 0)
-        mm("b", 3, 1, 1)
-        mm("a", 3, 1, 1)
-        mm("b", 3, 1, 2)
-        mm("a", 3, 1, 2)
-        mm("b", 3, 1, 3)
-        mm("a", 3, 1, 3)
-        drain_s(0, 0)
-        drain_s(0, 1)
-        drain_s(0, 2)
-        drain_s(1, 0)
-        drain_s(1, 1)
-        drain_s(1, 2)
-        drain_s_cols(1, 3, 0, 256)
-        drain_s_cols(1, 3, 256, 512)
-        round_s(1, 384, 512)
-        drain_v(0, 3)
-        round_v(0, 0, 256)
-        round_v(0, 256, 512)
-        q_out(0, 0, 256)
-        q_out(0, 256, 512)
-        round_v(1, 0, 256)
-        round_v(1, 256, 384)
-        q_out(1, 0, 256)
-        q_out(1, 256, 512)
-        store_res(0, 0, 1)
-        store_res(0, 1, 2)
-        store_res(0, 2, 3)
-        store_res(0, 3, 4)
-        store_res(1, 0, 1)
-        store_res(1, 1, 2)
-        store_words(0, 512)
-        store_res(1, 2, 4)
-        store_words(512, 768)
-        store_words(768, 1024)
-        store_scales(0)
-        store_scales(1)
-        store_scales(2)
-        store_scales(3)
+        products("b", 3, 0)
+        quantise_one("b", 1, 1)
+        products("b", 1, 1)
+
+        square(2, 1, 0)
+        square(2, 1, 1)
+        round_piece_vector(2, 1, 0)
+        quantise_one("a", 1, 1)
+        products("a", 1, 1)
+        round_piece_vector(2, 1, 1)
+        square(3, 1, 0)
+        square(3, 1, 1)
+        round_piece_vector(3, 1, 0)
+        quantise_one("b", 2, 1)
+        products("b", 2, 1)
+        quantise_one("a", 2, 1)
+        products("a", 2, 1)
+        round_piece_vector(3, 1, 1)
+        quantise(3, 1, columns("a", 0, PIECE))
+        quantise_one("b", 3, 1)
+        quantise(3, 1, columns("a", PIECE, HALF))
+        for r in range(PACK):
+            product("b", 3, 1, r)
+            product("a", 3, 1, r)
+
+        for r in range(PACK - 1):
+            drain_scalar(0, r, 0, HALF)
+            store_rows(0, r, r + 1)
+        nc.vector.tensor_copy(out=res[0][:, PACK - 1, :], in_=banks[0, PACK - 1][:])
+        store_rows(0, PACK - 1, PACK)
+        for s in range(2):
+            round_result_vector(0, s * PIECE, (s + 1) * PIECE)
+        for r in range(2):
+            drain_scalar(1, r, 0, HALF)
+            store_rows(1, r, r + 1)
+        for s in range(2):
+            quantise_result(0, s)
+        store_words(0, HALF)
+
+        drain_scalar(1, 2, 0, HALF)
+        drain_scalar(1, 3, 0, PIECE)
+        drain_scalar(1, 3, PIECE, HALF)
+        store_rows(1, 2, PACK)
+        round_result_vector(1, 0, PIECE)
+        o, i = woven(res16[1][:, LAST_VECTOR:HALF, :], res[1][:, :, LAST_VECTOR:HALF])
+        nc.scalar.copy(out=o, in_=i)
+        round_result_vector(1, PIECE, LAST_VECTOR)
+        for s in range(2):
+            quantise_result(1, s)
+            store_words(HALF + s * PIECE, HALF + (s + 1) * PIECE)
+        for r in range(4):
+            (nc.scalar if r < 2 else nc.sync).dma_start(
+                out=out_2[0, r:16:4, :].bitcast(I32),
+                in_=o_scales[r:P:QUADRANT, :].bitcast(I32),
+            )

@@ -17,13 +17,11 @@ ACT = mybir.ActivationFunctionType
 P = 128
 PACK = 4
 PASSES = K // (P * PACK)
-HALF = 512
-PIECE = HALF // 2
+BANK = 512
+PIECE = 256
 QUADRANT = 32
 RUN = 4
-
-VECTOR_KEEPS = {(2, 0): 160, (3, 0): 224, (1, 1): 192}
-LAST_VECTOR = 384
+RANGES = {"A": (0, 512), "B": (512, 256), "C": (768, 256)}
 
 
 def tile_mix_feat_fm_quadpl_none_kernel(
@@ -41,37 +39,37 @@ def tile_mix_feat_fm_quadpl_none_kernel(
         sc8 = keep.tile([P, PACK, P], U8, align_bytes=64)
         w4, w8, sc4 = {}, {}, {}
 
-        units = {}
-        for a in range(PASSES):
-            for h in range(T // HALF):
-                label = "%d%d" % (a, h)
-                units[a, h] = (
-                    keep.tile([P, 2 * HALF], I32, name="c" + label, align_bytes=64),
-                    keep.tile([P, 2 * HALF], U8, name="s" + label, align_bytes=64),
-                    keep.tile([P, 2 * HALF, PACK], BF16, name="g" + label, align_bytes=64),
+        units, xs, res, res16, banks = {}, {}, {}, {}, {}
+        for g, (first, width) in RANGES.items():
+            for a in range(PASSES):
+                label = "%s%d" % (g, a)
+                units[g, a] = (
+                    keep.tile([P, 2 * width], I32, name="c" + label, align_bytes=64),
+                    keep.tile([P, 2 * width], U8, name="s" + label, align_bytes=64),
+                    keep.tile([P, 2 * width, PACK], BF16, name="g" + label, align_bytes=64),
                 )
-        res, res16, banks = {}, {}, {}
-        for h in range(T // HALF):
-            res[h] = keep.tile([P, PACK, HALF], F32, name="res%d" % h, align_bytes=256)
-            res16[h] = keep.tile([P, HALF, PACK], BF16, name="res16_%d" % h, align_bytes=64)
-            for r in range(PACK):
-                banks[h, r] = psum.tile([P, HALF], F32, name="acc%d_%d" % (h, r))
+            res[g] = keep.tile([P, PACK, width], F32, name="res" + g, align_bytes=256)
+            res16[g] = keep.tile([P, width, PACK], BF16, name="res16" + g, align_bytes=64)
+            for b in range(PACK * width // BANK):
+                banks[g, b] = psum.tile([P, BANK // width, width], F32, name="acc%s%d" % (g, b))
         o_codes = keep.tile([P, T], I32, align_bytes=256)
         o_scales = keep.tile([P, T], U8, align_bytes=256)
         zero = keep.tile([P, 1], F32)
         bias = keep.tile([P, 1], F32)
-        xs = {}
 
-        def load_piece(a, h, s):
+        def load_piece(g, a, s=0):
             if s == 0:
-                xs[a, h] = keep.tile([P, 2, PACK, PIECE], F32, name="x%d%d" % (a, h), align_bytes=256)
-            t0 = h * HALF + s * PIECE
+                shape = [P, RANGES[g][1] // PIECE, PACK, PIECE]
+                xs[g, a] = keep.tile(shape, F32, name="x%s%d" % (g, a), align_bytes=256)
+            t0 = RANGES[g][0] + s * PIECE
             src = x[P * PACK * a : P * PACK * (a + 1), t0 : t0 + PIECE]
-            nc.sync.dma_start(out=xs[a, h][:, s, :, :], in_=src.rearrange("(p j) t -> p j t", j=PACK))
+            nc.sync.dma_start(out=xs[g, a][:, s, :, :], in_=src.rearrange("(p j) t -> p j t", j=PACK))
 
-        def load_unit(a, h):
-            load_piece(a, h, 0)
-            load_piece(a, h, 1)
+        def load_whole(a):
+            t = keep.tile([P, PACK, BANK], F32, name="xA%d" % a, align_bytes=256)
+            xs["A", a] = t[:].rearrange("p j (s t) -> p s j t", s=2)
+            src = x[P * PACK * a : P * PACK * (a + 1), 0:BANK]
+            nc.sync.dma_start(out=t[:], in_=src.rearrange("(p j) t -> p j t", j=PACK))
 
         def load_w8_scales():
             for q in range(P // QUADRANT):
@@ -105,54 +103,54 @@ def tile_mix_feat_fm_quadpl_none_kernel(
                 src.rearrange("p j (c i) -> p c j i", i=RUN),
             )
 
-        def columns(kind, c0, c1):
-            first = 0 if kind == "a" else HALF
+        def columns(kind, g, c0, c1):
+            first = 0 if kind == "a" else RANGES[g][1]
             return slice(first + c0, first + c1)
 
-        def piece_views(kind, a, h, s):
-            dst = units[a, h][2][:, columns(kind, s * PIECE, (s + 1) * PIECE), :]
-            return woven(dst, xs[a, h][:, s, :, :])
+        def piece_views(kind, g, a, s, c0, c1):
+            dst = units[g, a][2][:, columns(kind, g, s * PIECE + c0, s * PIECE + c1), :]
+            return woven(dst, xs[g, a][:, s, :, c0:c1])
 
-        def square(a, h, s):
-            o, i = piece_views("a", a, h, s)
+        def square(g, a, s=0, c0=0, c1=PIECE):
+            o, i = piece_views("a", g, a, s, c0, c1)
             nc.scalar.activation(out=o, in_=i, func=ACT.Square, bias=bias[:])
 
-        def round_piece_vector(a, h, s):
-            o, i = piece_views("b", a, h, s)
+        def round_vector(g, a, s=0, c0=0, c1=PIECE):
+            o, i = piece_views("b", g, a, s, c0, c1)
             nc.vector.tensor_copy(out=o, in_=i)
 
-        def round_piece_scalar(a, h, s):
-            o, i = piece_views("b", a, h, s)
+        def round_scalar(g, a, s=0, c0=0, c1=PIECE):
+            o, i = piece_views("b", g, a, s, c0, c1)
             nc.scalar.copy(out=o, in_=i)
 
-        def share_views(a, h, c0, c1):
-            dst = units[a, h][2][:, columns("b", 0, HALF), :].rearrange("p (s t) j -> p s t j", s=2)
+        def share_views(a, c0, c1):
+            dst = units["A", a][2][:, columns("b", "A", 0, BANK), :].rearrange("p (s t) j -> p s t j", s=2)
             return (
                 dst[:, :, c0:c1, :].rearrange("p s (c i) j -> p s c j i", i=RUN),
-                xs[a, h][:, :, :, c0:c1].rearrange("p s j (c i) -> p s c j i", i=RUN),
+                xs["A", a][:, :, :, c0:c1].rearrange("p s j (c i) -> p s c j i", i=RUN),
             )
 
-        def round_share_vector(a, h):
-            o, i = share_views(a, h, 0, VECTOR_KEEPS[a, h])
+        def round_share_vector(a, keeps):
+            o, i = share_views(a, 0, keeps)
             nc.vector.tensor_copy(out=o, in_=i)
 
-        def round_share_scalar(a, h):
-            o, i = share_views(a, h, VECTOR_KEEPS[a, h], PIECE)
+        def round_share_scalar(a, keeps):
+            o, i = share_views(a, keeps, PIECE)
             nc.scalar.copy(out=o, in_=i)
 
-        def quantise(a, h, cols):
-            codes, scales, wide = units[a, h]
+        def quantise(g, a, cols):
+            codes, scales, wide = units[g, a]
             nc.vector.quantize_mx(
                 out=codes[:, cols].bitcast(FP8X4),
                 scales=scales[:, cols],
                 in_=wide[:, cols, :].rearrange("p t j -> p (t j)"),
             )
 
-        def quantise_one(kind, a, h):
-            quantise(a, h, columns(kind, 0, HALF))
+        def quantise_one(kind, g, a):
+            quantise(g, a, columns(kind, g, 0, RANGES[g][1]))
 
-        def quantise_both(a, h):
-            quantise(a, h, slice(0, 2 * HALF))
+        def quantise_both(g, a):
+            quantise(g, a, slice(0, 2 * RANGES[g][1]))
 
         def dealt(table, label, a0, a1, width, dtype):
             t = keep.tile([P, PACK, a1 - a0, width], dtype, name="%s%d" % (label, a0), align_bytes=64)
@@ -186,178 +184,221 @@ def tile_mix_feat_fm_quadpl_none_kernel(
 
         done = {}
 
-        def product(kind, a, h, r):
-            before = done.get((h, r), 0)
-            done[h, r] = before + 1
+        def product(kind, g, a, r):
+            width = RANGES[g][1]
+            hands = BANK // width
+            bank = (g, r // hands)
+            before = done.get(bank, 0)
+            done[bank] = before + 1
             if kind == "a":
                 weights, weight_scales = w4[a][:, r, :].bitcast(FP4X4), sc4[a][:, r, :]
             else:
                 weights, weight_scales = w8[a][:, r, :].bitcast(FP8X4), sc8[4 * a : P, r, :]
-            codes, scales = units[a, h][:2]
-            cols = columns(kind, 0, HALF)
+            codes, scales = units[g, a][:2]
+            cols = columns(kind, g, 0, width)
             nc.tensor.matmul_mx(
-                out=banks[h, r][:],
+                out=banks[bank][:, r % hands, :],
                 lhsT=weights,
                 lhsT_scale=weight_scales,
                 rhs=codes[:, cols].bitcast(FP8X4),
                 rhs_scale=scales[:, cols],
                 start=before == 0,
-                stop=before == 2 * PASSES - 1,
+                stop=before == 2 * PASSES * hands - 1,
             )
 
-        def products(kind, a, h):
+        def products(kind, g, a):
             for r in range(PACK):
-                product(kind, a, h, r)
+                product(kind, g, a, r)
+
+        def products_both(g, a):
+            for r in range(PACK):
+                product("b", g, a, r)
+                product("a", g, a, r)
 
         out_rows = out_0.rearrange("(p r) t -> p r t", r=PACK)
         out_words = out_1[0].rearrange("p t i -> p (t i)").bitcast(I32)
 
-        def drain_scalar(h, r, c0, c1):
-            nc.scalar.copy(out=res[h][:, r, c0:c1], in_=banks[h, r][:, c0:c1])
+        def bank_rows(g, b):
+            hands = BANK // RANGES[g][1]
+            return slice(b * hands, (b + 1) * hands)
 
-        def store_rows(h, r0, r1):
-            nc.sync.dma_start(out=out_rows[:, r0:r1, h * HALF : (h + 1) * HALF], in_=res[h][:, r0:r1, :])
+        def drain_scalar(g, b):
+            nc.scalar.copy(out=res[g][:, bank_rows(g, b), :], in_=banks[g, b][:])
 
-        def round_result_vector(h, c0, c1):
-            o, i = woven(res16[h][:, c0:c1, :], res[h][:, :, c0:c1])
+        def drain_part(g, b, c0, c1):
+            nc.scalar.copy(out=res[g][:, bank_rows(g, b), c0:c1], in_=banks[g, b][:, :, c0:c1])
+
+        def drain_vector(g, b):
+            nc.vector.tensor_copy(out=res[g][:, bank_rows(g, b), :], in_=banks[g, b][:])
+
+        def store_rows(g, r0, r1):
+            first, width = RANGES[g]
+            nc.sync.dma_start(out=out_rows[:, r0:r1, first : first + width], in_=res[g][:, r0:r1, :])
+
+        def result_views(g, c0, c1):
+            return woven(res16[g][:, c0:c1, :], res[g][:, :, c0:c1])
+
+        def drain_columns(c0, c1):
+            for r in range(PACK):
+                nc.scalar.copy(out=res["A"][:, r, c0:c1], in_=banks["A", r][:, 0, c0:c1])
+
+        def store_columns(c0, c1):
+            nc.sync.dma_start(out=out_rows[:, :, c0:c1], in_=res["A"][:, :, c0:c1])
+
+        def round_result_vector(g, c0, c1):
+            o, i = result_views(g, c0, c1)
             nc.vector.tensor_copy(out=o, in_=i)
 
-        def quantise_result(h, s):
-            t0 = h * HALF + s * PIECE
+        def round_result_scalar(g, c0, c1):
+            o, i = result_views(g, c0, c1)
+            nc.scalar.copy(out=o, in_=i)
+
+        def quantise_result(g, c0, c1):
+            t0 = RANGES[g][0]
             nc.vector.quantize_mx(
-                out=o_codes[:, t0 : t0 + PIECE].bitcast(FP8X4),
-                scales=o_scales[:, t0 : t0 + PIECE],
-                in_=res16[h][:, s * PIECE : (s + 1) * PIECE, :].rearrange("p t j -> p (t j)"),
+                out=o_codes[:, t0 + c0 : t0 + c1].bitcast(FP8X4),
+                scales=o_scales[:, t0 + c0 : t0 + c1],
+                in_=res16[g][:, c0:c1, :].rearrange("p t j -> p (t j)"),
             )
 
         def store_words(t0, t1):
             nc.sync.dma_start(out=out_words[:, t0:t1], in_=o_codes[:, t0:t1])
 
+        def store_scales(queues, t0, t1):
+            for r in range(4):
+                queues[r].dma_start(
+                    out=out_2[0, r:16:4, t0:t1].bitcast(I32),
+                    in_=o_scales[r:P:QUADRANT, t0:t1].bitcast(I32),
+                )
+
         nc.vector.memset(zero[:], 0.0)
         nc.vector.memset(sc_raw[:].rearrange("p a n -> p (a n)").bitcast(I32), 0)
         nc.scalar.activation(out=bias[:], in_=zero[:], func=ACT.Square)
 
-        load_piece(0, 0, 0)
-        load_w8_scales()
-        load_piece(0, 0, 1)
-        load_unit(0, 1)
-        load_w8(0, 1)
+        load_piece("A", 0, 0)
         load_w4_scales()
+        load_piece("A", 0, 1)
         load_w4(0, 2)
-        load_unit(1, 0)
-        load_unit(2, 0)
-        load_w8(1, 3)
-        load_unit(3, 0)
+        load_piece("B", 0)
+        load_piece("C", 0)
+        load_w8_scales()
+        load_piece("A", 1, 0)
+        load_w8(0, 2)
+        load_piece("A", 1, 1)
+        load_piece("A", 2, 0)
+        load_piece("A", 2, 1)
         load_w4(2, 4)
-        load_unit(1, 1)
-        load_w8(3, 4)
-        load_unit(2, 1)
-        load_unit(3, 1)
+        load_piece("A", 3, 0)
+        load_piece("A", 3, 1)
+        load_w8(2, 4)
+        load_piece("B", 1)
+        load_piece("B", 2)
+        load_piece("B", 3)
+        load_piece("C", 1)
+        load_piece("C", 2)
+        load_piece("C", 3)
 
-        square(0, 0, 0)
-        round_piece_vector(0, 0, 0)
-        deal_w8_scales()
-        square(0, 0, 1)
-        round_piece_vector(0, 0, 1)
-        quantise_one("b", 0, 0)
-        quantise_one("a", 0, 0)
-
-        square(0, 1, 0)
-        round_piece_vector(0, 1, 0)
-        round_piece_scalar(0, 1, 1)
-        square(0, 1, 1)
-        deal_w8(0, 1)
-        products("b", 0, 0)
+        square("A", 0, 0)
+        round_vector("A", 0, 0)
         deal_w4_scales()
+        round_scalar("A", 0, 1, 192, PIECE)
+        square("A", 0, 1)
+        round_vector("A", 0, 1, 0, 192)
         deal_w4(0, 2)
-        products("a", 0, 0)
-        quantise_one("a", 0, 1)
-        products("a", 0, 1)
-
-        for s in range(2):
-            square(1, 0, s)
-            round_piece_vector(1, 0, s)
-        quantise_one("b", 0, 1)
-        products("b", 0, 1)
-        quantise_both(1, 0)
-        products("a", 1, 0)
-
-        square(2, 0, 0)
-        square(2, 0, 1)
-        round_share_scalar(2, 0)
-        round_share_vector(2, 0)
-        deal_w8(1, 3)
-        products("b", 1, 0)
-        quantise_one("a", 2, 0)
-        quantise_one("b", 2, 0)
-        products("b", 2, 0)
-
-        square(3, 0, 0)
-        square(3, 0, 1)
-        round_share_scalar(3, 0)
-        round_share_vector(3, 0)
+        quantise_both("A", 0)
+        products("a", "A", 0)
+        square("B", 0, 0)
+        round_vector("B", 0, 0)
+        square("C", 0, 0)
+        round_vector("C", 0, 0)
+        quantise_both("B", 0)
+        products("a", "B", 0)
+        deal_w8_scales()
+        quantise_both("C", 0)
+        products("a", "C", 0)
+        square("A", 1, 0)
+        round_scalar("A", 1, 0, 96, PIECE)
+        round_vector("A", 1, 0, 0, 96)
+        deal_w8(0, 2)
+        products("b", "A", 0)
+        products("b", "B", 0)
+        products("b", "C", 0)
+        square("A", 1, 1)
+        round_vector("A", 1, 1)
+        square("A", 2, 0)
+        round_vector("A", 2, 0)
+        quantise_both("A", 1)
+        products_both("A", 1)
+        round_scalar("A", 2, 1, 192, PIECE)
+        square("A", 2, 1)
+        round_vector("A", 2, 1, 0, 192)
         deal_w4(2, 4)
-        products("a", 2, 0)
-        quantise_both(3, 0)
-        products("a", 3, 0)
-
-        square(1, 1, 0)
-        round_share_scalar(1, 1)
-        square(1, 1, 1)
-        round_share_vector(1, 1)
-        deal_w8(3, 4)
-        products("b", 3, 0)
-        quantise_one("b", 1, 1)
-        products("b", 1, 1)
-
-        square(2, 1, 0)
-        square(2, 1, 1)
-        round_piece_vector(2, 1, 0)
-        quantise_one("a", 1, 1)
-        products("a", 1, 1)
-        round_piece_vector(2, 1, 1)
-        square(3, 1, 0)
-        square(3, 1, 1)
-        round_piece_vector(3, 1, 0)
-        quantise_one("b", 2, 1)
-        products("b", 2, 1)
-        quantise_one("a", 2, 1)
-        products("a", 2, 1)
-        round_piece_vector(3, 1, 1)
-        quantise(3, 1, columns("a", 0, PIECE))
-        quantise_one("b", 3, 1)
-        quantise(3, 1, columns("a", PIECE, HALF))
-        for r in range(PACK):
-            product("b", 3, 1, r)
-            product("a", 3, 1, r)
-
-        for r in range(PACK - 1):
-            drain_scalar(0, r, 0, HALF)
-            store_rows(0, r, r + 1)
-        nc.vector.tensor_copy(out=res[0][:, PACK - 1, :], in_=banks[0, PACK - 1][:])
-        store_rows(0, PACK - 1, PACK)
-        for s in range(2):
-            round_result_vector(0, s * PIECE, (s + 1) * PIECE)
-        for r in range(2):
-            drain_scalar(1, r, 0, HALF)
-            store_rows(1, r, r + 1)
-        for s in range(2):
-            quantise_result(0, s)
-        store_words(0, HALF)
-
-        drain_scalar(1, 2, 0, HALF)
-        drain_scalar(1, 3, 0, PIECE)
-        drain_scalar(1, 3, PIECE, HALF)
-        store_rows(1, 2, PACK)
-        round_result_vector(1, 0, PIECE)
-        o, i = woven(res16[1][:, LAST_VECTOR:HALF, :], res[1][:, :, LAST_VECTOR:HALF])
-        nc.scalar.copy(out=o, in_=i)
-        round_result_vector(1, PIECE, LAST_VECTOR)
-        for s in range(2):
-            quantise_result(1, s)
-            store_words(HALF + s * PIECE, HALF + (s + 1) * PIECE)
-        for r in range(4):
-            (nc.scalar if r < 2 else nc.sync).dma_start(
-                out=out_2[0, r:16:4, :].bitcast(I32),
-                in_=o_scales[r:P:QUADRANT, :].bitcast(I32),
-            )
+        quantise_both("A", 2)
+        products("a", "A", 2)
+        round_scalar("A", 3, 0, 64, PIECE)
+        square("A", 3, 0)
+        round_vector("A", 3, 0, 0, 64)
+        square("A", 3, 1)
+        round_vector("A", 3, 1)
+        deal_w8(2, 4)
+        products("b", "A", 2)
+        quantise_one("b", "A", 3)
+        products("b", "A", 3)
+        quantise_one("a", "A", 3)
+        products("a", "A", 3)
+        square("B", 1, 0)
+        round_vector("B", 1, 0)
+        square("B", 2, 0)
+        round_vector("B", 2, 0)
+        quantise_both("B", 1)
+        products_both("B", 1)
+        drain_scalar("A", 0)
+        store_rows("A", 0, 1)
+        square("B", 3, 0)
+        round_vector("B", 3, 0)
+        quantise_both("B", 2)
+        products_both("B", 2)
+        square("C", 1, 0)
+        round_vector("C", 1, 0)
+        quantise_both("B", 3)
+        products_both("B", 3)
+        square("C", 2, 0)
+        round_vector("C", 2, 0)
+        quantise_both("C", 1)
+        products_both("C", 1)
+        drain_scalar("A", 1)
+        store_rows("A", 1, 2)
+        square("C", 3, 0)
+        round_vector("C", 3, 0)
+        quantise_both("C", 2)
+        products_both("C", 2)
+        drain_vector("A", 2)
+        store_rows("A", 2, 3)
+        quantise_one("b", "C", 3)
+        products("b", "C", 3)
+        quantise_one("a", "C", 3)
+        products("a", "C", 3)
+        drain_scalar("A", 3)
+        store_rows("A", 3, 4)
+        drain_scalar("B", 0)
+        store_rows("B", 0, 2)
+        drain_scalar("B", 1)
+        store_rows("B", 2, 4)
+        round_result_vector("A", 0, 256)
+        round_result_vector("A", 256, 512)
+        quantise_result("A", 0, 256)
+        quantise_result("A", 256, 512)
+        drain_scalar("C", 0)
+        store_rows("C", 0, 2)
+        store_words(0, 512)
+        drain_scalar("C", 1)
+        store_rows("C", 2, 4)
+        round_result_scalar("B", 192, 256)
+        round_result_vector("B", 0, 192)
+        round_result_scalar("C", 160, 256)
+        round_result_vector("C", 0, 160)
+        quantise_result("B", 0, 256)
+        store_words(512, 768)
+        quantise_result("C", 0, 256)
+        store_words(768, 1024)
+        store_scales((nc.scalar, nc.scalar, nc.sync, nc.sync), 0, T)

@@ -22,6 +22,7 @@ PIECE = 256
 QUADRANT = 32
 RUN = 4
 RANGES = {"A": (0, 512), "B": (512, 256), "C": (768, 256)}
+BY_PIECE = ()
 
 
 def tile_mix_feat_fm_quadpl_none_kernel(
@@ -103,12 +104,15 @@ def tile_mix_feat_fm_quadpl_none_kernel(
                 src.rearrange("p j (c i) -> p c j i", i=RUN),
             )
 
-        def columns(kind, g, c0, c1):
-            first = 0 if kind == "a" else RANGES[g][1]
+        def columns(kind, g, a, c0, c1):
+            if (g, a) in BY_PIECE:
+                first = c0 // PIECE * PIECE + (0 if kind == "a" else PIECE)
+            else:
+                first = 0 if kind == "a" else RANGES[g][1]
             return slice(first + c0, first + c1)
 
         def piece_views(kind, g, a, s, c0, c1):
-            dst = units[g, a][2][:, columns(kind, g, s * PIECE + c0, s * PIECE + c1), :]
+            dst = units[g, a][2][:, columns(kind, g, a, s * PIECE + c0, s * PIECE + c1), :]
             return woven(dst, xs[g, a][:, s, :, c0:c1])
 
         def square(g, a, s=0, c0=0, c1=PIECE):
@@ -123,19 +127,19 @@ def tile_mix_feat_fm_quadpl_none_kernel(
             o, i = piece_views("b", g, a, s, c0, c1)
             nc.scalar.copy(out=o, in_=i)
 
-        def share_views(a, c0, c1):
-            dst = units["A", a][2][:, columns("b", "A", 0, BANK), :].rearrange("p (s t) j -> p s t j", s=2)
+        def share_views(g, a, c0, c1):
+            dst = units[g, a][2][:, columns("b", g, a, 0, BANK), :].rearrange("p (s t) j -> p s t j", s=2)
             return (
                 dst[:, :, c0:c1, :].rearrange("p s (c i) j -> p s c j i", i=RUN),
-                xs["A", a][:, :, :, c0:c1].rearrange("p s j (c i) -> p s c j i", i=RUN),
+                xs[g, a][:, :, :, c0:c1].rearrange("p s j (c i) -> p s c j i", i=RUN),
             )
 
-        def round_share_vector(a, keeps):
-            o, i = share_views(a, 0, keeps)
+        def round_share_vector(g, a, keeps):
+            o, i = share_views(g, a, 0, keeps)
             nc.vector.tensor_copy(out=o, in_=i)
 
-        def round_share_scalar(a, keeps):
-            o, i = share_views(a, keeps, PIECE)
+        def round_share_scalar(g, a, keeps):
+            o, i = share_views(g, a, keeps, PIECE)
             nc.scalar.copy(out=o, in_=i)
 
         def quantise(g, a, cols):
@@ -147,7 +151,10 @@ def tile_mix_feat_fm_quadpl_none_kernel(
             )
 
         def quantise_one(kind, g, a):
-            quantise(g, a, columns(kind, g, 0, RANGES[g][1]))
+            quantise(g, a, columns(kind, g, a, 0, RANGES[g][1]))
+
+        def quantise_piece(g, a, s):
+            quantise(g, a, slice(2 * s * PIECE, 2 * (s + 1) * PIECE))
 
         def quantise_both(g, a):
             quantise(g, a, slice(0, 2 * RANGES[g][1]))
@@ -184,36 +191,37 @@ def tile_mix_feat_fm_quadpl_none_kernel(
 
         done = {}
 
-        def product(kind, g, a, r):
+        def product(kind, g, a, r, c0=0, c1=None):
             width = RANGES[g][1]
+            c1 = c1 or width
             hands = BANK // width
             bank = (g, r // hands)
             before = done.get(bank, 0)
-            done[bank] = before + 1
+            done[bank] = before + c1 - c0
             if kind == "a":
                 weights, weight_scales = w4[a][:, r, :].bitcast(FP4X4), sc4[a][:, r, :]
             else:
                 weights, weight_scales = w8[a][:, r, :].bitcast(FP8X4), sc8[4 * a : P, r, :]
             codes, scales = units[g, a][:2]
-            cols = columns(kind, g, 0, width)
+            cols = columns(kind, g, a, c0, c1)
             nc.tensor.matmul_mx(
-                out=banks[bank][:, r % hands, :],
+                out=banks[bank][:, r % hands, c0:c1],
                 lhsT=weights,
                 lhsT_scale=weight_scales,
                 rhs=codes[:, cols].bitcast(FP8X4),
                 rhs_scale=scales[:, cols],
                 start=before == 0,
-                stop=before == 2 * PASSES * hands - 1,
+                stop=done[bank] == 2 * PASSES * BANK,
             )
 
-        def products(kind, g, a):
+        def products(kind, g, a, c0=0, c1=None):
             for r in range(PACK):
-                product(kind, g, a, r)
+                product(kind, g, a, r, c0, c1)
 
-        def products_both(g, a):
+        def products_both(g, a, c0=0, c1=None):
             for r in range(PACK):
-                product("b", g, a, r)
-                product("a", g, a, r)
+                product("b", g, a, r, c0, c1)
+                product("a", g, a, r, c0, c1)
 
         out_rows = out_0.rearrange("(p r) t -> p r t", r=PACK)
         out_words = out_1[0].rearrange("p t i -> p (t i)").bitcast(I32)
@@ -237,13 +245,6 @@ def tile_mix_feat_fm_quadpl_none_kernel(
 
         def result_views(g, c0, c1):
             return woven(res16[g][:, c0:c1, :], res[g][:, :, c0:c1])
-
-        def drain_columns(c0, c1):
-            for r in range(PACK):
-                nc.scalar.copy(out=res["A"][:, r, c0:c1], in_=banks["A", r][:, 0, c0:c1])
-
-        def store_columns(c0, c1):
-            nc.sync.dma_start(out=out_rows[:, :, c0:c1], in_=res["A"][:, :, c0:c1])
 
         def round_result_vector(g, c0, c1):
             o, i = result_views(g, c0, c1)
@@ -301,9 +302,8 @@ def tile_mix_feat_fm_quadpl_none_kernel(
         square("A", 0, 0)
         round_vector("A", 0, 0)
         deal_w4_scales()
-        round_scalar("A", 0, 1, 192, PIECE)
         square("A", 0, 1)
-        round_vector("A", 0, 1, 0, 192)
+        round_vector("A", 0, 1)
         deal_w4(0, 2)
         quantise_both("A", 0)
         products("a", "A", 0)
@@ -317,8 +317,7 @@ def tile_mix_feat_fm_quadpl_none_kernel(
         quantise_both("C", 0)
         products("a", "C", 0)
         square("A", 1, 0)
-        round_scalar("A", 1, 0, 96, PIECE)
-        round_vector("A", 1, 0, 0, 96)
+        round_scalar("A", 1, 0)
         deal_w8(0, 2)
         products("b", "A", 0)
         products("b", "B", 0)
@@ -329,15 +328,13 @@ def tile_mix_feat_fm_quadpl_none_kernel(
         round_vector("A", 2, 0)
         quantise_both("A", 1)
         products_both("A", 1)
-        round_scalar("A", 2, 1, 192, PIECE)
         square("A", 2, 1)
-        round_vector("A", 2, 1, 0, 192)
+        round_vector("A", 2, 1)
         deal_w4(2, 4)
         quantise_both("A", 2)
         products("a", "A", 2)
-        round_scalar("A", 3, 0, 64, PIECE)
+        round_scalar("A", 3, 0)
         square("A", 3, 0)
-        round_vector("A", 3, 0, 0, 64)
         square("A", 3, 1)
         round_vector("A", 3, 1)
         deal_w8(2, 4)
@@ -352,12 +349,12 @@ def tile_mix_feat_fm_quadpl_none_kernel(
         round_vector("B", 2, 0)
         quantise_both("B", 1)
         products_both("B", 1)
-        drain_scalar("A", 0)
-        store_rows("A", 0, 1)
         square("B", 3, 0)
         round_vector("B", 3, 0)
         quantise_both("B", 2)
         products_both("B", 2)
+        drain_scalar("A", 0)
+        store_rows("A", 0, 1)
         square("C", 1, 0)
         round_vector("C", 1, 0)
         quantise_both("B", 3)
@@ -374,10 +371,8 @@ def tile_mix_feat_fm_quadpl_none_kernel(
         products_both("C", 2)
         drain_vector("A", 2)
         store_rows("A", 2, 3)
-        quantise_one("b", "C", 3)
-        products("b", "C", 3)
-        quantise_one("a", "C", 3)
-        products("a", "C", 3)
+        quantise_both("C", 3)
+        products_both("C", 3)
         drain_scalar("A", 3)
         store_rows("A", 3, 4)
         drain_scalar("B", 0)

@@ -22,7 +22,17 @@ PIECE = 256
 QUADRANT = 32
 RUN = 4
 RANGES = {"A": (0, 512), "B": (512, 256), "C": (768, 256)}
-BY_PIECE = ()
+UNITS = {
+    "A0": ((0, 0), (0, 256)),
+    "A1": ((1, 0), (1, 256)),
+    "A2": ((2, 0), (2, 256)),
+    "A3": ((3, 0), (3, 256)),
+    "B0C0": ((0, 512), (0, 768)),
+    "B1B2": ((1, 512), (2, 512)),
+    "B3C1": ((3, 512), (1, 768)),
+    "C2C3": ((2, 768), (3, 768)),
+}
+BY_PIECE = ("B1B2", "B3C1", "C2C3",)
 
 
 def tile_mix_feat_fm_quadpl_none_kernel(
@@ -40,15 +50,14 @@ def tile_mix_feat_fm_quadpl_none_kernel(
         sc8 = keep.tile([P, PACK, P], U8, align_bytes=64)
         w4, w8, sc4 = {}, {}, {}
 
-        units, xs, res, res16, banks = {}, {}, {}, {}, {}
+        xs, values, codes, scales = {}, {}, {}, {}
+        for u in UNITS:
+            xs[u] = keep.tile([P, PACK, BANK], F32, name="x" + u, align_bytes=256)
+            codes[u] = keep.tile([P, 2 * BANK], I32, name="c" + u, align_bytes=64)
+            scales[u] = keep.tile([P, 2 * BANK], U8, name="s" + u, align_bytes=64)
+            values[u] = keep.tile([P, 2 * BANK, PACK], BF16, name="g" + u, align_bytes=64)
+        res, res16, banks = {}, {}, {}
         for g, (first, width) in RANGES.items():
-            for a in range(PASSES):
-                label = "%s%d" % (g, a)
-                units[g, a] = (
-                    keep.tile([P, 2 * width], I32, name="c" + label, align_bytes=64),
-                    keep.tile([P, 2 * width], U8, name="s" + label, align_bytes=64),
-                    keep.tile([P, 2 * width, PACK], BF16, name="g" + label, align_bytes=64),
-                )
             res[g] = keep.tile([P, PACK, width], F32, name="res" + g, align_bytes=256)
             res16[g] = keep.tile([P, width, PACK], BF16, name="res16" + g, align_bytes=64)
             for b in range(PACK * width // BANK):
@@ -58,19 +67,13 @@ def tile_mix_feat_fm_quadpl_none_kernel(
         zero = keep.tile([P, 1], F32)
         bias = keep.tile([P, 1], F32)
 
-        def load_piece(g, a, s=0):
-            if s == 0:
-                shape = [P, RANGES[g][1] // PIECE, PACK, PIECE]
-                xs[g, a] = keep.tile(shape, F32, name="x%s%d" % (g, a), align_bytes=256)
-            t0 = RANGES[g][0] + s * PIECE
+        def load_piece(u, s):
+            a, t0 = UNITS[u][s]
             src = x[P * PACK * a : P * PACK * (a + 1), t0 : t0 + PIECE]
-            nc.sync.dma_start(out=xs[g, a][:, s, :, :], in_=src.rearrange("(p j) t -> p j t", j=PACK))
-
-        def load_whole(a):
-            t = keep.tile([P, PACK, BANK], F32, name="xA%d" % a, align_bytes=256)
-            xs["A", a] = t[:].rearrange("p j (s t) -> p s j t", s=2)
-            src = x[P * PACK * a : P * PACK * (a + 1), 0:BANK]
-            nc.sync.dma_start(out=t[:], in_=src.rearrange("(p j) t -> p j t", j=PACK))
+            nc.sync.dma_start(
+                out=xs[u][:, :, s * PIECE : (s + 1) * PIECE],
+                in_=src.rearrange("(p j) t -> p j t", j=PACK),
+            )
 
         def load_w8_scales():
             for q in range(P // QUADRANT):
@@ -104,60 +107,43 @@ def tile_mix_feat_fm_quadpl_none_kernel(
                 src.rearrange("p j (c i) -> p c j i", i=RUN),
             )
 
-        def columns(kind, g, a, c0, c1):
-            if (g, a) in BY_PIECE:
+        def columns(kind, u, c0, c1):
+            if u in BY_PIECE:
                 first = c0 // PIECE * PIECE + (0 if kind == "a" else PIECE)
             else:
-                first = 0 if kind == "a" else RANGES[g][1]
+                first = 0 if kind == "a" else BANK
             return slice(first + c0, first + c1)
 
-        def piece_views(kind, g, a, s, c0, c1):
-            dst = units[g, a][2][:, columns(kind, g, a, s * PIECE + c0, s * PIECE + c1), :]
-            return woven(dst, xs[g, a][:, s, :, c0:c1])
+        def unit_views(kind, u, c0, c1):
+            return woven(values[u][:, columns(kind, u, c0, c1), :], xs[u][:, :, c0:c1])
 
-        def square(g, a, s=0, c0=0, c1=PIECE):
-            o, i = piece_views("a", g, a, s, c0, c1)
+        def square(u, c0, c1):
+            o, i = unit_views("a", u, c0, c1)
             nc.scalar.activation(out=o, in_=i, func=ACT.Square, bias=bias[:])
 
-        def round_vector(g, a, s=0, c0=0, c1=PIECE):
-            o, i = piece_views("b", g, a, s, c0, c1)
+        def round_vector(u, c0, c1):
+            o, i = unit_views("b", u, c0, c1)
             nc.vector.tensor_copy(out=o, in_=i)
 
-        def round_scalar(g, a, s=0, c0=0, c1=PIECE):
-            o, i = piece_views("b", g, a, s, c0, c1)
+        def round_scalar(u, c0, c1):
+            o, i = unit_views("b", u, c0, c1)
             nc.scalar.copy(out=o, in_=i)
 
-        def share_views(g, a, c0, c1):
-            dst = units[g, a][2][:, columns("b", g, a, 0, BANK), :].rearrange("p (s t) j -> p s t j", s=2)
-            return (
-                dst[:, :, c0:c1, :].rearrange("p s (c i) j -> p s c j i", i=RUN),
-                xs[g, a][:, :, :, c0:c1].rearrange("p s j (c i) -> p s c j i", i=RUN),
-            )
-
-        def round_share_vector(g, a, keeps):
-            o, i = share_views(g, a, 0, keeps)
-            nc.vector.tensor_copy(out=o, in_=i)
-
-        def round_share_scalar(g, a, keeps):
-            o, i = share_views(g, a, keeps, PIECE)
-            nc.scalar.copy(out=o, in_=i)
-
-        def quantise(g, a, cols):
-            codes, scales, wide = units[g, a]
+        def quantise(u, cols):
             nc.vector.quantize_mx(
-                out=codes[:, cols].bitcast(FP8X4),
-                scales=scales[:, cols],
-                in_=wide[:, cols, :].rearrange("p t j -> p (t j)"),
+                out=codes[u][:, cols].bitcast(FP8X4),
+                scales=scales[u][:, cols],
+                in_=values[u][:, cols, :].rearrange("p t j -> p (t j)"),
             )
 
-        def quantise_one(kind, g, a):
-            quantise(g, a, columns(kind, g, a, 0, RANGES[g][1]))
+        def quantise_one(kind, u, c0=0, c1=BANK):
+            quantise(u, columns(kind, u, c0, c1))
 
-        def quantise_piece(g, a, s):
-            quantise(g, a, slice(2 * s * PIECE, 2 * (s + 1) * PIECE))
+        def quantise_piece(u, s):
+            quantise(u, slice(s * BANK, (s + 1) * BANK))
 
-        def quantise_both(g, a):
-            quantise(g, a, slice(0, 2 * RANGES[g][1]))
+        def quantise_both(u):
+            quantise(u, slice(0, 2 * BANK))
 
         def dealt(table, label, a0, a1, width, dtype):
             t = keep.tile([P, PACK, a1 - a0, width], dtype, name="%s%d" % (label, a0), align_bytes=64)
@@ -191,37 +177,37 @@ def tile_mix_feat_fm_quadpl_none_kernel(
 
         done = {}
 
-        def product(kind, g, a, r, c0=0, c1=None):
+        def product(kind, u, s, r):
+            a, t0 = UNITS[u][s]
+            g = [name for name, (first, width) in RANGES.items() if first <= t0][-1]
             width = RANGES[g][1]
-            c1 = c1 or width
             hands = BANK // width
             bank = (g, r // hands)
             before = done.get(bank, 0)
-            done[bank] = before + c1 - c0
+            done[bank] = before + 1
             if kind == "a":
                 weights, weight_scales = w4[a][:, r, :].bitcast(FP4X4), sc4[a][:, r, :]
             else:
                 weights, weight_scales = w8[a][:, r, :].bitcast(FP8X4), sc8[4 * a : P, r, :]
-            codes, scales = units[g, a][:2]
-            cols = columns(kind, g, a, c0, c1)
+            cols = columns(kind, u, s * PIECE, s * PIECE + width)
             nc.tensor.matmul_mx(
-                out=banks[bank][:, r % hands, c0:c1],
+                out=banks[bank][:, r % hands, :],
                 lhsT=weights,
                 lhsT_scale=weight_scales,
-                rhs=codes[:, cols].bitcast(FP8X4),
-                rhs_scale=scales[:, cols],
+                rhs=codes[u][:, cols].bitcast(FP8X4),
+                rhs_scale=scales[u][:, cols],
                 start=before == 0,
-                stop=done[bank] == 2 * PASSES * BANK,
+                stop=before == 2 * PASSES * hands - 1,
             )
 
-        def products(kind, g, a, c0=0, c1=None):
+        def products(kind, u, s=0):
             for r in range(PACK):
-                product(kind, g, a, r, c0, c1)
+                product(kind, u, s, r)
 
-        def products_both(g, a, c0=0, c1=None):
+        def products_both(u, s=0):
             for r in range(PACK):
-                product("b", g, a, r, c0, c1)
-                product("a", g, a, r, c0, c1)
+                product("b", u, s, r)
+                product("a", u, s, r)
 
         out_rows = out_0.rearrange("(p r) t -> p r t", r=PACK)
         out_words = out_1[0].rearrange("p t i -> p (t i)").bitcast(I32)
@@ -276,103 +262,99 @@ def tile_mix_feat_fm_quadpl_none_kernel(
         nc.vector.memset(sc_raw[:].rearrange("p a n -> p (a n)").bitcast(I32), 0)
         nc.scalar.activation(out=bias[:], in_=zero[:], func=ACT.Square)
 
-        load_piece("A", 0, 0)
+        load_piece("A0", 0)
         load_w4_scales()
-        load_piece("A", 0, 1)
+        load_piece("A0", 1)
         load_w4(0, 2)
-        load_piece("B", 0)
-        load_piece("C", 0)
+        load_piece("B0C0", 0)
+        load_piece("B0C0", 1)
         load_w8_scales()
-        load_piece("A", 1, 0)
+        load_piece("A1", 0)
+        load_piece("A1", 1)
         load_w8(0, 2)
-        load_piece("A", 1, 1)
-        load_piece("A", 2, 0)
-        load_piece("A", 2, 1)
+        load_piece("A2", 0)
+        load_piece("A2", 1)
         load_w4(2, 4)
-        load_piece("A", 3, 0)
-        load_piece("A", 3, 1)
+        load_piece("A3", 0)
+        load_piece("A3", 1)
         load_w8(2, 4)
-        load_piece("B", 1)
-        load_piece("B", 2)
-        load_piece("B", 3)
-        load_piece("C", 1)
-        load_piece("C", 2)
-        load_piece("C", 3)
+        load_piece("B1B2", 0)
+        load_piece("B1B2", 1)
+        load_piece("B3C1", 0)
+        load_piece("B3C1", 1)
+        load_piece("C2C3", 0)
+        load_piece("C2C3", 1)
 
-        square("A", 0, 0)
-        round_vector("A", 0, 0)
+        square("A0", 0, PIECE)
+        round_vector("A0", 0, PIECE)
         deal_w4_scales()
-        square("A", 0, 1)
-        round_vector("A", 0, 1)
+        square("A0", PIECE, BANK)
+        round_vector("A0", PIECE, BANK)
         deal_w4(0, 2)
-        quantise_both("A", 0)
-        products("a", "A", 0)
-        square("B", 0, 0)
-        round_vector("B", 0, 0)
-        square("C", 0, 0)
-        round_vector("C", 0, 0)
-        quantise_both("B", 0)
-        products("a", "B", 0)
+        quantise_both("A0")
+        products("a", "A0")
+        square("B0C0", 0, PIECE)
+        square("B0C0", PIECE, BANK)
+        round_vector("B0C0", 0, BANK)
         deal_w8_scales()
-        quantise_both("C", 0)
-        products("a", "C", 0)
-        square("A", 1, 0)
-        round_scalar("A", 1, 0)
+        quantise_both("B0C0")
+        products("a", "B0C0", 0)
+        products("a", "B0C0", 1)
+        square("A1", 0, PIECE)
+        square("A1", PIECE, BANK)
+        round_scalar("A1", 384, 512)
+        round_vector("A1", 0, 384)
         deal_w8(0, 2)
-        products("b", "A", 0)
-        products("b", "B", 0)
-        products("b", "C", 0)
-        square("A", 1, 1)
-        round_vector("A", 1, 1)
-        square("A", 2, 0)
-        round_vector("A", 2, 0)
-        quantise_both("A", 1)
-        products_both("A", 1)
-        square("A", 2, 1)
-        round_vector("A", 2, 1)
+        products("b", "A0")
+        products("b", "B0C0", 0)
+        products("b", "B0C0", 1)
+        quantise_both("A1")
+        products_both("A1")
+        square("A2", 0, PIECE)
+        square("A2", PIECE, BANK)
+        round_vector("A2", 0, BANK)
         deal_w4(2, 4)
-        quantise_both("A", 2)
-        products("a", "A", 2)
-        round_scalar("A", 3, 0)
-        square("A", 3, 0)
-        square("A", 3, 1)
-        round_vector("A", 3, 1)
+        quantise_both("A2")
+        products("a", "A2")
+        round_scalar("A3", 0, PIECE)
+        square("A3", 0, BANK)
+        round_vector("A3", PIECE, BANK)
         deal_w8(2, 4)
-        products("b", "A", 2)
-        quantise_one("b", "A", 3)
-        products("b", "A", 3)
-        quantise_one("a", "A", 3)
-        products("a", "A", 3)
-        square("B", 1, 0)
-        round_vector("B", 1, 0)
-        square("B", 2, 0)
-        round_vector("B", 2, 0)
-        quantise_both("B", 1)
-        products_both("B", 1)
-        square("B", 3, 0)
-        round_vector("B", 3, 0)
-        quantise_both("B", 2)
-        products_both("B", 2)
+        products("b", "A2")
+        quantise_one("b", "A3")
+        products("b", "A3")
+        square("B1B2", 0, PIECE)
+        round_vector("B1B2", 0, PIECE)
+        quantise_one("a", "A3")
+        products("a", "A3")
+        square("B1B2", PIECE, BANK)
+        round_vector("B1B2", PIECE, BANK)
+        quantise_piece("B1B2", 0)
+        products_both("B1B2", 0)
+        square("B3C1", 0, PIECE)
+        round_vector("B3C1", 0, PIECE)
+        quantise_piece("B1B2", 1)
+        products_both("B1B2", 1)
         drain_scalar("A", 0)
         store_rows("A", 0, 1)
-        square("C", 1, 0)
-        round_vector("C", 1, 0)
-        quantise_both("B", 3)
-        products_both("B", 3)
-        square("C", 2, 0)
-        round_vector("C", 2, 0)
-        quantise_both("C", 1)
-        products_both("C", 1)
+        square("B3C1", PIECE, BANK)
+        round_vector("B3C1", PIECE, BANK)
+        quantise_piece("B3C1", 0)
+        products_both("B3C1", 0)
+        square("C2C3", 0, PIECE)
+        round_vector("C2C3", 0, PIECE)
+        quantise_piece("B3C1", 1)
+        products_both("B3C1", 1)
         drain_scalar("A", 1)
         store_rows("A", 1, 2)
-        square("C", 3, 0)
-        round_vector("C", 3, 0)
-        quantise_both("C", 2)
-        products_both("C", 2)
+        square("C2C3", PIECE, BANK)
+        round_vector("C2C3", PIECE, BANK)
+        quantise_piece("C2C3", 0)
+        products_both("C2C3", 0)
         drain_vector("A", 2)
         store_rows("A", 2, 3)
-        quantise_both("C", 3)
-        products_both("C", 3)
+        quantise_piece("C2C3", 1)
+        products_both("C2C3", 1)
         drain_scalar("A", 3)
         store_rows("A", 3, 4)
         drain_scalar("B", 0)

@@ -47,19 +47,19 @@ def tile_mix_feat_fm_quadpl_none_kernel(
         w4_raw = keep.tile([P, PASSES, 2 * M], U8, align_bytes=256)
         w8_raw = keep.tile([P, PASSES, M], I32, align_bytes=256)
         sc_raw = keep.tile([P, PASSES + 1, M], U8, align_bytes=256)
-        sc8 = keep.tile([P, PACK, P], U8, align_bytes=64)
+        sc8 = keep.tile([P, PACK, P], U8, align_bytes=256)
         w4, w8, sc4 = {}, {}, {}
 
         xs, values, codes, scales = {}, {}, {}, {}
         for u in UNITS:
             xs[u] = keep.tile([P, PACK, BANK], F32, name="x" + u, align_bytes=256)
-            codes[u] = keep.tile([P, 2 * BANK], I32, name="c" + u, align_bytes=64)
-            scales[u] = keep.tile([P, 2 * BANK], U8, name="s" + u, align_bytes=64)
-            values[u] = keep.tile([P, 2 * BANK, PACK], BF16, name="g" + u, align_bytes=64)
+            codes[u] = keep.tile([P, 2 * BANK], I32, name="c" + u, align_bytes=256)
+            scales[u] = keep.tile([P, 2 * BANK], U8, name="s" + u, align_bytes=256)
+            values[u] = keep.tile([P, 2 * BANK, PACK], BF16, name="g" + u, align_bytes=256)
         res, res16, banks = {}, {}, {}
         for g, (first, width) in RANGES.items():
             res[g] = keep.tile([P, PACK, width], F32, name="res" + g, align_bytes=256)
-            res16[g] = keep.tile([P, width, PACK], BF16, name="res16" + g, align_bytes=64)
+            res16[g] = keep.tile([P, width, PACK], BF16, name="res16" + g, align_bytes=256)
             for b in range(PACK * width // BANK):
                 banks[g, b] = psum.tile([P, BANK // width, width], F32, name="acc%s%d" % (g, b))
         o_codes = keep.tile([P, T], I32, align_bytes=256)
@@ -146,7 +146,7 @@ def tile_mix_feat_fm_quadpl_none_kernel(
             quantise(u, slice(0, 2 * BANK))
 
         def dealt(table, label, a0, a1, width, dtype):
-            t = keep.tile([P, PACK, a1 - a0, width], dtype, name="%s%d" % (label, a0), align_bytes=64)
+            t = keep.tile([P, PACK, a1 - a0, width], dtype, name="%s%d" % (label, a0), align_bytes=256)
             for a in range(a0, a1):
                 table[a] = t[:, :, a - a0, :]
             return t

@@ -28,11 +28,11 @@ UNITS = {
     "A2": ((2, 0), (2, 256)),
     "A3": ((3, 0), (3, 256)),
     "B0C0": ((0, 512), (0, 768)),
-    "B1B2": ((1, 512), (2, 512)),
-    "B3C1": ((3, 512), (1, 768)),
+    "B1C1": ((1, 512), (1, 768)),
+    "B2B3": ((2, 512), (3, 512)),
     "C2C3": ((2, 768), (3, 768)),
 }
-BY_PIECE = ("B1B2", "B3C1", "C2C3",)
+BY_PIECE = ("B2B3", "C2C3",)
 
 
 def tile_mix_feat_fm_quadpl_none_kernel(
@@ -204,6 +204,11 @@ def tile_mix_feat_fm_quadpl_none_kernel(
             for r in range(PACK):
                 product(kind, u, s, r)
 
+        def products_pair(kind, u):
+            for r in range(PACK):
+                product(kind, u, 0, r)
+                product(kind, u, 1, r)
+
         def products_both(u, s=0):
             for r in range(PACK):
                 product("b", u, s, r)
@@ -272,16 +277,16 @@ def tile_mix_feat_fm_quadpl_none_kernel(
         load_piece("A1", 0)
         load_piece("A1", 1)
         load_w8(0, 2)
+        load_piece("B1C1", 0)
+        load_piece("B1C1", 1)
         load_piece("A2", 0)
         load_piece("A2", 1)
         load_w4(2, 4)
         load_piece("A3", 0)
         load_piece("A3", 1)
         load_w8(2, 4)
-        load_piece("B1B2", 0)
-        load_piece("B1B2", 1)
-        load_piece("B3C1", 0)
-        load_piece("B3C1", 1)
+        load_piece("B2B3", 0)
+        load_piece("B2B3", 1)
         load_piece("C2C3", 0)
         load_piece("C2C3", 1)
 
@@ -298,21 +303,26 @@ def tile_mix_feat_fm_quadpl_none_kernel(
         round_vector("B0C0", 0, BANK)
         deal_w8_scales()
         quantise_both("B0C0")
-        products("a", "B0C0", 0)
-        products("a", "B0C0", 1)
+        products_pair("a", "B0C0")
         square("A1", 0, PIECE)
         square("A1", PIECE, BANK)
         round_scalar("A1", 384, 512)
         round_vector("A1", 0, 384)
         deal_w8(0, 2)
         products("b", "A0")
-        products("b", "B0C0", 0)
-        products("b", "B0C0", 1)
+        products_pair("b", "B0C0")
         quantise_both("A1")
         products_both("A1")
+        square("B1C1", 0, PIECE)
+        square("B1C1", PIECE, BANK)
+        round_vector("B1C1", 0, BANK)
         square("A2", 0, PIECE)
+        round_vector("A2", 0, PIECE)
+        quantise_both("B1C1")
+        products_pair("b", "B1C1")
+        products_pair("a", "B1C1")
         square("A2", PIECE, BANK)
-        round_vector("A2", 0, BANK)
+        round_vector("A2", PIECE, BANK)
         deal_w4(2, 4)
         quantise_both("A2")
         products("a", "A2")
@@ -323,28 +333,20 @@ def tile_mix_feat_fm_quadpl_none_kernel(
         products("b", "A2")
         quantise_one("b", "A3")
         products("b", "A3")
-        square("B1B2", 0, PIECE)
-        round_vector("B1B2", 0, PIECE)
+        square("B2B3", 0, PIECE)
+        round_vector("B2B3", 0, PIECE)
         quantise_one("a", "A3")
         products("a", "A3")
-        square("B1B2", PIECE, BANK)
-        round_vector("B1B2", PIECE, BANK)
-        quantise_piece("B1B2", 0)
-        products_both("B1B2", 0)
-        square("B3C1", 0, PIECE)
-        round_vector("B3C1", 0, PIECE)
-        quantise_piece("B1B2", 1)
-        products_both("B1B2", 1)
-        drain_scalar("A", 0)
-        store_rows("A", 0, 1)
-        square("B3C1", PIECE, BANK)
-        round_vector("B3C1", PIECE, BANK)
-        quantise_piece("B3C1", 0)
-        products_both("B3C1", 0)
+        square("B2B3", PIECE, BANK)
+        round_vector("B2B3", PIECE, BANK)
+        quantise_piece("B2B3", 0)
+        products_both("B2B3", 0)
         square("C2C3", 0, PIECE)
         round_vector("C2C3", 0, PIECE)
-        quantise_piece("B3C1", 1)
-        products_both("B3C1", 1)
+        quantise_piece("B2B3", 1)
+        products_both("B2B3", 1)
+        drain_scalar("A", 0)
+        store_rows("A", 0, 1)
         drain_scalar("A", 1)
         store_rows("A", 1, 2)
         square("C2C3", PIECE, BANK)

from contextlib import ExitStack

import concourse.mybir as mybir

K, M, T = 2048, 512, 1024
FLOPS = 2 * 2 * K * M * T

F32 = mybir.dt.float32
BF16 = mybir.dt.bfloat16
I32 = mybir.dt.int32
U8 = mybir.dt.uint8
U16 = mybir.dt.uint16
FP8X4 = mybir.dt.float8_e4m3fn_x4
FP4X4 = mybir.dt.float4_e2m1fn_x4
ACT = mybir.ActivationFunctionType

P = 128
PACK = 4
PASSES = K // (P * PACK)
BANK = 512
PIECE = 256
QUADRANT = 32
RUN = 4
RANGES = {"A": (0, 512), "B": (512, 256), "C": (768, 256)}
UNITS = {
    "A0": ((0, 0), (0, 256)),
    "A1": ((1, 0), (1, 256)),
    "A2": ((2, 0), (2, 256)),
    "A3": ((3, 0), (3, 256)),
    "B0C0": ((0, 512), (0, 768)),
    "B1C1": ((1, 512), (1, 768)),
    "B2B3": ((2, 512), (3, 512)),
    "C2C3": ((2, 768), (3, 768)),
}
BY_PIECE = ("B2B3", "C2C3",)


def tile_mix_feat_fm_quadpl_none_kernel(
    tc, x, w4_words, w4_scales, w8_words, w8_scales, out_0, out_1, out_2
):
    nc = tc.nc
    with ExitStack() as ctx:
        keep = ctx.enter_context(tc.tile_pool(name="keep", bufs=1))
        psum = ctx.enter_context(tc.psum_pool(name="psum", bufs=1))
        ctx.enter_context(tc.manual_schedule())

        w4_raw = keep.tile([P, PASSES, 2 * M], U8, align_bytes=256)
        w8_raw = keep.tile([P, PASSES, M], I32, align_bytes=256)
        sc_raw = keep.tile([P, PASSES + 1, M], U8, align_bytes=256)
        sc8 = keep.tile([P, PACK, P], U8, align_bytes=256)
        w4, w8, sc4 = {}, {}, {}

        xs, values, codes, scales = {}, {}, {}, {}
        for u in UNITS:
            xs[u] = keep.tile([P, PACK, BANK], F32, name="x" + u, align_bytes=256)
            codes[u] = keep.tile([P, 2 * BANK], I32, name="c" + u, align_bytes=256)
            scales[u] = keep.tile([P, 2 * BANK], U8, name="s" + u, align_bytes=256)
            values[u] = keep.tile([P, 2 * BANK, PACK], BF16, name="g" + u, align_bytes=256)
        res, res16, banks = {}, {}, {}
        for g, (first, width) in RANGES.items():
            res[g] = keep.tile([P, PACK, width], F32, name="res" + g, align_bytes=256)
            res16[g] = keep.tile([P, width, PACK], BF16, name="res16" + g, align_bytes=256)
            for b in range(PACK * width // BANK):
                banks[g, b] = psum.tile([P, BANK // width, width], F32, name="acc%s%d" % (g, b))
        o_codes = keep.tile([P, T], I32, align_bytes=256)
        o_scales = keep.tile([P, T], U8, align_bytes=256)
        zero = keep.tile([P, 1], F32)
        bias = keep.tile([P, 1], F32)

        def load_piece(u, s):
            a, t0 = UNITS[u][s]
            src = x[P * PACK * a : P * PACK * (a + 1), t0 : t0 + PIECE]
            nc.sync.dma_start(
                out=xs[u][:, :, s * PIECE : (s + 1) * PIECE],
                in_=src.rearrange("(p j) t -> p j t", j=PACK),
            )

        def load_w8_scales():
            for q in range(P // QUADRANT):
                nc.sync.dma_start(
                    out=sc_raw[QUADRANT * q : QUADRANT * q + 4 * PASSES, PASSES, :].bitcast(I32),
                    in_=w8_scales[:, 4 * q : 4 * q + 4, :].bitcast(I32),
                )

        def load_w4_scales():
            for r in range(4):
                nc.sync.dma_start(
                    out=sc_raw[r:P:QUADRANT, 0:PASSES, :].bitcast(I32),
                    in_=w4_scales[:, r:16:4, :].rearrange("a q n -> q a n").bitcast(I32),
                )

        def load_w4(a0, a1):
            nc.sync.dma_start(
                out=w4_raw[:, a0:a1, :].bitcast(I32),
                in_=w4_words[a0:a1].rearrange("a p n -> p a n").bitcast(I32),
            )

        def load_w8(a0, a1):
            nc.sync.dma_start(
                out=w8_raw[:, a0:a1, :],
                in_=w8_words[a0:a1].rearrange("a p n i -> p a (n i)").bitcast(I32),
            )

        def woven(dst, src):
            return (
                dst.rearrange("p (c i) j -> p c j i", i=RUN),
                src.rearrange("p j (c i) -> p c j i", i=RUN),
            )

        def columns(kind, u, c0, c1):
            if u in BY_PIECE:
                first = c0 // PIECE * PIECE + (0 if kind == "a" else PIECE)
            else:
                first = 0 if kind == "a" else BANK
            return slice(first + c0, first + c1)

        def unit_views(kind, u, c0, c1):
            return woven(values[u][:, columns(kind, u, c0, c1), :], xs[u][:, :, c0:c1])

        def square(u, c0, c1):
            o, i = unit_views("a", u, c0, c1)
            nc.scalar.activation(out=o, in_=i, func=ACT.Square, bias=bias[:])

        def round_vector(u, c0, c1):
            o, i = unit_views("b", u, c0, c1)
            nc.vector.tensor_copy(out=o, in_=i)

        def round_scalar(u, c0, c1):
            o, i = unit_views("b", u, c0, c1)
            nc.scalar.copy(out=o, in_=i)

        def quantise(u, cols):
            nc.vector.quantize_mx(
                out=codes[u][:, cols].bitcast(FP8X4),
                scales=scales[u][:, cols],
                in_=values[u][:, cols, :].rearrange("p t j -> p (t j)"),
            )

        def quantise_one(kind, u, c0=0, c1=BANK):
            quantise(u, columns(kind, u, c0, c1))

        def quantise_piece(u, s):
            quantise(u, slice(s * BANK, (s + 1) * BANK))

        def quantise_both(u):
            quantise(u, slice(0, 2 * BANK))

        def dealt(table, label, a0, a1, width, dtype):
            t = keep.tile([P, PACK, a1 - a0, width], dtype, name="%s%d" % (label, a0), align_bytes=256)
            for a in range(a0, a1):
                table[a] = t[:, :, a - a0, :]
            return t

        def deal(dst, src, run):
            nc.vector.tensor_copy(
                out=dst.rearrange("p (g u) a (c i) -> p g (a c) u i", g=2, i=run),
                in_=src.rearrange("p a (c i g u) -> p g (a c) u i", g=2, u=2, i=run),
            )

        def deal_w4(a0, a1):
            t = dealt(w4, "w4d", a0, a1, 2 * P, U8)
            deal(t[:].bitcast(U16), w4_raw[:, a0:a1, :].bitcast(U16), 4)

        def deal_w8(a0, a1):
            t = dealt(w8, "w8d", a0, a1, P, I32)
            deal(t[:], w8_raw[:, a0:a1, :], 2)

        def deal_w4_scales():
            t = dealt(sc4, "sc4d", 0, PASSES, P, U8)
            deal(t[:], sc_raw[:, 0:PASSES, :], 8)

        def deal_w8_scales():
            nc.vector.tensor_copy(
                out=sc8[:].rearrange("p (g u) (c i) -> p g c u i", g=2, i=8),
                in_=sc_raw[:, PASSES, :].rearrange("p (c i g u) -> p g c u i", g=2, u=2, i=8),
            )

        done = {}

        def product(kind, u, s, r):
            a, t0 = UNITS[u][s]
            g = [name for name, (first, width) in RANGES.items() if first <= t0][-1]
            width = RANGES[g][1]
            hands = BANK // width
            bank = (g, r // hands)
            before = done.get(bank, 0)
            done[bank] = before + 1
            if kind == "a":
                weights, weight_scales = w4[a][:, r, :].bitcast(FP4X4), sc4[a][:, r, :]
            else:
                weights, weight_scales = w8[a][:, r, :].bitcast(FP8X4), sc8[4 * a : P, r, :]
            cols = columns(kind, u, s * PIECE, s * PIECE + width)
            nc.tensor.matmul_mx(
                out=banks[bank][:, r % hands, :],
                lhsT=weights,
                lhsT_scale=weight_scales,
                rhs=codes[u][:, cols].bitcast(FP8X4),
                rhs_scale=scales[u][:, cols],
                start=before == 0,
                stop=before == 2 * PASSES * hands - 1,
            )

        def products(kind, u, s=0):
            for r in range(PACK):
                product(kind, u, s, r)

        def products_pair(kind, u):
            for r in range(PACK):
                product(kind, u, 0, r)
                product(kind, u, 1, r)

        def products_both(u, s=0):
            for r in range(PACK):
                product("b", u, s, r)
                product("a", u, s, r)

        out_rows = out_0.rearrange("(p r) t -> p r t", r=PACK)
        out_words = out_1[0].rearrange("p t i -> p (t i)").bitcast(I32)

        def bank_rows(g, b):
            hands = BANK // RANGES[g][1]
            return slice(b * hands, (b + 1) * hands)

        def drain_scalar(g, b):
            nc.scalar.copy(out=res[g][:, bank_rows(g, b), :], in_=banks[g, b][:])

        def drain_part(g, b, c0, c1):
            nc.scalar.copy(out=res[g][:, bank_rows(g, b), c0:c1], in_=banks[g, b][:, :, c0:c1])

        def drain_vector(g, b):
            nc.vector.tensor_copy(out=res[g][:, bank_rows(g, b), :], in_=banks[g, b][:])

        def store_rows(g, r0, r1):
            first, width = RANGES[g]
            nc.sync.dma_start(out=out_rows[:, r0:r1, first : first + width], in_=res[g][:, r0:r1, :])

        def result_views(g, c0, c1):
            return woven(res16[g][:, c0:c1, :], res[g][:, :, c0:c1])

        def round_result_vector(g, c0, c1):
            o, i = result_views(g, c0, c1)
            nc.vector.tensor_copy(out=o, in_=i)

        def round_result_scalar(g, c0, c1):
            o, i = result_views(g, c0, c1)
            nc.scalar.copy(out=o, in_=i)

        def quantise_result(g, c0, c1):
            t0 = RANGES[g][0]
            nc.vector.quantize_mx(
                out=o_codes[:, t0 + c0 : t0 + c1].bitcast(FP8X4),
                scales=o_scales[:, t0 + c0 : t0 + c1],
                in_=res16[g][:, c0:c1, :].rearrange("p t j -> p (t j)"),
            )

        def store_words(t0, t1):
            nc.sync.dma_start(out=out_words[:, t0:t1], in_=o_codes[:, t0:t1])

        def store_scales(queues, t0, t1):
            for r in range(4):
                queues[r].dma_start(
                    out=out_2[0, r:16:4, t0:t1].bitcast(I32),
                    in_=o_scales[r:P:QUADRANT, t0:t1].bitcast(I32),
                )

        nc.vector.memset(zero[:], 0.0)
        nc.vector.memset(sc_raw[:].rearrange("p a n -> p (a n)").bitcast(I32), 0)
        nc.scalar.activation(out=bias[:], in_=zero[:], func=ACT.Square)

        load_piece("A0", 0)
        load_w4_scales()
        load_piece("A0", 1)
        load_w4(0, 2)
        load_piece("B0C0", 0)
        load_piece("B0C0", 1)
        load_w8_scales()
        load_piece("A1", 0)
        load_piece("A1", 1)
        load_w8(0, 2)
        load_piece("B1C1", 0)
        load_piece("B1C1", 1)
        load_piece("A2", 0)
        load_piece("A2", 1)
        load_w4(2, 4)
        load_piece("A3", 0)
        load_piece("A3", 1)
        load_w8(2, 4)
        load_piece("B2B3", 0)
        load_piece("B2B3", 1)
        load_piece("C2C3", 0)
        load_piece("C2C3", 1)

        square("A0", 0, PIECE)
        round_vector("A0", 0, PIECE)
        deal_w4_scales()
        square("A0", PIECE, BANK)
        round_vector("A0", PIECE, BANK)
        deal_w4(0, 2)
        quantise_both("A0")
        products("a", "A0")
        square("B0C0", 0, PIECE)
        square("B0C0", PIECE, BANK)
        round_vector("B0C0", 0, BANK)
        deal_w8_scales()
        quantise_both("B0C0")
        products_pair("a", "B0C0")
        square("A1", 0, PIECE)
        square("A1", PIECE, BANK)
        round_scalar("A1", 384, 512)
        round_vector("A1", 0, 384)
        deal_w8(0, 2)
        products("b", "A0")
        products_pair("b", "B0C0")
        quantise_both("A1")
        products_both("A1")
        square("B1C1", 0, PIECE)
        square("B1C1", PIECE, BANK)
        round_vector("B1C1", 0, BANK)
        square("A2", 0, PIECE)
        round_vector("A2", 0, PIECE)
        quantise_both("B1C1")
        products_pair("b", "B1C1")
        products_pair("a", "B1C1")
        square("A2", PIECE, BANK)
        round_vector("A2", PIECE, BANK)
        deal_w4(2, 4)
        quantise_both("A2")
        products("a", "A2")
        round_scalar("A3", 0, PIECE)
        square("A3", 0, BANK)
        round_vector("A3", PIECE, BANK)
        deal_w8(2, 4)
        products("b", "A2")
        quantise_one("b", "A3")
        products("b", "A3")
        square("B2B3", 0, PIECE)
        round_vector("B2B3", 0, PIECE)
        quantise_one("a", "A3")
        products("a", "A3")
        square("B2B3", PIECE, BANK)
        round_vector("B2B3", PIECE, BANK)
        quantise_piece("B2B3", 0)
        products_both("B2B3", 0)
        square("C2C3", 0, PIECE)
        round_vector("C2C3", 0, PIECE)
        quantise_piece("B2B3", 1)
        products_both("B2B3", 1)
        drain_scalar("A", 0)
        store_rows("A", 0, 1)
        drain_scalar("A", 1)
        store_rows("A", 1, 2)
        square("C2C3", PIECE, BANK)
        round_vector("C2C3", PIECE, BANK)
        quantise_piece("C2C3", 0)
        products_both("C2C3", 0)
        drain_vector("A", 2)
        store_rows("A", 2, 3)
        quantise_piece("C2C3", 1)
        products_both("C2C3", 1)
        drain_scalar("A", 3)
        store_rows("A", 3, 4)
        drain_scalar("B", 0)
        store_rows("B", 0, 2)
        drain_scalar("B", 1)
        store_rows("B", 2, 4)
        round_result_vector("A", 0, 256)
        round_result_vector("A", 256, 512)
        quantise_result("A", 0, 256)
        quantise_result("A", 256, 512)
        drain_scalar("C", 0)
        store_rows("C", 0, 2)
        store_words(0, 512)
        drain_scalar("C", 1)
        store_rows("C", 2, 4)
        round_result_scalar("B", 192, 256)
        round_result_vector("B", 0, 192)
        round_result_scalar("C", 160, 256)
        round_result_vector("C", 0, 160)
        quantise_result("B", 0, 256)
        store_words(512, 768)
        quantise_result("C", 0, 256)
        store_words(768, 1024)
        store_scales((nc.scalar, nc.scalar, nc.sync, nc.sync), 0, T)
